import numpy as np
import ml_dtypes


def mxq(x, axis, fmt="e4m3"):
    dtype, down = {"e4m3": (ml_dtypes.float8_e4m3fn, 7), "e5m2": (ml_dtypes.float8_e5m2, 14)}[fmt]
    v = np.moveaxis(np.asarray(x, np.float32).astype(ml_dtypes.bfloat16).astype(np.float64), axis, -1)
    blocks = v.reshape(v.shape[:-1] + (-1, 32))
    amax = np.abs(blocks).max(-1, keepdims=True)
    byte = np.maximum(np.where(amax > 0, np.frexp(amax)[1] - 1 + 127, 0) - down, 1)
    scale = np.exp2(byte - 127.0)
    codes = (blocks / scale).astype(np.float32).astype(dtype).astype(np.float64)
    return np.moveaxis((codes * scale).reshape(v.shape), -1, axis)


WIDE = False


def mx_kscale(k):
    if not WIDE:
        return np.ones(k)
    levels = np.array([18, -18])
    if k % 512:
        return np.exp2(np.random.permutation(np.resize(levels, k // 32))).repeat(32)
    a = np.empty((k // 512, 16))
    for p in range(k // 512):
        a[p, :8] = np.random.permutation(np.resize(levels, 8))
        for g in range(8):
            far = levels[np.abs(levels - a[p, g]) >= 10]
            a[p, g + 8] = far[np.random.randint(len(far))]
    return np.exp2(a.ravel()).repeat(32)


def f64(x):
    return np.asarray(x).astype(np.float64)


def striped(idx):
    return np.tile(np.asarray(idx).reshape(-1, 16).T, (8, 1)).astype(np.uint16)


def unstriped(offs):
    return offs[:16].T.reshape(-1).astype(np.int64)


V, E, D, DV = 1024, 1024, 512, 512


def setup_inputs():
    n = np.random.standard_normal
    u = mx_kscale(E)
    coarse = lambda x: x.astype(np.float32).astype(ml_dtypes.bfloat16).astype(np.float64)
    return {
        "xT": (coarse(n((D, V)))).astype(np.float32),
        "dyT": (coarse(n((DV, V)))).astype(np.float32),
        "hE": (np.random.randint(-15, 16, (DV, E)) / 16.0).astype(np.float32),
        "sw": np.tile(np.random.randint(8, 33, E) / 512.0 / u, (128, 1)).astype(np.float32),
        "tw": np.tile(np.random.randint(8, 33, E) / 16.0 * u, (128, 1)).astype(np.float32),
        "offs": striped(np.random.randint(0, V, E)),
        "offs2": striped(np.random.randint(0, V, E)),
    }


def reference(xT, dyT, hE, sw, tw, offs, offs2):
    h = f64(hE)
    xe = f64(sw)[:1] * f64(xT)[:, unstriped(offs)]
    dz = f64(tw)[:1] * f64(dyT)[:, unstriped(offs2)] * (1.0 - h * h)
    return mxq(xe, 1, "e4m3") @ mxq(dz, 1, "e5m2").T

@@ -1,0 +1,139 @@
+from contextlib import ExitStack
+
+import concourse.mybir as mybir
+from concourse.masks import make_identity
+
+V, E, D, DV = 1024, 1024, 512, 512
+FLOPS = 2 * E * D * DV
+
+F32 = mybir.dt.float32
+BF16 = mybir.dt.bfloat16
+U32 = mybir.dt.uint32
+U16 = mybir.dt.uint16
+U8 = mybir.dt.uint8
+E4M3 = mybir.dt.float8_e4m3fn_x4
+E5M2 = mybir.dt.float8_e5m2_x4
+ACT = mybir.ActivationFunctionType
+MULT = mybir.AluOpType.mult
+
+P = 128
+PACK = 4
+K_PASS = P * PACK
+PASSES = E // K_PASS
+LIST_COLS = K_PASS // 16
+D_TILES = D // P
+N_TILES = DV // P
+
+
+def tile_attend_gmw_tnh_kernel(tc, xT, dyT, hE, sw, tw, offs, offs2, out):
+    nc = tc.nc
+    with ExitStack() as ctx:
+        keep = ctx.enter_context(tc.tile_pool(name="keep", bufs=1))
+        ring = ctx.enter_context(tc.tile_pool(name="ring", bufs=3))
+        psum_t = ctx.enter_context(tc.psum_pool(name="psum_t", bufs=4))
+        psum_h = ctx.enter_context(tc.psum_pool(name="psum_h", bufs=2))
+        psum_o = ctx.enter_context(tc.psum_pool(name="psum_o", bufs=2))
+
+        dst_list = keep.tile([P, E // 16], U16, name="dst_list")
+        src_list = keep.tile([P, E // 16], U16, name="src_list")
+        dy_tiles = [keep.tile([P, V], F32, name="dy%d" % j) for j in range(N_TILES)]
+        h_tiles = [keep.tile([P, E], F32, name="h%d" % j) for j in range(N_TILES)]
+        x_tiles = [keep.tile([P, V], F32, name="x%d" % j) for j in range(D_TILES)]
+        sw_rows = keep.tile([P, E], F32, name="sw_rows")
+        tw_cols = keep.tile([P, PASSES, PACK], F32, name="tw_cols")
+        neg_tw_cols = keep.tile([P, PASSES, PACK], F32, name="neg_tw_cols")
+        ident = keep.tile([P, P], F32, name="ident")
+
+        for j in range(N_TILES):
+            nc.sync.dma_start(dy_tiles[j][:], dyT[j * P:(j + 1) * P, :])
+            if j == 0:
+                nc.sync.dma_start(dst_list[:], offs2)
+            nc.sync.dma_start(h_tiles[j][:], hE[j * P:(j + 1) * P, :])
+            if j == 0:
+                nc.sync.dma_start(tw_cols[:], tw[0, :].rearrange("(g p t) -> p g t", g=PASSES, t=PACK))
+        nc.sync.dma_start(src_list[:], offs)
+        nc.sync.dma_start(sw_rows[:], sw)
+        for j in range(D_TILES):
+            nc.sync.dma_start(x_tiles[j][:], xT[j * P:(j + 1) * P, :])
+
+        make_identity(nc, ident[:])
+        nc.scalar.activation(neg_tw_cols[:], tw_cols[:], ACT.Copy, scale=-1.0)
+
+        dz_bf = [keep.tile([P, DV, PACK], BF16, name="dz_bf%d" % g, align_bytes=64) for g in range(PASSES)]
+        dz_codes = [keep.tile([P, DV], U32, name="dz_codes%d" % g, align_bytes=64) for g in range(PASSES)]
+        dz_scales = [keep.tile([P, DV], U8, name="dz_scales%d" % g, align_bytes=64) for g in range(PASSES)]
+
+        def turn_pairs(bank, src):
+            for t in range(PACK):
+                nc.tensor.transpose(bank[:, t, :], src[:, t // 2, :, t % 2], ident[:])
+
+        for j in range(N_TILES):
+            factors = []
+            for g in range(PASSES):
+                h_sq = ring.tile([P, 2, P, 2], F32, name="h_sq")
+                nc.scalar.activation(
+                    h_sq[:].rearrange("p u s v -> p s u v"),
+                    h_tiles[j][:, g * K_PASS:(g + 1) * K_PASS].rearrange("p (s u v) -> p s u v", u=2, v=2),
+                    ACT.Square,
+                )
+                h_bank = psum_h.tile([P, PACK, P], F32, name="h_bank")
+                turn_pairs(h_bank, h_sq)
+                factor = ring.tile([P, PACK, P], F32, name="factor", bufs=4)
+                for t in range(PACK):
+                    nc.scalar.activation(
+                        factor[:, t, :], h_bank[:, t, :], ACT.Identity,
+                        bias=tw_cols[:, g, t:t + 1], scale=neg_tw_cols[:, g, t:t + 1],
+                    )
+                factors.append(factor)
+            banks = []
+            for g in range(PASSES):
+                dy_g = ring.tile([P, 2, P, 2], F32, name="dy_g")
+                nc.vector.tensor_copy(
+                    dy_g[:].bitcast(U32).rearrange("p u s v -> p s u v"),
+                    dy_tiles[j][:].bitcast(U32).indirect(dst_list[:, g * LIST_COLS:(g + 1) * LIST_COLS]),
+                )
+                bank = psum_t.tile([P, PACK, P], F32, name="bank")
+                turn_pairs(bank, dy_g)
+                banks.append(bank)
+            for g in range(PASSES):
+                nc.vector.tensor_tensor(
+                    dz_bf[g][:, j * P:(j + 1) * P, :].rearrange("p (c i) t -> p c t i", i=2),
+                    banks[g][:].rearrange("p t (c i) -> p c t i", i=2),
+                    factors[g][:].rearrange("p t (c i) -> p c t i", i=2),
+                    MULT,
+                )
+        for g in range(PASSES):
+            nc.vector.quantize_mx(
+                out=dz_codes[g][:].bitcast(E5M2), scales=dz_scales[g][:],
+                in_=dz_bf[g][:].rearrange("p n t -> p (n t)"),
+            )
+
+        for j in range(D_TILES):
+            acc = psum_o.tile([P, DV], F32, name="acc")
+            for g in range(PASSES):
+                xe = ring.tile([P, K_PASS], F32, name="xe")
+                nc.vector.tensor_tensor(
+                    xe[:],
+                    x_tiles[j][:].indirect(src_list[:, g * LIST_COLS:(g + 1) * LIST_COLS]),
+                    sw_rows[:, g * K_PASS:(g + 1) * K_PASS],
+                    MULT,
+                )
+                bank = psum_t.tile([P, PACK, P], F32, name="bank")
+                for t in range(PACK):
+                    nc.tensor.transpose(bank[:, t, :], xe[:, t:K_PASS:PACK], ident[:])
+                xe_bf = ring.tile([P, P, PACK], BF16, name="xe_bf", align_bytes=64)
+                nc.scalar.copy(xe_bf[:], bank[:].rearrange("p t d -> p d t"))
+                xe_codes = ring.tile([P, P], U32, name="xe_codes", align_bytes=64)
+                xe_scales = ring.tile([P, P], U8, name="xe_scales", align_bytes=64)
+                nc.vector.quantize_mx(
+                    out=xe_codes[:].bitcast(E4M3), scales=xe_scales[:],
+                    in_=xe_bf[:].rearrange("p d t -> p (d t)"),
+                )
+                nc.tensor.matmul_mx(
+                    out=acc[:], lhsT=xe_codes[:].bitcast(E4M3), lhsT_scale=xe_scales[:],
+                    rhs=dz_codes[g][:].bitcast(E5M2), rhs_scale=dz_scales[g][:],
+                    start=(g == 0), stop=(g == PASSES - 1),
+                )
+            result = ring.tile([P, DV], F32, name="result")
+            nc.scalar.copy(result[:], acc[:])
+            nc.sync.dma_start(out[j * P:(j + 1) * P, :], result[:])

@@ -30,9 +30,8 @@ def tile_attend_gmw_tnh_kernel(tc, xT, dyT, hE, sw, tw, offs, offs2, out):
     with ExitStack() as ctx:
         keep = ctx.enter_context(tc.tile_pool(name="keep", bufs=1))
         ring = ctx.enter_context(tc.tile_pool(name="ring", bufs=3))
-        psum_t = ctx.enter_context(tc.psum_pool(name="psum_t", bufs=4))
-        psum_h = ctx.enter_context(tc.psum_pool(name="psum_h", bufs=2))
-        psum_o = ctx.enter_context(tc.psum_pool(name="psum_o", bufs=2))
+        psum_t = ctx.enter_context(tc.psum_pool(name="psum_t", bufs=5))
+        psum_o = ctx.enter_context(tc.psum_pool(name="psum_o", bufs=3))
 
         dst_list = keep.tile([P, E // 16], U16, name="dst_list")
         src_list = keep.tile([P, E // 16], U16, name="src_list")
@@ -68,7 +67,6 @@ def tile_attend_gmw_tnh_kernel(tc, xT, dyT, hE, sw, tw, offs, offs2, out):
                 nc.tensor.transpose(bank[:, t, :], src[:, t // 2, :, t % 2], ident[:])
 
         for j in range(N_TILES):
-            factors = []
             for g in range(PASSES):
                 h_sq = ring.tile([P, 2, P, 2], F32, name="h_sq")
                 nc.scalar.activation(
@@ -76,30 +74,24 @@ def tile_attend_gmw_tnh_kernel(tc, xT, dyT, hE, sw, tw, offs, offs2, out):
                     h_tiles[j][:, g * K_PASS:(g + 1) * K_PASS].rearrange("p (s u v) -> p s u v", u=2, v=2),
                     ACT.Square,
                 )
-                h_bank = psum_h.tile([P, PACK, P], F32, name="h_bank")
-                turn_pairs(h_bank, h_sq)
+                bank = psum_t.tile([P, PACK, P], F32, name="bank")
+                turn_pairs(bank, h_sq)
                 factor = ring.tile([P, PACK, P], F32, name="factor", bufs=4)
                 for t in range(PACK):
                     nc.scalar.activation(
-                        factor[:, t, :], h_bank[:, t, :], ACT.Identity,
+                        factor[:, t, :], bank[:, t, :], ACT.Identity,
                         bias=tw_cols[:, g, t:t + 1], scale=neg_tw_cols[:, g, t:t + 1],
                     )
-                factors.append(factor)
-            banks = []
-            for g in range(PASSES):
-                dy_g = ring.tile([P, 2, P, 2], F32, name="dy_g")
+                dy_g = ring.tile([P, 2, P, 2], F32, name="dy_g", bufs=4)
                 nc.vector.tensor_copy(
                     dy_g[:].bitcast(U32).rearrange("p u s v -> p s u v"),
                     dy_tiles[j][:].bitcast(U32).indirect(dst_list[:, g * LIST_COLS:(g + 1) * LIST_COLS]),
                 )
-                bank = psum_t.tile([P, PACK, P], F32, name="bank")
                 turn_pairs(bank, dy_g)
-                banks.append(bank)
-            for g in range(PASSES):
                 nc.vector.tensor_tensor(
                     dz_bf[g][:, j * P:(j + 1) * P, :].rearrange("p (c i) t -> p c t i", i=2),
-                    banks[g][:].rearrange("p t (c i) -> p c t i", i=2),
-                    factors[g][:].rearrange("p t (c i) -> p c t i", i=2),
+                    bank[:].rearrange("p t (c i) -> p c t i", i=2),
+                    factor[:].rearrange("p t (c i) -> p c t i", i=2),
                     MULT,
                 )
         for g in range(PASSES):
@@ -111,29 +103,38 @@ def tile_attend_gmw_tnh_kernel(tc, xT, dyT, hE, sw, tw, offs, offs2, out):
         for j in range(D_TILES):
             acc = psum_o.tile([P, DV], F32, name="acc")
             for g in range(PASSES):
-                xe = ring.tile([P, K_PASS], F32, name="xe")
+                xe = ring.tile([P, K_PASS], F32, name="xe", bufs=2)
                 nc.vector.tensor_tensor(
                     xe[:],
                     x_tiles[j][:].indirect(src_list[:, g * LIST_COLS:(g + 1) * LIST_COLS]),
                     sw_rows[:, g * K_PASS:(g + 1) * K_PASS],
                     MULT,
                 )
+                xe_pairs = ring.tile([P, 2, P, 2], BF16, name="xe_pairs")
+                last = j == D_TILES - 1 and g >= 1
+                move = nc.vector.tensor_copy if last else nc.scalar.copy
+                move(xe_pairs[:], xe[:].rearrange("p (s u v) -> p u s v", u=2, v=2))
+                xe_words = xe_pairs[:].rearrange("p u s v -> p (u s v)").bitcast(F32)
                 bank = psum_t.tile([P, PACK, P], F32, name="bank")
-                for t in range(PACK):
-                    nc.tensor.transpose(bank[:, t, :], xe[:, t:K_PASS:PACK], ident[:])
-                xe_bf = ring.tile([P, P, PACK], BF16, name="xe_bf", align_bytes=64)
-                nc.scalar.copy(xe_bf[:], bank[:].rearrange("p t d -> p d t"))
+                for u in range(2):
+                    nc.tensor.transpose(bank[:, u, :], xe_words[:, u * P:(u + 1) * P], ident[:])
+                xe_bf = ring.tile([P, K_PASS], BF16, name="xe_bf", align_bytes=64)
+                move(
+                    xe_bf[:].bitcast(F32).rearrange("p (d u) -> p d u", u=2),
+                    bank[:, 0:2, :].rearrange("p u d -> p d u"),
+                )
                 xe_codes = ring.tile([P, P], U32, name="xe_codes", align_bytes=64)
                 xe_scales = ring.tile([P, P], U8, name="xe_scales", align_bytes=64)
-                nc.vector.quantize_mx(
-                    out=xe_codes[:].bitcast(E4M3), scales=xe_scales[:],
-                    in_=xe_bf[:].rearrange("p d t -> p (d t)"),
-                )
+                nc.vector.quantize_mx(out=xe_codes[:].bitcast(E4M3), scales=xe_scales[:], in_=xe_bf[:])
                 nc.tensor.matmul_mx(
                     out=acc[:], lhsT=xe_codes[:].bitcast(E4M3), lhsT_scale=xe_scales[:],
                     rhs=dz_codes[g][:].bitcast(E5M2), rhs_scale=dz_scales[g][:],
                     start=(g == 0), stop=(g == PASSES - 1),
                 )
             result = ring.tile([P, DV], F32, name="result")
-            nc.scalar.copy(result[:], acc[:])
-            nc.sync.dma_start(out[j * P:(j + 1) * P, :], result[:])
+            pieces = 2 if j == D_TILES - 1 else 1
+            width = DV // pieces
+            for c in range(pieces):
+                cols = slice(c * width, (c + 1) * width)
+                nc.scalar.copy(result[:, cols], acc[:, cols])
+                nc.sync.dma_start(out[j * P:(j + 1) * P, cols], result[:, cols])

@@ -20,6 +20,7 @@ P = 128
 PACK = 4
 K_PASS = P * PACK
 PASSES = E // K_PASS
+RUN = 16
 LIST_COLS = K_PASS // 16
 D_TILES = D // P
 N_TILES = DV // P
@@ -39,24 +40,34 @@ def tile_attend_gmw_tnh_kernel(tc, xT, dyT, hE, sw, tw, offs, offs2, out):
         h_tiles = [keep.tile([P, E], F32, name="h%d" % j) for j in range(N_TILES)]
         x_tiles = [keep.tile([P, V], F32, name="x%d" % j) for j in range(D_TILES)]
         sw_rows = keep.tile([P, E], F32, name="sw_rows")
-        tw_cols = keep.tile([P, PASSES, PACK], F32, name="tw_cols")
-        neg_tw_cols = keep.tile([P, PASSES, PACK], F32, name="neg_tw_cols")
+        tw_rows = keep.tile([P, 2 * P], F32, name="tw_rows")
+        tw_cols = keep.tile([P, 2, 2 * PASSES], F32, name="tw_cols")
+        neg_tw_cols = keep.tile([P, 2, 2 * PASSES], F32, name="neg_tw_cols")
         ident = keep.tile([P, P], F32, name="ident")
 
+        nc.vector.memset(tw_rows[:], 0.0)
         for j in range(N_TILES):
             nc.sync.dma_start(dy_tiles[j][:], dyT[j * P:(j + 1) * P, :])
             if j == 0:
                 nc.sync.dma_start(dst_list[:], offs2)
             nc.sync.dma_start(h_tiles[j][:], hE[j * P:(j + 1) * P, :])
             if j == 0:
-                nc.sync.dma_start(tw_cols[:], tw[0, :].rearrange("(g p t) -> p g t", g=PASSES, t=PACK))
+                for g in range(PASSES):
+                    nc.sync.dma_start(
+                        tw_rows[2 * g:2 * g + 2, :].rearrange("u (b r) -> u b r", r=RUN),
+                        tw[0, g * K_PASS:(g + 1) * K_PASS].rearrange("(b u r) -> u b r", u=2, r=RUN),
+                    )
         nc.sync.dma_start(src_list[:], offs)
         nc.sync.dma_start(sw_rows[:], sw)
         for j in range(D_TILES):
             nc.sync.dma_start(x_tiles[j][:], xT[j * P:(j + 1) * P, :])
 
         make_identity(nc, ident[:])
-        nc.scalar.activation(neg_tw_cols[:], tw_cols[:], ACT.Copy, scale=-1.0)
+        tw_bank = psum_o.tile([P, 2, P], F32, name="acc")
+        for v in range(2):
+            nc.tensor.transpose(tw_bank[:, v, :], tw_rows[:, v:2 * P:2], ident[:])
+        nc.scalar.copy(tw_cols[:], tw_bank[:, :, 0:2 * PASSES])
+        nc.scalar.activation(neg_tw_cols[:], tw_bank[:, :, 0:2 * PASSES], ACT.Copy, scale=-1.0)
 
         dz_bf = [keep.tile([P, DV, PACK], BF16, name="dz_bf%d" % g, align_bytes=64) for g in range(PASSES)]
         dz_codes = [keep.tile([P, DV], U32, name="dz_codes%d" % g, align_bytes=64) for g in range(PASSES)]
@@ -70,21 +81,22 @@ def tile_attend_gmw_tnh_kernel(tc, xT, dyT, hE, sw, tw, offs, offs2, out):
             for g in range(PASSES):
                 h_sq = ring.tile([P, 2, P, 2], F32, name="h_sq")
                 nc.scalar.activation(
-                    h_sq[:].rearrange("p u s v -> p s u v"),
-                    h_tiles[j][:, g * K_PASS:(g + 1) * K_PASS].rearrange("p (s u v) -> p s u v", u=2, v=2),
+                    h_sq[:].rearrange("p u (b i) v -> p b u (i v)", i=RUN // 2),
+                    h_tiles[j][:, g * K_PASS:(g + 1) * K_PASS].rearrange("p (b u r) -> p b u r", u=2, r=RUN),
                     ACT.Square,
                 )
                 bank = psum_t.tile([P, PACK, P], F32, name="bank")
                 turn_pairs(bank, h_sq)
                 factor = ring.tile([P, PACK, P], F32, name="factor", bufs=4)
                 for t in range(PACK):
+                    col = 2 * g + t // 2
                     nc.scalar.activation(
                         factor[:, t, :], bank[:, t, :], ACT.Identity,
-                        bias=tw_cols[:, g, t:t + 1], scale=neg_tw_cols[:, g, t:t + 1],
+                        bias=tw_cols[:, t % 2, col:col + 1], scale=neg_tw_cols[:, t % 2, col:col + 1],
                     )
                 dy_g = ring.tile([P, 2, P, 2], F32, name="dy_g", bufs=4)
                 nc.vector.tensor_copy(
-                    dy_g[:].bitcast(U32).rearrange("p u s v -> p s u v"),
+                    dy_g[:].bitcast(U32).rearrange("p u (b i) v -> p b u (i v)", i=RUN // 2),
                     dy_tiles[j][:].bitcast(U32).indirect(dst_list[:, g * LIST_COLS:(g + 1) * LIST_COLS]),
                 )
                 turn_pairs(bank, dy_g)
@@ -113,7 +125,10 @@ def tile_attend_gmw_tnh_kernel(tc, xT, dyT, hE, sw, tw, offs, offs2, out):
                 xe_pairs = ring.tile([P, 2, P, 2], BF16, name="xe_pairs")
                 last = j == D_TILES - 1 and g >= 1
                 move = nc.vector.tensor_copy if last else nc.scalar.copy
-                move(xe_pairs[:], xe[:].rearrange("p (s u v) -> p u s v", u=2, v=2))
+                move(
+                    xe_pairs[:].rearrange("p u (b i) v -> p u b (i v)", i=RUN // 2),
+                    xe[:].rearrange("p (b u r) -> p u b r", u=2, r=RUN),
+                )
                 xe_words = xe_pairs[:].rearrange("p u s v -> p (u s v)").bitcast(F32)
                 bank = psum_t.tile([P, PACK, P], F32, name="bank")
                 for u in range(2):

@@ -31,36 +31,59 @@ def tile_attend_gmw_tnh_kernel(tc, xT, dyT, hE, sw, tw, offs, offs2, out):
     with ExitStack() as ctx:
         keep = ctx.enter_context(tc.tile_pool(name="keep", bufs=1))
         ring = ctx.enter_context(tc.tile_pool(name="ring", bufs=3))
-        psum_t = ctx.enter_context(tc.psum_pool(name="psum_t", bufs=5))
-        psum_o = ctx.enter_context(tc.psum_pool(name="psum_o", bufs=3))
+        psum_t = ctx.enter_context(tc.psum_pool(name="psum_t", bufs=6))
+        psum_o = ctx.enter_context(tc.psum_pool(name="psum_o", bufs=2))
 
         dst_list = keep.tile([P, E // 16], U16, name="dst_list")
         src_list = keep.tile([P, E // 16], U16, name="src_list")
         dy_tiles = [keep.tile([P, V], F32, name="dy%d" % j) for j in range(N_TILES)]
-        h_tiles = [keep.tile([P, E], F32, name="h%d" % j) for j in range(N_TILES)]
+        h_tiles = [keep.tile([P, K_PASS], F32, name="h%d" % c) for c in range(N_TILES * PASSES)]
         x_tiles = [keep.tile([P, V], F32, name="x%d" % j) for j in range(D_TILES)]
-        sw_rows = keep.tile([P, E], F32, name="sw_rows")
+        sw_rows = [keep.tile([P, K_PASS], F32, name="sw_rows%d" % g) for g in range(PASSES)]
         tw_rows = keep.tile([P, 2 * P], F32, name="tw_rows")
         tw_cols = keep.tile([P, 2, 2 * PASSES], F32, name="tw_cols")
         neg_tw_cols = keep.tile([P, 2, 2 * PASSES], F32, name="neg_tw_cols")
         ident = keep.tile([P, P], F32, name="ident")
 
         nc.vector.memset(tw_rows[:], 0.0)
-        for j in range(N_TILES):
+        def load_dy(j):
             nc.sync.dma_start(dy_tiles[j][:], dyT[j * P:(j + 1) * P, :])
-            if j == 0:
-                nc.sync.dma_start(dst_list[:], offs2)
-            nc.sync.dma_start(h_tiles[j][:], hE[j * P:(j + 1) * P, :])
-            if j == 0:
-                for g in range(PASSES):
-                    nc.sync.dma_start(
-                        tw_rows[2 * g:2 * g + 2, :].rearrange("u (b r) -> u b r", r=RUN),
-                        tw[0, g * K_PASS:(g + 1) * K_PASS].rearrange("(b u r) -> u b r", u=2, r=RUN),
-                    )
-        nc.sync.dma_start(src_list[:], offs)
-        nc.sync.dma_start(sw_rows[:], sw)
-        for j in range(D_TILES):
+
+        def load_h(c):
+            j, g = divmod(c, PASSES)
+            nc.sync.dma_start(h_tiles[c][:], hE[j * P:(j + 1) * P, g * K_PASS:(g + 1) * K_PASS])
+
+        def load_x(j):
             nc.sync.dma_start(x_tiles[j][:], xT[j * P:(j + 1) * P, :])
+
+        def load_sw(g):
+            nc.sync.dma_start(sw_rows[g][:], sw[:, g * K_PASS:(g + 1) * K_PASS])
+
+        load_dy(0)
+        nc.sync.dma_start(dst_list[:], offs2)
+        load_h(0)
+        for g in range(PASSES):
+            nc.sync.dma_start(
+                tw_rows[2 * g:2 * g + 2, :].rearrange("u (b r) -> u b r", r=RUN),
+                tw[0, g * K_PASS:(g + 1) * K_PASS].rearrange("(b u r) -> u b r", u=2, r=RUN),
+            )
+        load_dy(1)
+        load_h(1)
+        load_h(2)
+        load_dy(2)
+        load_h(3)
+        load_h(4)
+        load_dy(3)
+        load_h(5)
+        nc.sync.dma_start(src_list[:], offs)
+        load_sw(0)
+        load_x(0)
+        load_h(6)
+        load_h(7)
+        load_sw(1)
+        load_x(1)
+        load_x(2)
+        load_x(3)
 
         make_identity(nc, ident[:])
         tw_bank = psum_o.tile([P, 2, P], F32, name="acc")
@@ -79,12 +102,13 @@ def tile_attend_gmw_tnh_kernel(tc, xT, dyT, hE, sw, tw, offs, offs2, out):
 
         for j in range(N_TILES):
             for g in range(PASSES):
-                h_sq = ring.tile([P, 2, P, 2], F32, name="h_sq")
-                nc.scalar.activation(
-                    h_sq[:].rearrange("p u (b i) v -> p b u (i v)", i=RUN // 2),
-                    h_tiles[j][:, g * K_PASS:(g + 1) * K_PASS].rearrange("p (b u r) -> p b u r", u=2, r=RUN),
-                    ACT.Square,
-                )
+                h_sq = ring.tile([P, 2, P, 2], F32, name="h_sq", bufs=4)
+                h_sq_view = h_sq[:].rearrange("p u (b i) v -> p b u (i v)", i=RUN // 2)
+                h_view = h_tiles[PASSES * j + g][:].rearrange("p (b u r) -> p b u r", u=2, r=RUN)
+                if 2 * j + g in (1, 2, 3):
+                    nc.gpsimd.tensor_tensor(h_sq_view, h_view, h_view, MULT)
+                else:
+                    nc.scalar.activation(h_sq_view, h_view, ACT.Square)
                 bank = psum_t.tile([P, PACK, P], F32, name="bank")
                 turn_pairs(bank, h_sq)
                 factor = ring.tile([P, PACK, P], F32, name="factor", bufs=4)
@@ -94,24 +118,42 @@ def tile_attend_gmw_tnh_kernel(tc, xT, dyT, hE, sw, tw, offs, offs2, out):
                         factor[:, t, :], bank[:, t, :], ACT.Identity,
                         bias=tw_cols[:, t % 2, col:col + 1], scale=neg_tw_cols[:, t % 2, col:col + 1],
                     )
-                dy_g = ring.tile([P, 2, P, 2], F32, name="dy_g", bufs=4)
+                dy_g = ring.tile([P, 2, P, 2], F32, name="dy_g", bufs=6)
                 nc.vector.tensor_copy(
                     dy_g[:].bitcast(U32).rearrange("p u (b i) v -> p b u (i v)", i=RUN // 2),
                     dy_tiles[j][:].bitcast(U32).indirect(dst_list[:, g * LIST_COLS:(g + 1) * LIST_COLS]),
                 )
                 turn_pairs(bank, dy_g)
-                nc.vector.tensor_tensor(
-                    dz_bf[g][:, j * P:(j + 1) * P, :].rearrange("p (c i) t -> p c t i", i=2),
-                    bank[:].rearrange("p t (c i) -> p c t i", i=2),
-                    factor[:].rearrange("p t (c i) -> p c t i", i=2),
-                    MULT,
-                )
+                if 2 * j + g in (0, 1, 2):
+                    dy_turned = ring.tile([P, P, PACK], F32, name="dy_turned")
+                    nc.scalar.copy(dy_turned[:], bank[:].rearrange("p t n -> p n t"))
+                    nc.gpsimd.tensor_tensor(
+                        dz_bf[g][:, j * P:(j + 1) * P, :], dy_turned[:],
+                        factor[:].rearrange("p t n -> p n t"), MULT,
+                    )
+                else:
+                    nc.vector.tensor_tensor(
+                        dz_bf[g][:, j * P:(j + 1) * P, :].rearrange("p (c i) t -> p c t i", i=4),
+                        bank[:].rearrange("p t (c i) -> p c t i", i=4),
+                        factor[:].rearrange("p t (c i) -> p c t i", i=4),
+                        MULT,
+                    )
         for g in range(PASSES):
             nc.vector.quantize_mx(
                 out=dz_codes[g][:].bitcast(E5M2), scales=dz_scales[g][:],
                 in_=dz_bf[g][:].rearrange("p n t -> p (n t)"),
             )
 
+        def store(j, acc):
+            result = ring.tile([P, DV], F32, name="result")
+            pieces = 2 if j == D_TILES - 1 else 1
+            width = DV // pieces
+            for c in range(pieces):
+                cols = slice(c * width, (c + 1) * width)
+                nc.scalar.copy(result[:, cols], acc[:, cols])
+                nc.sync.dma_start(out[j * P:(j + 1) * P, cols], result[:, cols])
+
+        waiting = []
         for j in range(D_TILES):
             acc = psum_o.tile([P, DV], F32, name="acc")
             for g in range(PASSES):
@@ -119,7 +161,7 @@ def tile_attend_gmw_tnh_kernel(tc, xT, dyT, hE, sw, tw, offs, offs2, out):
                 nc.vector.tensor_tensor(
                     xe[:],
                     x_tiles[j][:].indirect(src_list[:, g * LIST_COLS:(g + 1) * LIST_COLS]),
-                    sw_rows[:, g * K_PASS:(g + 1) * K_PASS],
+                    sw_rows[g][:],
                     MULT,
                 )
                 xe_pairs = ring.tile([P, 2, P, 2], BF16, name="xe_pairs")
@@ -138,6 +180,8 @@ def tile_attend_gmw_tnh_kernel(tc, xT, dyT, hE, sw, tw, offs, offs2, out):
                     xe_bf[:].bitcast(F32).rearrange("p (d u) -> p d u", u=2),
                     bank[:, 0:2, :].rearrange("p u d -> p d u"),
                 )
+                if waiting and g == 0:
+                    store(*waiting.pop())
                 xe_codes = ring.tile([P, P], U32, name="xe_codes", align_bytes=64)
                 xe_scales = ring.tile([P, P], U8, name="xe_scales", align_bytes=64)
                 nc.vector.quantize_mx(out=xe_codes[:].bitcast(E4M3), scales=xe_scales[:], in_=xe_bf[:])
@@ -146,10 +190,5 @@ def tile_attend_gmw_tnh_kernel(tc, xT, dyT, hE, sw, tw, offs, offs2, out):
                     rhs=dz_codes[g][:].bitcast(E5M2), rhs_scale=dz_scales[g][:],
                     start=(g == 0), stop=(g == PASSES - 1),
                 )
-            result = ring.tile([P, DV], F32, name="result")
-            pieces = 2 if j == D_TILES - 1 else 1
-            width = DV // pieces
-            for c in range(pieces):
-                cols = slice(c * width, (c + 1) * width)
-                nc.scalar.copy(result[:, cols], acc[:, cols])
-                nc.sync.dma_start(out[j * P:(j + 1) * P, cols], result[:, cols])
+            waiting.append((j, acc))
+        store(*waiting.pop())

@@ -24,28 +24,38 @@ RUN = 16
 LIST_COLS = K_PASS // 16
 D_TILES = D // P
 N_TILES = DV // P
+CHUNKS = N_TILES * PASSES
+GPSIMD_PRODUCTS = 4
+GPSIMD_SQUARES = ()
+H_BANKS = (0, 1, 2, 0, 3, 4, 5, 6)
+DY_BANKS = (1, 2, 0, 1, 3, 4, 5, 6)
+WORD_BANKS = (0, 1)
+X_BANKS = (7, 3, 7, 7)
+GPSIMD_X_TILES = 2
+FACTOR_LEAD = 2
+ACC_BANKS = (2, 0, 1, 4)
 
 
 def tile_attend_gmw_tnh_kernel(tc, xT, dyT, hE, sw, tw, offs, offs2, out):
     nc = tc.nc
     with ExitStack() as ctx:
         keep = ctx.enter_context(tc.tile_pool(name="keep", bufs=1))
-        ring = ctx.enter_context(tc.tile_pool(name="ring", bufs=3))
-        psum_t = ctx.enter_context(tc.psum_pool(name="psum_t", bufs=6))
-        psum_o = ctx.enter_context(tc.psum_pool(name="psum_o", bufs=2))
+        psum = ctx.enter_context(tc.psum_pool(name="psum", bufs=1))
 
         dst_list = keep.tile([P, E // 16], U16, name="dst_list")
         src_list = keep.tile([P, E // 16], U16, name="src_list")
         dy_tiles = [keep.tile([P, V], F32, name="dy%d" % j) for j in range(N_TILES)]
-        h_tiles = [keep.tile([P, K_PASS], F32, name="h%d" % c) for c in range(N_TILES * PASSES)]
+        h_tiles = [keep.tile([P, K_PASS], F32, name="h%d" % c) for c in range(CHUNKS)]
         x_tiles = [keep.tile([P, V], F32, name="x%d" % j) for j in range(D_TILES)]
         sw_rows = [keep.tile([P, K_PASS], F32, name="sw_rows%d" % g) for g in range(PASSES)]
-        tw_rows = keep.tile([P, 2 * P], F32, name="tw_rows")
-        tw_cols = keep.tile([P, 2, 2 * PASSES], F32, name="tw_cols")
-        neg_tw_cols = keep.tile([P, 2, 2 * PASSES], F32, name="neg_tw_cols")
+        tw_rows = keep.tile([P, PASSES * 2 * P], F32, name="tw_rows")
+        tw_cols = keep.tile([P, PASSES * 2, 2], F32, name="tw_cols")
+        neg_tw_cols = keep.tile([P, PASSES * 2, 2], F32, name="neg_tw_cols")
         ident = keep.tile([P, P], F32, name="ident")
+        banks = [psum.tile([P, PACK, P], F32, name="bank%d" % b) for b in range(8)]
 
         nc.vector.memset(tw_rows[:], 0.0)
+
         def load_dy(j):
             nc.sync.dma_start(dy_tiles[j][:], dyT[j * P:(j + 1) * P, :])
 
@@ -59,136 +69,192 @@ def tile_attend_gmw_tnh_kernel(tc, xT, dyT, hE, sw, tw, offs, offs2, out):
         def load_sw(g):
             nc.sync.dma_start(sw_rows[g][:], sw[:, g * K_PASS:(g + 1) * K_PASS])
 
-        load_dy(0)
-        nc.sync.dma_start(dst_list[:], offs2)
-        load_h(0)
-        for g in range(PASSES):
+        def load_tw():
             nc.sync.dma_start(
-                tw_rows[2 * g:2 * g + 2, :].rearrange("u (b r) -> u b r", r=RUN),
-                tw[0, g * K_PASS:(g + 1) * K_PASS].rearrange("(b u r) -> u b r", u=2, r=RUN),
+                tw_rows[0:2, :].rearrange("u (b r) -> u b r", r=RUN),
+                tw[0, :].rearrange("(b u r) -> u b r", u=2, r=RUN),
             )
-        load_dy(1)
-        load_h(1)
-        load_h(2)
-        load_dy(2)
-        load_h(3)
-        load_h(4)
-        load_dy(3)
-        load_h(5)
+
+        load_x(0)
         nc.sync.dma_start(src_list[:], offs)
         load_sw(0)
-        load_x(0)
+        load_tw()
+        load_h(0)
+        load_x(1)
+        load_h(1)
+        load_h(2)
+        load_dy(0)
+        nc.sync.dma_start(dst_list[:], offs2)
+        load_h(3)
+        load_sw(1)
+        load_dy(1)
+        load_h(4)
+        load_dy(2)
+        load_dy(3)
+        load_h(5)
         load_h(6)
         load_h(7)
-        load_sw(1)
-        load_x(1)
         load_x(2)
         load_x(3)
 
         make_identity(nc, ident[:])
-        tw_bank = psum_o.tile([P, 2, P], F32, name="acc")
-        for v in range(2):
-            nc.tensor.transpose(tw_bank[:, v, :], tw_rows[:, v:2 * P:2], ident[:])
-        nc.scalar.copy(tw_cols[:], tw_bank[:, :, 0:2 * PASSES])
-        nc.scalar.activation(neg_tw_cols[:], tw_bank[:, :, 0:2 * PASSES], ACT.Copy, scale=-1.0)
+        tw_bank = banks[7]
+        for g in range(PASSES):
+            for v in range(2):
+                nc.tensor.transpose(tw_bank[:, 2 * g + v, :], tw_rows[:, g * 2 * P + v:(g + 1) * 2 * P:2], ident[:])
+        nc.scalar.copy(tw_cols[:], tw_bank[:, :, 0:2])
+        nc.scalar.activation(neg_tw_cols[:], tw_bank[:, :, 0:2], ACT.Copy, scale=-1.0)
 
         dz_bf = [keep.tile([P, DV, PACK], BF16, name="dz_bf%d" % g, align_bytes=64) for g in range(PASSES)]
         dz_codes = [keep.tile([P, DV], U32, name="dz_codes%d" % g, align_bytes=64) for g in range(PASSES)]
         dz_scales = [keep.tile([P, DV], U8, name="dz_scales%d" % g, align_bytes=64) for g in range(PASSES)]
+        squares = [keep.tile([P, K_PASS], F32, name="h_sq%d" % s) for s in range(3)]
+        factors = [keep.tile([P, K_PASS], F32, name="factor%d" % c, align_bytes=64) for c in range(CHUNKS)]
+        turned = [keep.tile([P, K_PASS], F32, name="dy_turned%d" % c, align_bytes=64) for c in range(GPSIMD_PRODUCTS)]
 
-        def turn_pairs(bank, src):
+        def in_runs(ap):
+            return ap.rearrange("p (b u r) -> p b u r", u=2, r=RUN)
+
+        def dealt(ap):
+            return ap.rearrange("p (u b r) -> p b u r", u=2, r=RUN)
+
+        def edges(index_list, g):
+            return index_list[:, g * LIST_COLS:(g + 1) * LIST_COLS]
+
+        def turn_values(bank, src):
             for t in range(PACK):
-                nc.tensor.transpose(bank[:, t, :], src[:, t // 2, :, t % 2], ident[:])
+                u, v = divmod(t, 2)
+                nc.tensor.transpose(bank[:, t, :], src[:, u * 2 * P + v:(u + 1) * 2 * P:2], ident[:])
 
-        for j in range(N_TILES):
-            for g in range(PASSES):
-                h_sq = ring.tile([P, 2, P, 2], F32, name="h_sq", bufs=4)
-                h_sq_view = h_sq[:].rearrange("p u (b i) v -> p b u (i v)", i=RUN // 2)
-                h_view = h_tiles[PASSES * j + g][:].rearrange("p (b u r) -> p b u r", u=2, r=RUN)
-                if 2 * j + g in (1, 2, 3):
-                    nc.gpsimd.tensor_tensor(h_sq_view, h_view, h_view, MULT)
-                else:
-                    nc.scalar.activation(h_sq_view, h_view, ACT.Square)
-                bank = psum_t.tile([P, PACK, P], F32, name="bank")
-                turn_pairs(bank, h_sq)
-                factor = ring.tile([P, PACK, P], F32, name="factor", bufs=4)
-                for t in range(PACK):
-                    col = 2 * g + t // 2
-                    nc.scalar.activation(
-                        factor[:, t, :], bank[:, t, :], ACT.Identity,
-                        bias=tw_cols[:, t % 2, col:col + 1], scale=neg_tw_cols[:, t % 2, col:col + 1],
-                    )
-                dy_g = ring.tile([P, 2, P, 2], F32, name="dy_g", bufs=6)
-                nc.vector.tensor_copy(
-                    dy_g[:].bitcast(U32).rearrange("p u (b i) v -> p b u (i v)", i=RUN // 2),
-                    dy_tiles[j][:].bitcast(U32).indirect(dst_list[:, g * LIST_COLS:(g + 1) * LIST_COLS]),
+        def square(c):
+            h_sq = squares[c % len(squares)]
+            h_view = in_runs(h_tiles[c][:])
+            if c in GPSIMD_SQUARES:
+                nc.gpsimd.tensor_tensor(dealt(h_sq[:]), h_view, h_view, MULT)
+            else:
+                nc.scalar.activation(dealt(h_sq[:]), h_view, ACT.Square)
+
+        def turn_words(bank, words):
+            for u in range(2):
+                nc.tensor.transpose(bank[:, u, :], words[:, u * P:(u + 1) * P], ident[:])
+
+        early_pairs = []
+        for c in range(GPSIMD_X_TILES * PASSES):
+            j, g = divmod(c, PASSES)
+            x_g = keep.tile([P, K_PASS], F32, name="x_g%d" % c)
+            nc.vector.tensor_copy(dealt(x_g[:].bitcast(U32)), x_tiles[j][:].bitcast(U32).indirect(edges(src_list, g)))
+            pairs = keep.tile([P, K_PASS], BF16, name="early_pairs%d" % c)
+            nc.gpsimd.tensor_tensor(
+                pairs[:].rearrange("p (u b r) -> p u b r", u=2, r=RUN),
+                x_g[:].rearrange("p (u b r) -> p u b r", u=2, r=RUN),
+                sw_rows[g][:].rearrange("p (b u r) -> p u b r", u=2, r=RUN),
+                MULT,
+            )
+            early_pairs.append(pairs)
+
+        def make_factor(c):
+            g = c % PASSES
+            if c + 1 < CHUNKS:
+                square(c + 1)
+            h_bank = banks[H_BANKS[c]]
+            turn_values(h_bank, squares[c % len(squares)])
+            for t in range(PACK):
+                u, v = divmod(t, 2)
+                nc.scalar.activation(
+                    factors[c][:, t * P:(t + 1) * P], h_bank[:, t, :], ACT.Identity,
+                    bias=tw_cols[:, 2 * g + v, u:u + 1], scale=neg_tw_cols[:, 2 * g + v, u:u + 1],
                 )
-                turn_pairs(bank, dy_g)
-                if 2 * j + g in (0, 1, 2):
-                    dy_turned = ring.tile([P, P, PACK], F32, name="dy_turned")
-                    nc.scalar.copy(dy_turned[:], bank[:].rearrange("p t n -> p n t"))
-                    nc.gpsimd.tensor_tensor(
-                        dz_bf[g][:, j * P:(j + 1) * P, :], dy_turned[:],
-                        factor[:].rearrange("p t n -> p n t"), MULT,
-                    )
-                else:
-                    nc.vector.tensor_tensor(
-                        dz_bf[g][:, j * P:(j + 1) * P, :].rearrange("p (c i) t -> p c t i", i=4),
-                        bank[:].rearrange("p t (c i) -> p c t i", i=4),
-                        factor[:].rearrange("p t (c i) -> p c t i", i=4),
-                        MULT,
-                    )
+
+        square(0)
+        for c in range(FACTOR_LEAD):
+            make_factor(c)
+        for c in range(CHUNKS):
+            j, g = divmod(c, PASSES)
+            if c + FACTOR_LEAD < CHUNKS:
+                make_factor(c + FACTOR_LEAD)
+            dy_g = keep.tile([P, K_PASS], F32, name="dy_g%d" % c)
+            nc.vector.tensor_copy(dealt(dy_g[:].bitcast(U32)), dy_tiles[j][:].bitcast(U32).indirect(edges(dst_list, g)))
+            factor = factors[c][:].rearrange("p (t n) -> p t n", t=PACK)
+            dy_bank = banks[DY_BANKS[c]]
+            turn_values(dy_bank, dy_g)
+            dz_part = dz_bf[g][:, j * P:(j + 1) * P, :]
+            if c < GPSIMD_PRODUCTS:
+                dy_turned = turned[c][:].rearrange("p (n t) -> p n t", t=PACK)
+                nc.scalar.copy(dy_turned, dy_bank[:].rearrange("p t n -> p n t"))
+                nc.gpsimd.tensor_tensor(dz_part, dy_turned, factor.rearrange("p t n -> p n t"), MULT)
+            else:
+                nc.vector.tensor_tensor(
+                    dz_part.rearrange("p (c i) t -> p c t i", i=4),
+                    dy_bank[:].rearrange("p t (c i) -> p c t i", i=4),
+                    factor.rearrange("p t (c i) -> p c t i", i=4),
+                    MULT,
+                )
+
+        def multiply(j, g, codes, scales):
+            nc.tensor.matmul_mx(
+                out=banks[ACC_BANKS[j]][:].rearrange("p t n -> p (t n)"),
+                lhsT=codes.bitcast(E4M3), lhsT_scale=scales,
+                rhs=dz_codes[g][:].bitcast(E5M2), rhs_scale=dz_scales[g][:],
+                start=(g == 0), stop=(g == PASSES - 1),
+            )
+
+        def store(j):
+            acc = banks[ACC_BANKS[j]][:].rearrange("p t n -> p (t n)")
+            result = staged[j]
+            pieces = 2 if j == D_TILES - 1 else 1
+            width = DV // pieces
+            for piece in range(pieces):
+                cols = slice(piece * width, (piece + 1) * width)
+                nc.scalar.copy(result[:, cols], acc[:, cols])
+                nc.sync.dma_start(out[j * P:(j + 1) * P, cols], result[:, cols])
+
+        spare = keep.tile([P, DV], F32, name="spare")
+        staged = [factors[0], factors[CHUNKS - 1], spare, factors[1]]
+        early_words = [factors[CHUNKS - 3], factors[CHUNKS - 2]]
+        early_codes = []
+        for j in range(GPSIMD_X_TILES):
+            bank = banks[WORD_BANKS[j]]
+            for g in range(PASSES):
+                turn_words(bank[:, 2 * g:2 * g + 2, :], early_pairs[PASSES * j + g][:].bitcast(F32))
+            nc.scalar.copy(
+                early_words[j][:].rearrange("p (g d u) -> p g d u", g=PASSES, u=2),
+                bank[:].rearrange("p (g u) d -> p g d u", u=2),
+            )
+            codes = keep.tile([P, PASSES * P], U32, name="early_codes%d" % j, align_bytes=64)
+            scales = keep.tile([P, PASSES * P], U8, name="early_scales%d" % j, align_bytes=64)
+            nc.vector.quantize_mx(out=codes[:].bitcast(E4M3), scales=scales[:], in_=early_words[j][:].bitcast(BF16))
+            early_codes.append((codes, scales))
         for g in range(PASSES):
             nc.vector.quantize_mx(
                 out=dz_codes[g][:].bitcast(E5M2), scales=dz_scales[g][:],
                 in_=dz_bf[g][:].rearrange("p n t -> p (n t)"),
             )
-
-        def store(j, acc):
-            result = ring.tile([P, DV], F32, name="result")
-            pieces = 2 if j == D_TILES - 1 else 1
-            width = DV // pieces
-            for c in range(pieces):
-                cols = slice(c * width, (c + 1) * width)
-                nc.scalar.copy(result[:, cols], acc[:, cols])
-                nc.sync.dma_start(out[j * P:(j + 1) * P, cols], result[:, cols])
-
-        waiting = []
-        for j in range(D_TILES):
-            acc = psum_o.tile([P, DV], F32, name="acc")
+        for j, (codes, scales) in enumerate(early_codes):
             for g in range(PASSES):
-                xe = ring.tile([P, K_PASS], F32, name="xe", bufs=2)
-                nc.vector.tensor_tensor(
-                    xe[:],
-                    x_tiles[j][:].indirect(src_list[:, g * LIST_COLS:(g + 1) * LIST_COLS]),
-                    sw_rows[g][:],
-                    MULT,
-                )
-                xe_pairs = ring.tile([P, 2, P, 2], BF16, name="xe_pairs")
-                last = j == D_TILES - 1 and g >= 1
-                move = nc.vector.tensor_copy if last else nc.scalar.copy
-                move(
-                    xe_pairs[:].rearrange("p u (b i) v -> p u b (i v)", i=RUN // 2),
-                    xe[:].rearrange("p (b u r) -> p u b r", u=2, r=RUN),
-                )
-                xe_words = xe_pairs[:].rearrange("p u s v -> p (u s v)").bitcast(F32)
-                bank = psum_t.tile([P, PACK, P], F32, name="bank")
-                for u in range(2):
-                    nc.tensor.transpose(bank[:, u, :], xe_words[:, u * P:(u + 1) * P], ident[:])
-                xe_bf = ring.tile([P, K_PASS], BF16, name="xe_bf", align_bytes=64)
-                move(
-                    xe_bf[:].bitcast(F32).rearrange("p (d u) -> p d u", u=2),
-                    bank[:, 0:2, :].rearrange("p u d -> p d u"),
-                )
-                if waiting and g == 0:
-                    store(*waiting.pop())
-                xe_codes = ring.tile([P, P], U32, name="xe_codes", align_bytes=64)
-                xe_scales = ring.tile([P, P], U8, name="xe_scales", align_bytes=64)
-                nc.vector.quantize_mx(out=xe_codes[:].bitcast(E4M3), scales=xe_scales[:], in_=xe_bf[:])
-                nc.tensor.matmul_mx(
-                    out=acc[:], lhsT=xe_codes[:].bitcast(E4M3), lhsT_scale=xe_scales[:],
-                    rhs=dz_codes[g][:].bitcast(E5M2), rhs_scale=dz_scales[g][:],
-                    start=(g == 0), stop=(g == PASSES - 1),
-                )
-            waiting.append((j, acc))
-        store(*waiting.pop())
+                multiply(j, g, codes[:, g * P:(g + 1) * P], scales[:, g * P:(g + 1) * P])
+
+        store(0)
+        slots = [factors[GPSIMD_PRODUCTS - 1][:], turned[-1][:], factors[CHUNKS - 1][:],
+                 dz_bf[0][:].rearrange("p n t -> p (n t)").bitcast(F32)[:, 0:K_PASS]]
+        late = (D_TILES - GPSIMD_X_TILES) * PASSES
+        for c in range(late):
+            j, g = GPSIMD_X_TILES + c // PASSES, c % PASSES
+            xe = slots[c]
+            nc.vector.tensor_tensor(xe, x_tiles[j][:].indirect(edges(src_list, g)), sw_rows[g][:], MULT)
+            move = nc.vector.tensor_copy if c == late - 1 else nc.scalar.copy
+            pair_words = (turned[0], turned[1], spare, turned[2])[c][:, 0:K_PASS // 2]
+            move(
+                pair_words.bitcast(BF16).rearrange("p (u b r) -> p u b r", u=2, r=RUN),
+                xe.rearrange("p (b u r) -> p u b r", u=2, r=RUN),
+            )
+            bank = banks[X_BANKS[c]]
+            turn_words(bank, pair_words)
+            words = keep.tile([P, K_PASS // 2], F32, name="late_words%d" % c, align_bytes=64)
+            move(words[:].rearrange("p (d u) -> p d u", u=2), bank[:, 0:2, :].rearrange("p u d -> p d u"))
+            if c >= GPSIMD_X_TILES:
+                store(c - 1)
+            codes = keep.tile([P, P], U32, name="xe_codes%d" % c, align_bytes=64)
+            scales = keep.tile([P, P], U8, name="xe_scales%d" % c, align_bytes=64)
+            nc.vector.quantize_mx(out=codes[:].bitcast(E4M3), scales=scales[:], in_=words[:].bitcast(BF16))
+            multiply(j, g, codes[:], scales[:])
+        store(D_TILES - 1)

@@ -30,7 +30,7 @@ GPSIMD_SQUARES = ()
 H_BANKS = (0, 1, 2, 0, 3, 4, 5, 6)
 DY_BANKS = (1, 2, 0, 1, 3, 4, 5, 6)
 WORD_BANKS = (0, 1)
-X_BANKS = (7, 3, 7, 7)
+X_BANKS = (7, 3, 7, 3)
 GPSIMD_X_TILES = 2
 FACTOR_LEAD = 2
 ACC_BANKS = (2, 0, 1, 4)
@@ -48,7 +48,8 @@ def tile_attend_gmw_tnh_kernel(tc, xT, dyT, hE, sw, tw, offs, offs2, out):
         h_tiles = [keep.tile([P, K_PASS], F32, name="h%d" % c) for c in range(CHUNKS)]
         x_tiles = [keep.tile([P, V], F32, name="x%d" % j) for j in range(D_TILES)]
         sw_rows = [keep.tile([P, K_PASS], F32, name="sw_rows%d" % g) for g in range(PASSES)]
-        tw_rows = keep.tile([P, PASSES * 2 * P], F32, name="tw_rows")
+        tw_line = keep.tile([PASSES, K_PASS], F32, name="tw_line")
+        tw_rows = keep.tile([P, K_PASS], F32, name="tw_rows")
         tw_cols = keep.tile([P, PASSES * 2, 2], F32, name="tw_cols")
         neg_tw_cols = keep.tile([P, PASSES * 2, 2], F32, name="neg_tw_cols")
         ident = keep.tile([P, P], F32, name="ident")
@@ -70,15 +71,12 @@ def tile_attend_gmw_tnh_kernel(tc, xT, dyT, hE, sw, tw, offs, offs2, out):
             nc.sync.dma_start(sw_rows[g][:], sw[:, g * K_PASS:(g + 1) * K_PASS])
 
         def load_tw():
-            nc.sync.dma_start(
-                tw_rows[0:2, :].rearrange("u (b r) -> u b r", r=RUN),
-                tw[0, :].rearrange("(b u r) -> u b r", u=2, r=RUN),
-            )
+            nc.sync.dma_start(tw_line[:], tw[0, :].rearrange("(g e) -> g e", g=PASSES))
 
+        load_tw()
         load_x(0)
         nc.sync.dma_start(src_list[:], offs)
         load_sw(0)
-        load_tw()
         load_h(0)
         load_x(1)
         load_h(1)
@@ -97,11 +95,15 @@ def tile_attend_gmw_tnh_kernel(tc, xT, dyT, hE, sw, tw, offs, offs2, out):
         load_x(2)
         load_x(3)
 
+        nc.vector.tensor_copy(
+            tw_rows[0:PASSES, :].rearrange("g (u b r) -> g u b r", u=2, r=RUN),
+            tw_line[:].rearrange("g (b u r) -> g u b r", u=2, r=RUN),
+        )
         make_identity(nc, ident[:])
         tw_bank = banks[7]
-        for g in range(PASSES):
-            for v in range(2):
-                nc.tensor.transpose(tw_bank[:, 2 * g + v, :], tw_rows[:, g * 2 * P + v:(g + 1) * 2 * P:2], ident[:])
+        for t in range(PACK):
+            u, v = divmod(t, 2)
+            nc.tensor.transpose(tw_bank[:, t, :], tw_rows[:, u * 2 * P + v:(u + 1) * 2 * P:2], ident[:])
         nc.scalar.copy(tw_cols[:], tw_bank[:, :, 0:2])
         nc.scalar.activation(neg_tw_cols[:], tw_bank[:, :, 0:2], ACT.Copy, scale=-1.0)
 
@@ -109,7 +111,7 @@ def tile_attend_gmw_tnh_kernel(tc, xT, dyT, hE, sw, tw, offs, offs2, out):
         dz_codes = [keep.tile([P, DV], U32, name="dz_codes%d" % g, align_bytes=64) for g in range(PASSES)]
         dz_scales = [keep.tile([P, DV], U8, name="dz_scales%d" % g, align_bytes=64) for g in range(PASSES)]
         squares = [keep.tile([P, K_PASS], F32, name="h_sq%d" % s) for s in range(3)]
-        factors = [keep.tile([P, K_PASS], F32, name="factor%d" % c, align_bytes=64) for c in range(CHUNKS)]
+        factors = [keep.tile([P, 3 * K_PASS // 2], F32, name="factor%d" % c, align_bytes=64) for c in range(CHUNKS)]
         turned = [keep.tile([P, K_PASS], F32, name="dy_turned%d" % c, align_bytes=64) for c in range(GPSIMD_PRODUCTS)]
 
         def in_runs(ap):
@@ -162,7 +164,7 @@ def tile_attend_gmw_tnh_kernel(tc, xT, dyT, hE, sw, tw, offs, offs2, out):
                 u, v = divmod(t, 2)
                 nc.scalar.activation(
                     factors[c][:, t * P:(t + 1) * P], h_bank[:, t, :], ACT.Identity,
-                    bias=tw_cols[:, 2 * g + v, u:u + 1], scale=neg_tw_cols[:, 2 * g + v, u:u + 1],
+                    bias=tw_cols[:, t, g:g + 1], scale=neg_tw_cols[:, t, g:g + 1],
                 )
 
         square(0)
@@ -174,7 +176,7 @@ def tile_attend_gmw_tnh_kernel(tc, xT, dyT, hE, sw, tw, offs, offs2, out):
                 make_factor(c + FACTOR_LEAD)
             dy_g = keep.tile([P, K_PASS], F32, name="dy_g%d" % c)
             nc.vector.tensor_copy(dealt(dy_g[:].bitcast(U32)), dy_tiles[j][:].bitcast(U32).indirect(edges(dst_list, g)))
-            factor = factors[c][:].rearrange("p (t n) -> p t n", t=PACK)
+            factor = factors[c][:, 0:K_PASS].rearrange("p (t n) -> p t n", t=PACK)
             dy_bank = banks[DY_BANKS[c]]
             turn_values(dy_bank, dy_g)
             dz_part = dz_bf[g][:, j * P:(j + 1) * P, :]
@@ -209,20 +211,20 @@ def tile_attend_gmw_tnh_kernel(tc, xT, dyT, hE, sw, tw, offs, offs2, out):
                 nc.sync.dma_start(out[j * P:(j + 1) * P, cols], result[:, cols])
 
         spare = keep.tile([P, DV], F32, name="spare")
-        staged = [factors[0], factors[CHUNKS - 1], spare, factors[1]]
-        early_words = [factors[CHUNKS - 3], factors[CHUNKS - 2]]
+        staged = [factors[0], factors[CHUNKS - 1][:, K_PASS // 2:], spare, factors[1]]
+        early_words = [factors[CHUNKS - 3][:, 0:K_PASS], factors[CHUNKS - 2][:, 0:K_PASS]]
         early_codes = []
         for j in range(GPSIMD_X_TILES):
             bank = banks[WORD_BANKS[j]]
             for g in range(PASSES):
                 turn_words(bank[:, 2 * g:2 * g + 2, :], early_pairs[PASSES * j + g][:].bitcast(F32))
             nc.scalar.copy(
-                early_words[j][:].rearrange("p (g d u) -> p g d u", g=PASSES, u=2),
+                early_words[j].rearrange("p (g d u) -> p g d u", g=PASSES, u=2),
                 bank[:].rearrange("p (g u) d -> p g d u", u=2),
             )
             codes = keep.tile([P, PASSES * P], U32, name="early_codes%d" % j, align_bytes=64)
             scales = keep.tile([P, PASSES * P], U8, name="early_scales%d" % j, align_bytes=64)
-            nc.vector.quantize_mx(out=codes[:].bitcast(E4M3), scales=scales[:], in_=early_words[j][:].bitcast(BF16))
+            nc.vector.quantize_mx(out=codes[:].bitcast(E4M3), scales=scales[:], in_=early_words[j].bitcast(BF16))
             early_codes.append((codes, scales))
         for g in range(PASSES):
             nc.vector.quantize_mx(
@@ -234,22 +236,23 @@ def tile_attend_gmw_tnh_kernel(tc, xT, dyT, hE, sw, tw, offs, offs2, out):
                 multiply(j, g, codes[:, g * P:(g + 1) * P], scales[:, g * P:(g + 1) * P])
 
         store(0)
-        slots = [factors[GPSIMD_PRODUCTS - 1][:], turned[-1][:], factors[CHUNKS - 1][:],
+        slots = [factors[GPSIMD_PRODUCTS - 1][:, 0:K_PASS], turned[-1][:], factors[CHUNKS - 1][:, 0:K_PASS],
                  dz_bf[0][:].rearrange("p n t -> p (n t)").bitcast(F32)[:, 0:K_PASS]]
         late = (D_TILES - GPSIMD_X_TILES) * PASSES
+        word_tiles = [keep.tile([P, K_PASS // 2], F32, name="late_words%d" % c, align_bytes=64) for c in range(late - 1)]
         for c in range(late):
             j, g = GPSIMD_X_TILES + c // PASSES, c % PASSES
             xe = slots[c]
             nc.vector.tensor_tensor(xe, x_tiles[j][:].indirect(edges(src_list, g)), sw_rows[g][:], MULT)
             move = nc.vector.tensor_copy if c == late - 1 else nc.scalar.copy
-            pair_words = (turned[0], turned[1], spare, turned[2])[c][:, 0:K_PASS // 2]
+            pair_words = (turned[0], turned[1], spare, factors[CHUNKS - 1])[c][:, 0:K_PASS // 2]
             move(
                 pair_words.bitcast(BF16).rearrange("p (u b r) -> p u b r", u=2, r=RUN),
                 xe.rearrange("p (b u r) -> p u b r", u=2, r=RUN),
             )
             bank = banks[X_BANKS[c]]
             turn_words(bank, pair_words)
-            words = keep.tile([P, K_PASS // 2], F32, name="late_words%d" % c, align_bytes=64)
+            words = word_tiles[min(c, late - 2)]
             move(words[:].rearrange("p (d u) -> p d u", u=2), bank[:, 0:2, :].rearrange("p u d -> p d u"))
             if c >= GPSIMD_X_TILES:
                 store(c - 1)

@@ -27,13 +27,15 @@ N_TILES = DV // P
 CHUNKS = N_TILES * PASSES
 GPSIMD_PRODUCTS = 4
 GPSIMD_SQUARES = ()
-H_BANKS = (0, 1, 2, 0, 3, 4, 5, 6)
-DY_BANKS = (1, 2, 0, 1, 3, 4, 5, 6)
-WORD_BANKS = (0, 1)
-X_BANKS = (7, 3, 7, 3)
 GPSIMD_X_TILES = 2
-FACTOR_LEAD = 2
-ACC_BANKS = (2, 0, 1, 4)
+GROUPS = ((0,), (1,), (2,), (3,), (4,), (5,), (6,), (7,))
+BLOCKS = K_PASS // (2 * RUN)
+SCALAR_BLOCKS = 8
+GROUP_BANKS = ((0,), (1,), (2,), (3,), (0,), (1,), (2,), (3,))
+DY_BANKS = (4, 5, 4, 5, 0, 1, 2, 3)
+WORD_BANKS = (4, 5)
+X_BANKS = (7, 0, 7, 0)
+ACC_BANKS = (6, 4, 5, 1)
 
 
 def tile_attend_gmw_tnh_kernel(tc, xT, dyT, hE, sw, tw, offs, offs2, out):
@@ -47,8 +49,7 @@ def tile_attend_gmw_tnh_kernel(tc, xT, dyT, hE, sw, tw, offs, offs2, out):
         dy_tiles = [keep.tile([P, V], F32, name="dy%d" % j) for j in range(N_TILES)]
         h_tiles = [keep.tile([P, K_PASS], F32, name="h%d" % c) for c in range(CHUNKS)]
         x_tiles = [keep.tile([P, V], F32, name="x%d" % j) for j in range(D_TILES)]
-        sw_rows = [keep.tile([P, K_PASS], F32, name="sw_rows%d" % g) for g in range(PASSES)]
-        tw_line = keep.tile([PASSES, K_PASS], F32, name="tw_line")
+        sw_all = keep.tile([P, E], F32, name="sw_all")
         tw_rows = keep.tile([P, K_PASS], F32, name="tw_rows")
         tw_cols = keep.tile([P, PASSES * 2, 2], F32, name="tw_cols")
         neg_tw_cols = keep.tile([P, PASSES * 2, 2], F32, name="neg_tw_cols")
@@ -67,24 +68,23 @@ def tile_attend_gmw_tnh_kernel(tc, xT, dyT, hE, sw, tw, offs, offs2, out):
         def load_x(j):
             nc.sync.dma_start(x_tiles[j][:], xT[j * P:(j + 1) * P, :])
 
-        def load_sw(g):
-            nc.sync.dma_start(sw_rows[g][:], sw[:, g * K_PASS:(g + 1) * K_PASS])
-
         def load_tw():
-            nc.sync.dma_start(tw_line[:], tw[0, :].rearrange("(g e) -> g e", g=PASSES))
+            nc.sync.dma_start(
+                tw_rows[0:2, :].rearrange("u (b r) -> u b r", r=RUN),
+                tw[0, :].rearrange("(b u r) -> u b r", u=2, r=RUN),
+            )
 
-        load_tw()
         load_x(0)
         nc.sync.dma_start(src_list[:], offs)
-        load_sw(0)
+        load_tw()
         load_h(0)
         load_x(1)
+        nc.sync.dma_start(sw_all[:], sw)
         load_h(1)
-        load_h(2)
         load_dy(0)
         nc.sync.dma_start(dst_list[:], offs2)
+        load_h(2)
         load_h(3)
-        load_sw(1)
         load_dy(1)
         load_h(4)
         load_dy(2)
@@ -95,23 +95,20 @@ def tile_attend_gmw_tnh_kernel(tc, xT, dyT, hE, sw, tw, offs, offs2, out):
         load_x(2)
         load_x(3)
 
-        nc.vector.tensor_copy(
-            tw_rows[0:PASSES, :].rearrange("g (u b r) -> g u b r", u=2, r=RUN),
-            tw_line[:].rearrange("g (b u r) -> g u b r", u=2, r=RUN),
-        )
         make_identity(nc, ident[:])
         tw_bank = banks[7]
-        for t in range(PACK):
-            u, v = divmod(t, 2)
-            nc.tensor.transpose(tw_bank[:, t, :], tw_rows[:, u * 2 * P + v:(u + 1) * 2 * P:2], ident[:])
+        for g in range(PASSES):
+            for v in range(2):
+                nc.tensor.transpose(tw_bank[:, 2 * g + v, :], tw_rows[:, g * 2 * P + v:(g + 1) * 2 * P:2], ident[:])
         nc.scalar.copy(tw_cols[:], tw_bank[:, :, 0:2])
         nc.scalar.activation(neg_tw_cols[:], tw_bank[:, :, 0:2], ACT.Copy, scale=-1.0)
 
         dz_bf = [keep.tile([P, DV, PACK], BF16, name="dz_bf%d" % g, align_bytes=64) for g in range(PASSES)]
         dz_codes = [keep.tile([P, DV], U32, name="dz_codes%d" % g, align_bytes=64) for g in range(PASSES)]
-        dz_scales = [keep.tile([P, DV], U8, name="dz_scales%d" % g, align_bytes=64) for g in range(PASSES)]
-        squares = [keep.tile([P, K_PASS], F32, name="h_sq%d" % s) for s in range(3)]
-        factors = [keep.tile([P, 3 * K_PASS // 2], F32, name="factor%d" % c, align_bytes=64) for c in range(CHUNKS)]
+        squares = [keep.tile([P, K_PASS], F32, name="h_sq%d" % c) for c in range(CHUNKS)]
+        factors = [keep.tile([P, K_PASS * len(group)], F32, name="factor%d" % q, align_bytes=64)
+                   for q, group in enumerate(GROUPS)]
+        picked = [keep.tile([P, K_PASS], F32, name="dy_g%d" % c, align_bytes=64) for c in range(CHUNKS)]
         turned = [keep.tile([P, K_PASS], F32, name="dy_turned%d" % c, align_bytes=64) for c in range(GPSIMD_PRODUCTS)]
 
         def in_runs(ap):
@@ -123,141 +120,214 @@ def tile_attend_gmw_tnh_kernel(tc, xT, dyT, hE, sw, tw, offs, offs2, out):
         def edges(index_list, g):
             return index_list[:, g * LIST_COLS:(g + 1) * LIST_COLS]
 
-        def turn_values(bank, src):
-            for t in range(PACK):
-                u, v = divmod(t, 2)
-                nc.tensor.transpose(bank[:, t, :], src[:, u * 2 * P + v:(u + 1) * 2 * P:2], ident[:])
-
-        def square(c):
-            h_sq = squares[c % len(squares)]
-            h_view = in_runs(h_tiles[c][:])
-            if c in GPSIMD_SQUARES:
-                nc.gpsimd.tensor_tensor(dealt(h_sq[:]), h_view, h_view, MULT)
-            else:
-                nc.scalar.activation(dealt(h_sq[:]), h_view, ACT.Square)
-
         def turn_words(bank, words):
             for u in range(2):
                 nc.tensor.transpose(bank[:, u, :], words[:, u * P:(u + 1) * P], ident[:])
 
+        def place(src, t):
+            u, v = divmod(t, 2)
+            return src[:, u * 2 * P + v:(u + 1) * 2 * P:2]
+
         early_pairs = []
-        for c in range(GPSIMD_X_TILES * PASSES):
-            j, g = divmod(c, PASSES)
-            x_g = keep.tile([P, K_PASS], F32, name="x_g%d" % c)
-            nc.vector.tensor_copy(dealt(x_g[:].bitcast(U32)), x_tiles[j][:].bitcast(U32).indirect(edges(src_list, g)))
-            pairs = keep.tile([P, K_PASS], BF16, name="early_pairs%d" % c)
+        for j in range(GPSIMD_X_TILES):
+            x_g = keep.tile([P, E], F32, name="x_g%d" % j)
+            for g in range(PASSES):
+                nc.vector.tensor_copy(
+                    x_g[:, g * K_PASS:(g + 1) * K_PASS].bitcast(U32), x_tiles[j][:].bitcast(U32).indirect(edges(src_list, g)),
+                )
+            pairs = keep.tile([P, E], BF16, name="early_pairs%d" % j)
             nc.gpsimd.tensor_tensor(
-                pairs[:].rearrange("p (u b r) -> p u b r", u=2, r=RUN),
-                x_g[:].rearrange("p (u b r) -> p u b r", u=2, r=RUN),
-                sw_rows[g][:].rearrange("p (b u r) -> p u b r", u=2, r=RUN),
-                MULT,
+                dealt(pairs[:]), in_runs(x_g[:]), in_runs(sw_all[:]), MULT,
             )
             early_pairs.append(pairs)
 
-        def make_factor(c):
-            g = c % PASSES
-            if c + 1 < CHUNKS:
-                square(c + 1)
-            h_bank = banks[H_BANKS[c]]
-            turn_values(h_bank, squares[c % len(squares)])
+        def square(c):
+            h_view = in_runs(h_tiles[c][:])
+            if c in GPSIMD_SQUARES:
+                nc.gpsimd.tensor_tensor(dealt(squares[c][:]), h_view, h_view, MULT)
+            else:
+                nc.scalar.activation(dealt(squares[c][:]), h_view, ACT.Square)
+
+        def make_factors(q):
+            group = GROUPS[q]
+            g = group[0] % PASSES
+            width = len(group) * P
+            room = [banks[b][:].rearrange("p t n -> p (t n)") for b in GROUP_BANKS[q]]
+            places = [room[t * width // K_PASS][:, t * width % K_PASS:t * width % K_PASS + width] for t in range(PACK)]
+            for side, c in enumerate(group):
+                for t in range(PACK):
+                    nc.tensor.transpose(places[t][:, side * P:(side + 1) * P], place(squares[c], t), ident[:])
             for t in range(PACK):
-                u, v = divmod(t, 2)
                 nc.scalar.activation(
-                    factors[c][:, t * P:(t + 1) * P], h_bank[:, t, :], ACT.Identity,
-                    bias=tw_cols[:, t, g:g + 1], scale=neg_tw_cols[:, t, g:g + 1],
+                    factors[q][:, t * width:(t + 1) * width], places[t], ACT.Identity,
+                    bias=tw_cols[:, 2 * g + t % 2, t // 2:t // 2 + 1],
+                    scale=neg_tw_cols[:, 2 * g + t % 2, t // 2:t // 2 + 1],
                 )
 
-        square(0)
-        for c in range(FACTOR_LEAD):
-            make_factor(c)
-        for c in range(CHUNKS):
+        def factor_of(c):
+            q = [c in group for group in GROUPS].index(True)
+            side = GROUPS[q].index(c)
+            return factors[q][:].rearrange("p (t n) -> p t n", t=PACK)[:, :, side * P:(side + 1) * P]
+
+        def gather_dy(c):
             j, g = divmod(c, PASSES)
-            if c + FACTOR_LEAD < CHUNKS:
-                make_factor(c + FACTOR_LEAD)
-            dy_g = keep.tile([P, K_PASS], F32, name="dy_g%d" % c)
-            nc.vector.tensor_copy(dealt(dy_g[:].bitcast(U32)), dy_tiles[j][:].bitcast(U32).indirect(edges(dst_list, g)))
-            factor = factors[c][:, 0:K_PASS].rearrange("p (t n) -> p t n", t=PACK)
+            nc.vector.tensor_copy(
+                dealt(picked[c][:].bitcast(U32)), dy_tiles[j][:].bitcast(U32).indirect(edges(dst_list, g)),
+            )
+
+        def product(c):
+            j, g = divmod(c, PASSES)
             dy_bank = banks[DY_BANKS[c]]
-            turn_values(dy_bank, dy_g)
+            for t in range(PACK):
+                nc.tensor.transpose(dy_bank[:, t, :], place(picked[c], t), ident[:])
             dz_part = dz_bf[g][:, j * P:(j + 1) * P, :]
             if c < GPSIMD_PRODUCTS:
                 dy_turned = turned[c][:].rearrange("p (n t) -> p n t", t=PACK)
                 nc.scalar.copy(dy_turned, dy_bank[:].rearrange("p t n -> p n t"))
-                nc.gpsimd.tensor_tensor(dz_part, dy_turned, factor.rearrange("p t n -> p n t"), MULT)
+                nc.gpsimd.tensor_tensor(dz_part, dy_turned, factor_of(c).rearrange("p t n -> p n t"), MULT)
             else:
                 nc.vector.tensor_tensor(
                     dz_part.rearrange("p (c i) t -> p c t i", i=4),
                     dy_bank[:].rearrange("p t (c i) -> p c t i", i=4),
-                    factor.rearrange("p t (c i) -> p c t i", i=4),
+                    factor_of(c).rearrange("p t (c i) -> p c t i", i=4),
                     MULT,
                 )
+
+        square(0)
+        make_factors(0)
+        square(1)
+        make_factors(1)
+        square(2)
+        square(3)
+        gather_dy(0)
+        product(0)
+        gather_dy(1)
+        product(1)
+        make_factors(2)
+        square(4)
+        gather_dy(2)
+        product(2)
+        make_factors(3)
+        gather_dy(3)
+        product(3)
+        make_factors(4)
+        square(5)
+        square(6)
+        square(7)
+        gather_dy(4)
+        gather_dy(5)
+        gather_dy(6)
+        gather_dy(7)
+        make_factors(5)
+        make_factors(6)
+        make_factors(7)
+        product(4)
+        product(5)
+        product(6)
+        product(7)
+
+        width = PASSES * P
+        planes = keep.tile([P, PASSES * DV + D_TILES * width], U8, name="planes", align_bytes=64)
+        first_late = PASSES * DV + GPSIMD_X_TILES * width
+        dz_scales = [planes[:, g * DV:(g + 1) * DV] for g in range(PASSES)]
 
         def multiply(j, g, codes, scales):
             nc.tensor.matmul_mx(
                 out=banks[ACC_BANKS[j]][:].rearrange("p t n -> p (t n)"),
                 lhsT=codes.bitcast(E4M3), lhsT_scale=scales,
-                rhs=dz_codes[g][:].bitcast(E5M2), rhs_scale=dz_scales[g][:],
+                rhs=dz_codes[g][:].bitcast(E5M2), rhs_scale=dz_scales[g],
                 start=(g == 0), stop=(g == PASSES - 1),
             )
 
+        last_factors = dz_bf[0][:].rearrange("p n t -> p (n t)").bitcast(F32)
+        spare = keep.tile([P, 2 * DV], F32, name="spare")
+        staged = [squares[0][:], spare[:, 0:DV], spare[:, DV:2 * DV], squares[1][:]]
+
         def store(j):
             acc = banks[ACC_BANKS[j]][:].rearrange("p t n -> p (t n)")
-            result = staged[j]
             pieces = 2 if j == D_TILES - 1 else 1
             width = DV // pieces
             for piece in range(pieces):
                 cols = slice(piece * width, (piece + 1) * width)
-                nc.scalar.copy(result[:, cols], acc[:, cols])
-                nc.sync.dma_start(out[j * P:(j + 1) * P, cols], result[:, cols])
+                nc.scalar.copy(staged[j][:, cols], acc[:, cols])
+                nc.sync.dma_start(out[j * P:(j + 1) * P, cols], staged[j][:, cols])
 
-        spare = keep.tile([P, DV], F32, name="spare")
-        staged = [factors[0], factors[CHUNKS - 1][:, K_PASS // 2:], spare, factors[1]]
-        early_words = [factors[CHUNKS - 3][:, 0:K_PASS], factors[CHUNKS - 2][:, 0:K_PASS]]
-        early_codes = []
+        room = keep.tile([P, GPSIMD_X_TILES * width], F32, name="early_codes", align_bytes=64)
+        code_room = [room[:, j * width:(j + 1) * width] for j in range(GPSIMD_X_TILES)]
+        early = []
         for j in range(GPSIMD_X_TILES):
             bank = banks[WORD_BANKS[j]]
-            for g in range(PASSES):
-                turn_words(bank[:, 2 * g:2 * g + 2, :], early_pairs[PASSES * j + g][:].bitcast(F32))
+            pair_words = early_pairs[j][:].bitcast(F32)
+            for place_pair in range(2 * PASSES):
+                nc.tensor.transpose(bank[:, place_pair, :], pair_words[:, place_pair * P:(place_pair + 1) * P], ident[:])
+            words = factors[5 + j]
             nc.scalar.copy(
-                early_words[j].rearrange("p (g d u) -> p g d u", g=PASSES, u=2),
-                bank[:].rearrange("p (g u) d -> p g d u", u=2),
+                words[:].rearrange("p (g d u) -> p g d u", g=PASSES, u=2),
+                bank[:].rearrange("p (u g) d -> p g d u", u=2),
             )
-            codes = keep.tile([P, PASSES * P], U32, name="early_codes%d" % j, align_bytes=64)
-            scales = keep.tile([P, PASSES * P], U8, name="early_scales%d" % j, align_bytes=64)
-            nc.vector.quantize_mx(out=codes[:].bitcast(E4M3), scales=scales[:], in_=early_words[j].bitcast(BF16))
-            early_codes.append((codes, scales))
-        for g in range(PASSES):
+            scales = planes[:, PASSES * DV + j * width:PASSES * DV + (j + 1) * width]
+            early.append((words, code_room[j].bitcast(U32), scales))
+
+        def quantize_early(j):
+            words, codes, scales = early[j]
+            nc.vector.quantize_mx(out=codes.bitcast(E4M3), scales=scales, in_=words[:].bitcast(BF16))
+
+        def quantize_dz(g):
             nc.vector.quantize_mx(
-                out=dz_codes[g][:].bitcast(E5M2), scales=dz_scales[g][:],
+                out=dz_codes[g][:].bitcast(E5M2), scales=dz_scales[g],
                 in_=dz_bf[g][:].rearrange("p n t -> p (n t)"),
             )
-        for j, (codes, scales) in enumerate(early_codes):
+
+        quantize_dz(0)
+        quantize_early(0)
+        quantize_dz(1)
+        for j in range(1, GPSIMD_X_TILES):
+            quantize_early(j)
+        for j, (words, codes, scales) in enumerate(early):
             for g in range(PASSES):
                 multiply(j, g, codes[:, g * P:(g + 1) * P], scales[:, g * P:(g + 1) * P])
-
         store(0)
-        slots = [factors[GPSIMD_PRODUCTS - 1][:, 0:K_PASS], turned[-1][:], factors[CHUNKS - 1][:, 0:K_PASS],
-                 dz_bf[0][:].rearrange("p n t -> p (n t)").bitcast(F32)[:, 0:K_PASS]]
+
+        slots = [factors[3][:, 0:K_PASS], turned[-1][:], last_factors[:, 0:K_PASS],
+                 dz_bf[1][:].rearrange("p n t -> p (n t)").bitcast(F32)[:, 0:K_PASS]]
+        pair_room = [turned[0], turned[1], spare[:, DV - 3 * P // 2:DV + P // 2], last_factors]
         late = (D_TILES - GPSIMD_X_TILES) * PASSES
         word_tiles = [keep.tile([P, K_PASS // 2], F32, name="late_words%d" % c, align_bytes=64) for c in range(late - 1)]
+
+        def finish(c):
+            j, g = GPSIMD_X_TILES + c // PASSES, c % PASSES
+            codes = keep.tile([P, P], U32, name="xe_codes%d" % c, align_bytes=64)
+            scales = planes[:, first_late + c * P:first_late + (c + 1) * P]
+            words = word_tiles[min(c, late - 2)]
+            nc.vector.quantize_mx(out=codes[:].bitcast(E4M3), scales=scales, in_=words[:].bitcast(BF16))
+            multiply(j, g, codes[:], scales)
+
         for c in range(late):
             j, g = GPSIMD_X_TILES + c // PASSES, c % PASSES
             xe = slots[c]
-            nc.vector.tensor_tensor(xe, x_tiles[j][:].indirect(edges(src_list, g)), sw_rows[g][:], MULT)
             move = nc.vector.tensor_copy if c == late - 1 else nc.scalar.copy
-            pair_words = (turned[0], turned[1], spare, factors[CHUNKS - 1])[c][:, 0:K_PASS // 2]
-            move(
-                pair_words.bitcast(BF16).rearrange("p (u b r) -> p u b r", u=2, r=RUN),
-                xe.rearrange("p (b u r) -> p u b r", u=2, r=RUN),
-            )
+            pair_words = pair_room[c][:, 0:K_PASS // 2]
+            pairs = pair_words.bitcast(BF16).rearrange("p (u b r) -> p u b r", u=2, r=RUN)
+            cuts = (0, SCALAR_BLOCKS, BLOCKS) if c == late - 1 else (0, BLOCKS)
+            for first, end in zip(cuts, cuts[1:]):
+                cols = slice(first * 2 * RUN, end * 2 * RUN)
+                nc.vector.tensor_tensor(
+                    xe[:, cols], x_tiles[j][:].indirect(edges(src_list, g)[:, 2 * first:2 * end]),
+                    sw_all[:, g * K_PASS:(g + 1) * K_PASS][:, cols], MULT,
+                )
+                (move if first else nc.scalar.copy)(
+                    pairs[:, :, first:end, :], xe[:, cols].rearrange("p (b u r) -> p u b r", u=2, r=RUN),
+                )
+            if c == late - 2:
+                finish(0)
+                finish(1)
             bank = banks[X_BANKS[c]]
             turn_words(bank, pair_words)
             words = word_tiles[min(c, late - 2)]
             move(words[:].rearrange("p (d u) -> p d u", u=2), bank[:, 0:2, :].rearrange("p u d -> p d u"))
-            if c >= GPSIMD_X_TILES:
-                store(c - 1)
-            codes = keep.tile([P, P], U32, name="xe_codes%d" % c, align_bytes=64)
-            scales = keep.tile([P, P], U8, name="xe_scales%d" % c, align_bytes=64)
-            nc.vector.quantize_mx(out=codes[:].bitcast(E4M3), scales=scales[:], in_=words[:].bitcast(BF16))
-            multiply(j, g, codes[:], scales[:])
+            if c == late - 2:
+                store(1)
+                store(2)
+            if c >= late - 2:
+                finish(c)
         store(D_TILES - 1)

@@ -25,17 +25,15 @@ LIST_COLS = K_PASS // 16
 D_TILES = D // P
 N_TILES = DV // P
 CHUNKS = N_TILES * PASSES
-GPSIMD_PRODUCTS = 4
-GPSIMD_SQUARES = ()
+GPSIMD_CHUNKS = 4
 GPSIMD_X_TILES = 2
-GROUPS = ((0,), (1,), (2,), (3,), (4,), (5,), (6,), (7,))
-BLOCKS = K_PASS // (2 * RUN)
-SCALAR_BLOCKS = 8
-GROUP_BANKS = ((0,), (1,), (2,), (3,), (0,), (1,), (2,), (3,))
+SPARE = 352
+LAST_EDGES = 128
+H_BANKS = (0, 1, 2, 3, 0, 1, 2, 3)
 DY_BANKS = (4, 5, 4, 5, 0, 1, 2, 3)
-WORD_BANKS = (4, 5)
-X_BANKS = (7, 0, 7, 0)
+X_BANKS = (4, 5, 7, 7, 0)
 ACC_BANKS = (6, 4, 5, 1)
+TW_BANK = 7
 
 
 def tile_attend_gmw_tnh_kernel(tc, xT, dyT, hE, sw, tw, offs, offs2, out):
@@ -44,12 +42,14 @@ def tile_attend_gmw_tnh_kernel(tc, xT, dyT, hE, sw, tw, offs, offs2, out):
         keep = ctx.enter_context(tc.tile_pool(name="keep", bufs=1))
         psum = ctx.enter_context(tc.psum_pool(name="psum", bufs=1))
 
-        dst_list = keep.tile([P, E // 16], U16, name="dst_list")
+        whole_dy = GPSIMD_CHUNKS // PASSES
+        last = D_TILES - 1
         src_list = keep.tile([P, E // 16], U16, name="src_list")
-        dy_tiles = [keep.tile([P, V], F32, name="dy%d" % j) for j in range(N_TILES)]
+        dst_list = keep.tile([P, E // 16], U16, name="dst_list")
+        x_tiles = [keep.tile([P, V + (SPARE if j < last else 0)], F32, name="x%d" % j) for j in range(D_TILES)]
+        dy_tiles = [keep.tile([P, V + (SPARE if j >= whole_dy else 0)], F32, name="dy%d" % j) for j in range(N_TILES)]
         h_tiles = [keep.tile([P, K_PASS], F32, name="h%d" % c) for c in range(CHUNKS)]
-        x_tiles = [keep.tile([P, V], F32, name="x%d" % j) for j in range(D_TILES)]
-        sw_all = keep.tile([P, E], F32, name="sw_all")
+        sw_rows = keep.tile([P, E], F32, name="sw_rows")
         tw_rows = keep.tile([P, K_PASS], F32, name="tw_rows")
         tw_cols = keep.tile([P, PASSES * 2, 2], F32, name="tw_cols")
         neg_tw_cols = keep.tile([P, PASSES * 2, 2], F32, name="neg_tw_cols")
@@ -58,28 +58,25 @@ def tile_attend_gmw_tnh_kernel(tc, xT, dyT, hE, sw, tw, offs, offs2, out):
 
         nc.vector.memset(tw_rows[:], 0.0)
 
+        def load_x(j):
+            nc.sync.dma_start(x_tiles[j][:, 0:V], xT[j * P:(j + 1) * P, :])
+
         def load_dy(j):
-            nc.sync.dma_start(dy_tiles[j][:], dyT[j * P:(j + 1) * P, :])
+            nc.sync.dma_start(dy_tiles[j][:, 0:V], dyT[j * P:(j + 1) * P, :])
 
         def load_h(c):
             j, g = divmod(c, PASSES)
             nc.sync.dma_start(h_tiles[c][:], hE[j * P:(j + 1) * P, g * K_PASS:(g + 1) * K_PASS])
 
-        def load_x(j):
-            nc.sync.dma_start(x_tiles[j][:], xT[j * P:(j + 1) * P, :])
-
-        def load_tw():
-            nc.sync.dma_start(
-                tw_rows[0:2, :].rearrange("u (b r) -> u b r", r=RUN),
-                tw[0, :].rearrange("(b u r) -> u b r", u=2, r=RUN),
-            )
-
         load_x(0)
         nc.sync.dma_start(src_list[:], offs)
-        load_tw()
+        nc.sync.dma_start(
+            tw_rows[0:2, :].rearrange("u (b r) -> u b r", r=RUN),
+            tw[0, :].rearrange("(b u r) -> u b r", u=2, r=RUN),
+        )
         load_h(0)
         load_x(1)
-        nc.sync.dma_start(sw_all[:], sw)
+        nc.sync.dma_start(sw_rows[:], sw)
         load_h(1)
         load_dy(0)
         nc.sync.dma_start(dst_list[:], offs2)
@@ -89,27 +86,21 @@ def tile_attend_gmw_tnh_kernel(tc, xT, dyT, hE, sw, tw, offs, offs2, out):
         load_h(4)
         load_dy(2)
         load_dy(3)
-        load_h(5)
-        load_h(6)
-        load_h(7)
+        for c in range(GPSIMD_CHUNKS + 1, CHUNKS):
+            load_h(c)
         load_x(2)
         load_x(3)
 
         make_identity(nc, ident[:])
-        tw_bank = banks[7]
+        for window in x_tiles[:GPSIMD_X_TILES] + dy_tiles[whole_dy:] + x_tiles[GPSIMD_X_TILES:last]:
+            nc.gpsimd.memset(window[:, V:], 0.0)
         for g in range(PASSES):
             for v in range(2):
-                nc.tensor.transpose(tw_bank[:, 2 * g + v, :], tw_rows[:, g * 2 * P + v:(g + 1) * 2 * P:2], ident[:])
-        nc.scalar.copy(tw_cols[:], tw_bank[:, :, 0:2])
-        nc.scalar.activation(neg_tw_cols[:], tw_bank[:, :, 0:2], ACT.Copy, scale=-1.0)
-
-        dz_bf = [keep.tile([P, DV, PACK], BF16, name="dz_bf%d" % g, align_bytes=64) for g in range(PASSES)]
-        dz_codes = [keep.tile([P, DV], U32, name="dz_codes%d" % g, align_bytes=64) for g in range(PASSES)]
-        squares = [keep.tile([P, K_PASS], F32, name="h_sq%d" % c) for c in range(CHUNKS)]
-        factors = [keep.tile([P, K_PASS * len(group)], F32, name="factor%d" % q, align_bytes=64)
-                   for q, group in enumerate(GROUPS)]
-        picked = [keep.tile([P, K_PASS], F32, name="dy_g%d" % c, align_bytes=64) for c in range(CHUNKS)]
-        turned = [keep.tile([P, K_PASS], F32, name="dy_turned%d" % c, align_bytes=64) for c in range(GPSIMD_PRODUCTS)]
+                nc.tensor.transpose(
+                    banks[TW_BANK][:, 2 * g + v, :], tw_rows[:, g * 2 * P + v:(g + 1) * 2 * P:2], ident[:],
+                )
+        nc.scalar.copy(tw_cols[:], banks[TW_BANK][:, :, 0:2])
+        nc.scalar.activation(neg_tw_cols[:], banks[TW_BANK][:, :, 0:2], ACT.Copy, scale=-1.0)
 
         def in_runs(ap):
             return ap.rearrange("p (b u r) -> p b u r", u=2, r=RUN)
@@ -120,214 +111,189 @@ def tile_attend_gmw_tnh_kernel(tc, xT, dyT, hE, sw, tw, offs, offs2, out):
         def edges(index_list, g):
             return index_list[:, g * LIST_COLS:(g + 1) * LIST_COLS]
 
-        def turn_words(bank, words):
-            for u in range(2):
-                nc.tensor.transpose(bank[:, u, :], words[:, u * P:(u + 1) * P], ident[:])
+        def turn_values(bank, src, g, passes):
+            for t in range(PACK):
+                u, v = divmod(t, 2)
+                first = (u * passes + g) * 2 * P
+                nc.tensor.transpose(bank[:, t, :], src[:, first + v:first + 2 * P:2], ident[:])
 
-        def place(src, t):
-            u, v = divmod(t, 2)
-            return src[:, u * 2 * P + v:(u + 1) * 2 * P:2]
+        def turn_words(bank, words, passes):
+            for run in range(2 * passes):
+                nc.tensor.transpose(bank[:, run, :], words[:, run * P:(run + 1) * P], ident[:])
 
-        early_pairs = []
-        for j in range(GPSIMD_X_TILES):
-            x_g = keep.tile([P, E], F32, name="x_g%d" % j)
-            for g in range(PASSES):
-                nc.vector.tensor_copy(
-                    x_g[:, g * K_PASS:(g + 1) * K_PASS].bitcast(U32), x_tiles[j][:].bitcast(U32).indirect(edges(src_list, g)),
-                )
-            pairs = keep.tile([P, E], BF16, name="early_pairs%d" % j)
-            nc.gpsimd.tensor_tensor(
-                dealt(pairs[:]), in_runs(x_g[:]), in_runs(sw_all[:]), MULT,
+        def weave_words(move, words, bank, passes):
+            move(
+                words.rearrange("p (g d u) -> p g d u", g=passes, u=2),
+                bank[:, 0:2 * passes, :].rearrange("p (u g) d -> p g d u", u=2),
             )
-            early_pairs.append(pairs)
+
+        x_pairs = []
+        for j in range(GPSIMD_X_TILES):
+            x_picked = keep.tile([P, E], F32, name="x_picked%d" % j)
+            nc.vector.tensor_copy(x_picked[:].bitcast(U32), x_tiles[j][:].bitcast(U32).indirect(src_list[:]))
+            pairs = keep.tile([P, E], BF16, name="x_pairs%d" % j)
+            nc.gpsimd.tensor_tensor(dealt(pairs[:]), in_runs(x_picked[:]), in_runs(sw_rows[:]), MULT)
+            x_pairs.append(pairs)
+
+        dz_bf = [keep.tile([P, DV, PACK], BF16, name="dz_bf%d" % g, align_bytes=64) for g in range(PASSES)]
+        squares = [keep.tile([P, K_PASS], F32, name="h_sq%d" % c) for c in range(CHUNKS)]
+        factor_room = keep.tile([P, CHUNKS * K_PASS], F32, name="factor_room", align_bytes=64)
+        factors = [factor_room[:, c * K_PASS:(c + 1) * K_PASS] for c in range(CHUNKS)]
+        turned = [keep.tile([P, K_PASS], F32, name="dy_turned%d" % c) for c in range(GPSIMD_CHUNKS)]
 
         def square(c):
-            h_view = in_runs(h_tiles[c][:])
-            if c in GPSIMD_SQUARES:
-                nc.gpsimd.tensor_tensor(dealt(squares[c][:]), h_view, h_view, MULT)
-            else:
-                nc.scalar.activation(dealt(squares[c][:]), h_view, ACT.Square)
+            nc.scalar.activation(dealt(squares[c][:]), in_runs(h_tiles[c][:]), ACT.Square)
 
-        def make_factors(q):
-            group = GROUPS[q]
-            g = group[0] % PASSES
-            width = len(group) * P
-            room = [banks[b][:].rearrange("p t n -> p (t n)") for b in GROUP_BANKS[q]]
-            places = [room[t * width // K_PASS][:, t * width % K_PASS:t * width % K_PASS + width] for t in range(PACK)]
-            for side, c in enumerate(group):
-                for t in range(PACK):
-                    nc.tensor.transpose(places[t][:, side * P:(side + 1) * P], place(squares[c], t), ident[:])
+        def make_factor(c):
+            g = c % PASSES
+            bank = banks[H_BANKS[c]]
+            turn_values(bank, squares[c], 0, 1)
             for t in range(PACK):
+                u, v = divmod(t, 2)
                 nc.scalar.activation(
-                    factors[q][:, t * width:(t + 1) * width], places[t], ACT.Identity,
-                    bias=tw_cols[:, 2 * g + t % 2, t // 2:t // 2 + 1],
-                    scale=neg_tw_cols[:, 2 * g + t % 2, t // 2:t // 2 + 1],
+                    factors[c][:, t * P:(t + 1) * P], bank[:, t, :], ACT.Identity,
+                    bias=tw_cols[:, 2 * g + v, u:u + 1], scale=neg_tw_cols[:, 2 * g + v, u:u + 1],
                 )
 
-        def factor_of(c):
-            q = [c in group for group in GROUPS].index(True)
-            side = GROUPS[q].index(c)
-            return factors[q][:].rearrange("p (t n) -> p t n", t=PACK)[:, :, side * P:(side + 1) * P]
-
-        def gather_dy(c):
+        def dz_part(c):
             j, g = divmod(c, PASSES)
+            return dz_bf[g][:, j * P:(j + 1) * P, :]
+
+        def dz_on_gpsimd(c):
+            j, g = divmod(c, PASSES)
+            picked = keep.tile([P, K_PASS], F32, name="dy_picked%d" % c)
             nc.vector.tensor_copy(
-                dealt(picked[c][:].bitcast(U32)), dy_tiles[j][:].bitcast(U32).indirect(edges(dst_list, g)),
+                dealt(picked[:].bitcast(U32)), dy_tiles[j][:].bitcast(U32).indirect(edges(dst_list, g)),
+            )
+            bank = banks[DY_BANKS[c]]
+            turn_values(bank, picked, 0, 1)
+            dy_turned = turned[c][:].rearrange("p (n t) -> p n t", t=PACK)
+            nc.scalar.copy(dy_turned, bank[:].rearrange("p t n -> p n t"))
+            nc.gpsimd.tensor_tensor(dz_part(c), dy_turned, factors[c].rearrange("p (t n) -> p n t", t=PACK), MULT)
+
+        def dz_on_vector(c, picked):
+            bank = banks[DY_BANKS[c]]
+            turn_values(bank, picked, c % PASSES, PASSES)
+            nc.vector.tensor_tensor(
+                dz_part(c).rearrange("p (c i) t -> p c t i", i=4),
+                bank[:].rearrange("p t (c i) -> p c t i", i=4),
+                factors[c].rearrange("p (t c i) -> p c t i", t=PACK, i=4),
+                MULT,
             )
 
-        def product(c):
-            j, g = divmod(c, PASSES)
-            dy_bank = banks[DY_BANKS[c]]
-            for t in range(PACK):
-                nc.tensor.transpose(dy_bank[:, t, :], place(picked[c], t), ident[:])
-            dz_part = dz_bf[g][:, j * P:(j + 1) * P, :]
-            if c < GPSIMD_PRODUCTS:
-                dy_turned = turned[c][:].rearrange("p (n t) -> p n t", t=PACK)
-                nc.scalar.copy(dy_turned, dy_bank[:].rearrange("p t n -> p n t"))
-                nc.gpsimd.tensor_tensor(dz_part, dy_turned, factor_of(c).rearrange("p t n -> p n t"), MULT)
-            else:
-                nc.vector.tensor_tensor(
-                    dz_part.rearrange("p (c i) t -> p c t i", i=4),
-                    dy_bank[:].rearrange("p t (c i) -> p c t i", i=4),
-                    factor_of(c).rearrange("p t (c i) -> p c t i", i=4),
-                    MULT,
-                )
-
         square(0)
-        make_factors(0)
+        make_factor(0)
         square(1)
-        make_factors(1)
+        make_factor(1)
         square(2)
         square(3)
-        gather_dy(0)
-        product(0)
-        gather_dy(1)
-        product(1)
-        make_factors(2)
+        dz_on_gpsimd(0)
+        dz_on_gpsimd(1)
+        make_factor(2)
         square(4)
-        gather_dy(2)
-        product(2)
-        make_factors(3)
-        gather_dy(3)
-        product(3)
-        make_factors(4)
-        square(5)
-        square(6)
-        square(7)
-        gather_dy(4)
-        gather_dy(5)
-        gather_dy(6)
-        gather_dy(7)
-        make_factors(5)
-        make_factors(6)
-        make_factors(7)
-        product(4)
-        product(5)
-        product(6)
-        product(7)
+        dz_on_gpsimd(2)
+        make_factor(3)
+        dz_on_gpsimd(3)
+        make_factor(4)
+        for c in range(GPSIMD_CHUNKS + 1, CHUNKS):
+            square(c)
+        dy_picked = []
+        for j in range(whole_dy, N_TILES):
+            picked = keep.tile([P, E], F32, name="dy_both%d" % j)
+            nc.vector.tensor_copy(dealt(picked[:].bitcast(U32)), dy_tiles[j][:].bitcast(U32).indirect(dst_list[:]))
+            dy_picked.extend([picked] * PASSES)
+        for c in range(GPSIMD_CHUNKS + 1, CHUNKS):
+            make_factor(c)
+        for c in range(GPSIMD_CHUNKS, CHUNKS):
+            dz_on_vector(c, dy_picked[c - GPSIMD_CHUNKS])
 
         width = PASSES * P
-        planes = keep.tile([P, PASSES * DV + D_TILES * width], U8, name="planes", align_bytes=64)
-        first_late = PASSES * DV + GPSIMD_X_TILES * width
-        dz_scales = [planes[:, g * DV:(g + 1) * DV] for g in range(PASSES)]
+        dz_codes = [keep.tile([P, DV], U32, name="dz_codes%d" % g, align_bytes=64) for g in range(PASSES)]
+        dz_scales = [keep.tile([P, DV], U8, name="dz_scales%d" % g, align_bytes=64) for g in range(PASSES)]
+        x_codes = keep.tile([P, D_TILES * width], U32, name="x_codes", align_bytes=64)
+        x_scales = keep.tile([P, D_TILES * width], U8, name="x_scales", align_bytes=64)
 
-        def multiply(j, g, codes, scales):
+        def quantize_dz(g):
+            nc.vector.quantize_mx(
+                out=dz_codes[g][:].bitcast(E5M2), scales=dz_scales[g][:],
+                in_=dz_bf[g][:].rearrange("p n t -> p (n t)"),
+            )
+
+        def quantize_x(first, words):
+            cols = slice(first * P, first * P + words.shape[1] // 2)
+            nc.vector.quantize_mx(out=x_codes[:, cols].bitcast(E4M3), scales=x_scales[:, cols], in_=words.bitcast(BF16))
+
+        def multiply(j, g):
+            cols = slice((PASSES * j + g) * P, (PASSES * j + g + 1) * P)
             nc.tensor.matmul_mx(
                 out=banks[ACC_BANKS[j]][:].rearrange("p t n -> p (t n)"),
-                lhsT=codes.bitcast(E4M3), lhsT_scale=scales,
-                rhs=dz_codes[g][:].bitcast(E5M2), rhs_scale=dz_scales[g],
+                lhsT=x_codes[:, cols].bitcast(E4M3), lhsT_scale=x_scales[:, cols],
+                rhs=dz_codes[g][:].bitcast(E5M2), rhs_scale=dz_scales[g][:],
                 start=(g == 0), stop=(g == PASSES - 1),
             )
 
-        last_factors = dz_bf[0][:].rearrange("p n t -> p (n t)").bitcast(F32)
         spare = keep.tile([P, 2 * DV], F32, name="spare")
         staged = [squares[0][:], spare[:, 0:DV], spare[:, DV:2 * DV], squares[1][:]]
 
         def store(j):
             acc = banks[ACC_BANKS[j]][:].rearrange("p t n -> p (t n)")
-            pieces = 2 if j == D_TILES - 1 else 1
-            width = DV // pieces
+            pieces = 2 if j == last else 1
+            piece_cols = DV // pieces
             for piece in range(pieces):
-                cols = slice(piece * width, (piece + 1) * width)
+                cols = slice(piece * piece_cols, (piece + 1) * piece_cols)
                 nc.scalar.copy(staged[j][:, cols], acc[:, cols])
                 nc.sync.dma_start(out[j * P:(j + 1) * P, cols], staged[j][:, cols])
 
-        room = keep.tile([P, GPSIMD_X_TILES * width], F32, name="early_codes", align_bytes=64)
-        code_room = [room[:, j * width:(j + 1) * width] for j in range(GPSIMD_X_TILES)]
-        early = []
+        early_words = factor_room[:, (CHUNKS - 3) * K_PASS:(CHUNKS - 1) * K_PASS]
         for j in range(GPSIMD_X_TILES):
-            bank = banks[WORD_BANKS[j]]
-            pair_words = early_pairs[j][:].bitcast(F32)
-            for place_pair in range(2 * PASSES):
-                nc.tensor.transpose(bank[:, place_pair, :], pair_words[:, place_pair * P:(place_pair + 1) * P], ident[:])
-            words = factors[5 + j]
-            nc.scalar.copy(
-                words[:].rearrange("p (g d u) -> p g d u", g=PASSES, u=2),
-                bank[:].rearrange("p (u g) d -> p g d u", u=2),
-            )
-            scales = planes[:, PASSES * DV + j * width:PASSES * DV + (j + 1) * width]
-            early.append((words, code_room[j].bitcast(U32), scales))
-
-        def quantize_early(j):
-            words, codes, scales = early[j]
-            nc.vector.quantize_mx(out=codes.bitcast(E4M3), scales=scales, in_=words[:].bitcast(BF16))
-
-        def quantize_dz(g):
-            nc.vector.quantize_mx(
-                out=dz_codes[g][:].bitcast(E5M2), scales=dz_scales[g],
-                in_=dz_bf[g][:].rearrange("p n t -> p (n t)"),
-            )
-
+            turn_words(banks[X_BANKS[j]], x_pairs[j][:].bitcast(F32), PASSES)
+            weave_words(nc.scalar.copy, early_words[:, j * K_PASS:(j + 1) * K_PASS], banks[X_BANKS[j]], PASSES)
         quantize_dz(0)
-        quantize_early(0)
+        quantize_x(0, early_words[:, 0:K_PASS])
         quantize_dz(1)
-        for j in range(1, GPSIMD_X_TILES):
-            quantize_early(j)
-        for j, (words, codes, scales) in enumerate(early):
+        quantize_x(PASSES, early_words[:, K_PASS:2 * K_PASS])
+        for j in range(GPSIMD_X_TILES):
             for g in range(PASSES):
-                multiply(j, g, codes[:, g * P:(g + 1) * P], scales[:, g * P:(g + 1) * P])
+                multiply(j, g)
         store(0)
 
-        slots = [factors[3][:, 0:K_PASS], turned[-1][:], last_factors[:, 0:K_PASS],
-                 dz_bf[1][:].rearrange("p n t -> p (n t)").bitcast(F32)[:, 0:K_PASS]]
-        pair_room = [turned[0], turned[1], spare[:, DV - 3 * P // 2:DV + P // 2], last_factors]
-        late = (D_TILES - GPSIMD_X_TILES) * PASSES
-        word_tiles = [keep.tile([P, K_PASS // 2], F32, name="late_words%d" % c, align_bytes=64) for c in range(late - 1)]
+        j = GPSIMD_X_TILES
+        xe = factor_room[:, (GPSIMD_CHUNKS - 2) * K_PASS:GPSIMD_CHUNKS * K_PASS]
+        nc.vector.tensor_tensor(xe, x_tiles[j][:].indirect(src_list[:]), sw_rows[:], MULT)
+        nc.scalar.copy(dealt(turned[0][:].bitcast(BF16)), in_runs(xe))
+        turn_words(banks[X_BANKS[j]], turned[0], PASSES)
+        weave_words(nc.scalar.copy, factors[0], banks[X_BANKS[j]], PASSES)
 
-        def finish(c):
-            j, g = GPSIMD_X_TILES + c // PASSES, c % PASSES
-            codes = keep.tile([P, P], U32, name="xe_codes%d" % c, align_bytes=64)
-            scales = planes[:, first_late + c * P:first_late + (c + 1) * P]
-            words = word_tiles[min(c, late - 2)]
-            nc.vector.quantize_mx(out=codes[:].bitcast(E4M3), scales=scales, in_=words[:].bitcast(BF16))
-            multiply(j, g, codes[:], scales)
-
-        for c in range(late):
-            j, g = GPSIMD_X_TILES + c // PASSES, c % PASSES
-            xe = slots[c]
-            move = nc.vector.tensor_copy if c == late - 1 else nc.scalar.copy
-            pair_words = pair_room[c][:, 0:K_PASS // 2]
-            pairs = pair_words.bitcast(BF16).rearrange("p (u b r) -> p u b r", u=2, r=RUN)
-            cuts = (0, SCALAR_BLOCKS, BLOCKS) if c == late - 1 else (0, BLOCKS)
+        dz_room = [dz_bf[g][:].rearrange("p n t -> p (n t)").bitcast(F32) for g in range(PASSES)]
+        pair_room = [spare[:, DV - 3 * P // 2:DV + P // 2], dz_room[0][:, 0:K_PASS // 2]]
+        last_words = keep.tile([P, K_PASS // 2], F32, name="last_words", align_bytes=64)
+        for g in range(PASSES):
+            final = g == PASSES - 1
+            move = nc.vector.tensor_copy if final else nc.scalar.copy
+            pairs = pair_room[g].bitcast(BF16).rearrange("p (u b r) -> p u b r", u=2, r=RUN)
+            cuts = (0, K_PASS - LAST_EDGES, K_PASS) if final else (0, K_PASS)
             for first, end in zip(cuts, cuts[1:]):
-                cols = slice(first * 2 * RUN, end * 2 * RUN)
+                cols = slice(first, end)
+                xe = dz_room[g][:, cols]
                 nc.vector.tensor_tensor(
-                    xe[:, cols], x_tiles[j][:].indirect(edges(src_list, g)[:, 2 * first:2 * end]),
-                    sw_all[:, g * K_PASS:(g + 1) * K_PASS][:, cols], MULT,
+                    xe,
+                    x_tiles[last][:].indirect(edges(src_list, g)[:, cols.start // 16:cols.stop // 16]),
+                    sw_rows[:, g * K_PASS:(g + 1) * K_PASS][:, cols], MULT,
                 )
-                (move if first else nc.scalar.copy)(
-                    pairs[:, :, first:end, :], xe[:, cols].rearrange("p (b u r) -> p u b r", u=2, r=RUN),
+                (move if end == K_PASS else nc.scalar.copy)(
+                    pairs[:, :, cols.start // (2 * RUN):cols.stop // (2 * RUN), :],
+                    xe.rearrange("p (b u r) -> p u b r", u=2, r=RUN),
                 )
-            if c == late - 2:
-                finish(0)
-                finish(1)
-            bank = banks[X_BANKS[c]]
-            turn_words(bank, pair_words)
-            words = word_tiles[min(c, late - 2)]
-            move(words[:].rearrange("p (d u) -> p d u", u=2), bank[:, 0:2, :].rearrange("p u d -> p d u"))
-            if c == late - 2:
+            if not final:
+                quantize_x(PASSES * j, factors[0])
+                multiply(j, 0)
+                multiply(j, 1)
+            bank = banks[X_BANKS[last + g]]
+            turn_words(bank, pair_room[g], 1)
+            weave_words(move, last_words[:], bank, 1)
+            if not final:
                 store(1)
                 store(2)
-            if c >= late - 2:
-                finish(c)
-        store(D_TILES - 1)
+            quantize_x(PASSES * last + g, last_words[:])
+            multiply(last, g)
+        store(last)

@@ -22,18 +22,13 @@ K_PASS = P * PACK
 PASSES = E // K_PASS
 RUN = 16
 LIST_COLS = K_PASS // 16
-D_TILES = D // P
-N_TILES = DV // P
-CHUNKS = N_TILES * PASSES
-GPSIMD_CHUNKS = 4
-GPSIMD_X_TILES = 2
-SPARE = 352
-LAST_EDGES = 128
-H_BANKS = (0, 1, 2, 3, 0, 1, 2, 3)
-DY_BANKS = (4, 5, 4, 5, 0, 1, 2, 3)
-X_BANKS = (4, 5, 7, 7, 0)
-ACC_BANKS = (6, 4, 5, 1)
-TW_BANK = 7
+TILES = D // P
+PAIRS = TILES // 2
+W_BANK = 7
+ROOMS = {
+    ("x_bf", 0): "dy0", ("dz_bf", 0): "dy1", ("factor", 0, 1): "x2", ("factor", 1, 0): "x3",
+    ("x_pairs", 1, 1): "h0_1",
+}
 
 
 def tile_attend_gmw_tnh_kernel(tc, xT, dyT, hE, sw, tw, offs, offs2, out):
@@ -42,65 +37,86 @@ def tile_attend_gmw_tnh_kernel(tc, xT, dyT, hE, sw, tw, offs, offs2, out):
         keep = ctx.enter_context(tc.tile_pool(name="keep", bufs=1))
         psum = ctx.enter_context(tc.psum_pool(name="psum", bufs=1))
 
-        whole_dy = GPSIMD_CHUNKS // PASSES
-        last = D_TILES - 1
+        def room(name, width, dtype, tag=None):
+            return keep.tile([P, width], dtype, name=name, tag=tag or name, align_bytes=64)
+
+        def grid(name, width, dtype, count=TILES):
+            return [[room("%s%d_%d" % (name, j, g), width, dtype, ROOMS.get((name, j, g))) for g in range(PASSES)] for j in range(count)]
+
         src_list = keep.tile([P, E // 16], U16, name="src_list")
         dst_list = keep.tile([P, E // 16], U16, name="dst_list")
-        x_tiles = [keep.tile([P, V + (SPARE if j < last else 0)], F32, name="x%d" % j) for j in range(D_TILES)]
-        dy_tiles = [keep.tile([P, V + (SPARE if j >= whole_dy else 0)], F32, name="dy%d" % j) for j in range(N_TILES)]
-        h_tiles = [keep.tile([P, K_PASS], F32, name="h%d" % c) for c in range(CHUNKS)]
-        sw_rows = keep.tile([P, E], F32, name="sw_rows")
-        tw_rows = keep.tile([P, K_PASS], F32, name="tw_rows")
-        tw_cols = keep.tile([P, PASSES * 2, 2], F32, name="tw_cols")
-        neg_tw_cols = keep.tile([P, PASSES * 2, 2], F32, name="neg_tw_cols")
+        x_tiles = [room("x%d" % j, V, F32) for j in range(TILES)]
+        dy_tiles = [room("dy%d" % k, V, F32) for k in range(TILES)]
+        h_parts = grid("h", K_PASS, F32)
+        sw_rows = [room("sw_rows%d" % g, K_PASS, F32) for g in range(PASSES)]
+        w_rows = room("w_rows", K_PASS, F32)
+        tw_cols = keep.tile([P, PASSES, 2, 2], F32, name="tw_cols")
+        neg_tw_cols = keep.tile([P, PASSES, 2, 2], F32, name="neg_tw_cols")
+        sw_cols = keep.tile([P, PASSES, 2, 2], F32, name="sw_cols")
         ident = keep.tile([P, P], F32, name="ident")
         banks = [psum.tile([P, PACK, P], F32, name="bank%d" % b) for b in range(8)]
 
-        nc.vector.memset(tw_rows[:], 0.0)
+        nc.vector.memset(w_rows[:], 0.0)
+
+        def rows(j):
+            return slice(j * P, (j + 1) * P)
+
+        def edge_cols(g):
+            return slice(g * K_PASS, (g + 1) * K_PASS)
 
         def load_x(j):
-            nc.sync.dma_start(x_tiles[j][:, 0:V], xT[j * P:(j + 1) * P, :])
+            nc.sync.dma_start(x_tiles[j][:], xT[rows(j), :])
 
-        def load_dy(j):
-            nc.sync.dma_start(dy_tiles[j][:, 0:V], dyT[j * P:(j + 1) * P, :])
+        def load_dy(k):
+            nc.sync.dma_start(dy_tiles[k][:], dyT[rows(k), :])
 
-        def load_h(c):
-            j, g = divmod(c, PASSES)
-            nc.sync.dma_start(h_tiles[c][:], hE[j * P:(j + 1) * P, g * K_PASS:(g + 1) * K_PASS])
+        def load_h(k, g):
+            nc.sync.dma_start(h_parts[k][g][:], hE[rows(k), edge_cols(g)])
 
+        def load_sw(g):
+            nc.sync.dma_start(sw_rows[g][:], sw[:, edge_cols(g)])
+
+        def load_row(first, weights):
+            nc.sync.dma_start(
+                w_rows[first:first + 2, :].rearrange("u (b r) -> u b r", r=RUN),
+                weights[0, :].rearrange("(b u r) -> u b r", u=2, r=RUN),
+            )
+
+        load_h(0, 0)
         load_x(0)
         nc.sync.dma_start(src_list[:], offs)
-        nc.sync.dma_start(
-            tw_rows[0:2, :].rearrange("u (b r) -> u b r", r=RUN),
-            tw[0, :].rearrange("(b u r) -> u b r", u=2, r=RUN),
-        )
-        load_h(0)
-        load_x(1)
-        nc.sync.dma_start(sw_rows[:], sw)
-        load_h(1)
+        load_row(0, tw)
+        load_row(2, sw)
         load_dy(0)
         nc.sync.dma_start(dst_list[:], offs2)
-        load_h(2)
-        load_h(3)
+        load_h(1, 0)
+        load_sw(1)
+        load_x(1)
         load_dy(1)
-        load_h(4)
-        load_dy(2)
-        load_dy(3)
-        for c in range(GPSIMD_CHUNKS + 1, CHUNKS):
-            load_h(c)
+        load_h(0, 1)
+        load_h(1, 1)
+        load_sw(0)
         load_x(2)
+        load_dy(2)
+        load_h(2, 0)
+        load_h(3, 0)
         load_x(3)
+        load_dy(3)
+        load_h(2, 1)
+        load_h(3, 1)
 
         make_identity(nc, ident[:])
-        for window in x_tiles[:GPSIMD_X_TILES] + dy_tiles[whole_dy:] + x_tiles[GPSIMD_X_TILES:last]:
-            nc.gpsimd.memset(window[:, V:], 0.0)
-        for g in range(PASSES):
-            for v in range(2):
-                nc.tensor.transpose(
-                    banks[TW_BANK][:, 2 * g + v, :], tw_rows[:, g * 2 * P + v:(g + 1) * 2 * P:2], ident[:],
-                )
-        nc.scalar.copy(tw_cols[:], banks[TW_BANK][:, :, 0:2])
-        nc.scalar.activation(neg_tw_cols[:], banks[TW_BANK][:, :, 0:2], ACT.Copy, scale=-1.0)
+
+        def turn_weights():
+            for g in range(PASSES):
+                for v in range(2):
+                    nc.tensor.transpose(banks[W_BANK][:, 2 * g + v, :], w_rows[:, g * 2 * P + v:(g + 1) * 2 * P:2], ident[:])
+
+        def copy_weights():
+            tw_turned = banks[W_BANK][:, :, 0:2].rearrange("p (g v) u -> p g u v", v=2)
+            nc.scalar.copy(tw_cols[:], tw_turned)
+            nc.scalar.activation(neg_tw_cols[:], tw_turned, ACT.Copy, scale=-1.0)
+            nc.scalar.copy(sw_cols[:], banks[W_BANK][:, :, 2:4].rearrange("p (g v) u -> p g u v", v=2))
 
         def in_runs(ap):
             return ap.rearrange("p (b u r) -> p b u r", u=2, r=RUN)
@@ -111,189 +127,230 @@ def tile_attend_gmw_tnh_kernel(tc, xT, dyT, hE, sw, tw, offs, offs2, out):
         def edges(index_list, g):
             return index_list[:, g * LIST_COLS:(g + 1) * LIST_COLS]
 
-        def turn_values(bank, src, g, passes):
+        def place(src, t):
+            u, v = divmod(t, 2)
+            return src[:, u * 2 * P + v:(u + 1) * 2 * P:2]
+
+        def turn_values(src, bank):
             for t in range(PACK):
-                u, v = divmod(t, 2)
-                first = (u * passes + g) * 2 * P
-                nc.tensor.transpose(bank[:, t, :], src[:, first + v:first + 2 * P:2], ident[:])
+                nc.tensor.transpose(banks[bank][:, t, :], place(src, t), ident[:])
 
-        def turn_words(bank, words, passes):
-            for run in range(2 * passes):
-                nc.tensor.transpose(bank[:, run, :], words[:, run * P:(run + 1) * P], ident[:])
+        x_picked = grid("x_picked", K_PASS, F32)
+        x_pairs = grid("x_pairs", K_PASS, BF16)
+        x_bf = [room("x_bf%d" % m, 2 * E, BF16, ROOMS.get(("x_bf", m))) for m in range(PAIRS)]
+        dy_picked = grid("dy_picked", K_PASS, F32)
+        squares = grid("sq", K_PASS, F32)
+        factors = grid("factor", 2 * K_PASS, F32, PAIRS)
+        groups = (((0, 0), (1, 0), (0, 1), (1, 1)), ((2, 0), (3, 0)), ((2, 1),), ((3, 1),))
+        home = {chunk: (n, at) for n, group in enumerate(groups) for at, chunk in enumerate(group)}
+        dz_bf = [room("dz_bf%d" % n, len(group) * K_PASS + (E if n == 0 else 0), BF16, ROOMS.get(("dz_bf", n))) for n, group in enumerate(groups)]
+        x_codes = [room("x_codes%d" % m, 2 * PASSES * P, U32, ROOMS.get(("x_codes", m))) for m in range(PAIRS)]
+        x_scales = [room("x_scales%d" % m, 2 * PASSES * P, U8) for m in range(PAIRS)]
+        dz_codes = [room("dz_codes%d" % n, len(group) * P, U32, ROOMS.get(("dz_codes", n))) for n, group in enumerate(groups)]
+        dz_scales = [room("dz_scales%d" % n, len(group) * P, U8) for n, group in enumerate(groups)]
+        staged = [room("staged%d" % n, K_PASS, F32, ROOMS.get(("staged", n))) for n in range(TILES)]
+        x_pairs[3] = [dz_bf[0][:, g * K_PASS:(g + 1) * K_PASS] for g in range(PASSES)]
+        x_bf[1] = dz_bf[0][:, E:3 * E]
+        dy_picked[1][1] = x_bf[0][:, E:2 * E].bitcast(F32)
+        dy_picked[3] = [x_bf[0][:, g * E:(g + 1) * E].bitcast(F32) for g in range(PASSES)]
+        squares[2][1] = x_picked[3][1]
+        staged[0] = x_bf[1][:, 0:E].bitcast(F32)
 
-        def weave_words(move, words, bank, passes):
+        def x_part(j, first, count):
+            start = ((j % 2) * PASSES + first) * K_PASS
+            return x_bf[j // 2][:, start:start + count * K_PASS]
+
+        def gather_x(j, g):
+            nc.scalar.activation(x_picked[j][g][:], x_tiles[j][:].indirect(edges(src_list, g)), ACT.Copy)
+
+        def pair_x(j, g, engine=nc.gpsimd):
+            engine.tensor_tensor(dealt(x_pairs[j][g][:]), in_runs(x_picked[j][g][:]), in_runs(sw_rows[g][:]), MULT)
+
+        def turn_pairs(j, g, bank):
+            words = x_pairs[j][g][:].bitcast(F32)
+            for u in range(2):
+                nc.tensor.transpose(banks[bank][:, 2 * g + u, :], words[:, u * P:(u + 1) * P], ident[:])
+
+        def weave_x(move, j, first, count, bank):
             move(
-                words.rearrange("p (g d u) -> p g d u", g=passes, u=2),
-                bank[:, 0:2 * passes, :].rearrange("p (u g) d -> p g d u", u=2),
+                x_part(j, first, count).bitcast(F32).rearrange("p (g d u) -> p g d u", g=count, u=2),
+                banks[bank][:, 2 * first:2 * (first + count), :].rearrange("p (g u) d -> p g d u", u=2),
             )
 
-        x_pairs = []
-        for j in range(GPSIMD_X_TILES):
-            x_picked = keep.tile([P, E], F32, name="x_picked%d" % j)
-            nc.vector.tensor_copy(x_picked[:].bitcast(U32), x_tiles[j][:].bitcast(U32).indirect(src_list[:]))
-            pairs = keep.tile([P, E], BF16, name="x_pairs%d" % j)
-            nc.gpsimd.tensor_tensor(dealt(pairs[:]), in_runs(x_picked[:]), in_runs(sw_rows[:]), MULT)
-            x_pairs.append(pairs)
-
-        dz_bf = [keep.tile([P, DV, PACK], BF16, name="dz_bf%d" % g, align_bytes=64) for g in range(PASSES)]
-        squares = [keep.tile([P, K_PASS], F32, name="h_sq%d" % c) for c in range(CHUNKS)]
-        factor_room = keep.tile([P, CHUNKS * K_PASS], F32, name="factor_room", align_bytes=64)
-        factors = [factor_room[:, c * K_PASS:(c + 1) * K_PASS] for c in range(CHUNKS)]
-        turned = [keep.tile([P, K_PASS], F32, name="dy_turned%d" % c) for c in range(GPSIMD_CHUNKS)]
-
-        def square(c):
-            nc.scalar.activation(dealt(squares[c][:]), in_runs(h_tiles[c][:]), ACT.Square)
-
-        def make_factor(c):
-            g = c % PASSES
-            bank = banks[H_BANKS[c]]
-            turn_values(bank, squares[c], 0, 1)
-            for t in range(PACK):
-                u, v = divmod(t, 2)
-                nc.scalar.activation(
-                    factors[c][:, t * P:(t + 1) * P], bank[:, t, :], ACT.Identity,
-                    bias=tw_cols[:, 2 * g + v, u:u + 1], scale=neg_tw_cols[:, 2 * g + v, u:u + 1],
-                )
-
-        def dz_part(c):
-            j, g = divmod(c, PASSES)
-            return dz_bf[g][:, j * P:(j + 1) * P, :]
-
-        def dz_on_gpsimd(c):
-            j, g = divmod(c, PASSES)
-            picked = keep.tile([P, K_PASS], F32, name="dy_picked%d" % c)
+        def gather_x_dealt(j, g):
             nc.vector.tensor_copy(
-                dealt(picked[:].bitcast(U32)), dy_tiles[j][:].bitcast(U32).indirect(edges(dst_list, g)),
+                dealt(x_picked[j][g][:].bitcast(U32)), x_tiles[j][:].bitcast(U32).indirect(edges(src_list, g)),
             )
-            bank = banks[DY_BANKS[c]]
-            turn_values(bank, picked, 0, 1)
-            dy_turned = turned[c][:].rearrange("p (n t) -> p n t", t=PACK)
-            nc.scalar.copy(dy_turned, bank[:].rearrange("p t n -> p n t"))
-            nc.gpsimd.tensor_tensor(dz_part(c), dy_turned, factors[c].rearrange("p (t n) -> p n t", t=PACK), MULT)
 
-        def dz_on_vector(c, picked):
-            bank = banks[DY_BANKS[c]]
-            turn_values(bank, picked, c % PASSES, PASSES)
+        def scale_x(j, g, bank):
             nc.vector.tensor_tensor(
-                dz_part(c).rearrange("p (c i) t -> p c t i", i=4),
-                bank[:].rearrange("p t (c i) -> p c t i", i=4),
-                factors[c].rearrange("p (t c i) -> p c t i", t=PACK, i=4),
+                x_part(j, g, 1).rearrange("p (d t) -> p d t", t=PACK),
+                banks[bank][:].rearrange("p t d -> p d t"),
+                sw_cols[:, g].rearrange("p u v -> p (u v)").unsqueeze(1).to_broadcast([P, P, PACK]),
                 MULT,
             )
 
-        square(0)
-        make_factor(0)
-        square(1)
-        make_factor(1)
-        square(2)
-        square(3)
-        dz_on_gpsimd(0)
-        dz_on_gpsimd(1)
-        make_factor(2)
-        square(4)
-        dz_on_gpsimd(2)
-        make_factor(3)
-        dz_on_gpsimd(3)
-        make_factor(4)
-        for c in range(GPSIMD_CHUNKS + 1, CHUNKS):
-            square(c)
-        dy_picked = []
-        for j in range(whole_dy, N_TILES):
-            picked = keep.tile([P, E], F32, name="dy_both%d" % j)
-            nc.vector.tensor_copy(dealt(picked[:].bitcast(U32)), dy_tiles[j][:].bitcast(U32).indirect(dst_list[:]))
-            dy_picked.extend([picked] * PASSES)
-        for c in range(GPSIMD_CHUNKS + 1, CHUNKS):
-            make_factor(c)
-        for c in range(GPSIMD_CHUNKS, CHUNKS):
-            dz_on_vector(c, dy_picked[c - GPSIMD_CHUNKS])
-
-        width = PASSES * P
-        dz_codes = [keep.tile([P, DV], U32, name="dz_codes%d" % g, align_bytes=64) for g in range(PASSES)]
-        dz_scales = [keep.tile([P, DV], U8, name="dz_scales%d" % g, align_bytes=64) for g in range(PASSES)]
-        x_codes = keep.tile([P, D_TILES * width], U32, name="x_codes", align_bytes=64)
-        x_scales = keep.tile([P, D_TILES * width], U8, name="x_scales", align_bytes=64)
-
-        def quantize_dz(g):
-            nc.vector.quantize_mx(
-                out=dz_codes[g][:].bitcast(E5M2), scales=dz_scales[g][:],
-                in_=dz_bf[g][:].rearrange("p n t -> p (n t)"),
+        def gather_dy(k, g):
+            nc.vector.tensor_copy(
+                dealt(dy_picked[k][g][:].bitcast(U32)), dy_tiles[k][:].bitcast(U32).indirect(edges(dst_list, g)),
             )
 
-        def quantize_x(first, words):
-            cols = slice(first * P, first * P + words.shape[1] // 2)
-            nc.vector.quantize_mx(out=x_codes[:, cols].bitcast(E4M3), scales=x_scales[:, cols], in_=words.bitcast(BF16))
+        def square(k, g):
+            nc.scalar.activation(dealt(squares[k][g][:]), in_runs(h_parts[k][g][:]), ACT.Square)
 
-        def multiply(j, g):
-            cols = slice((PASSES * j + g) * P, (PASSES * j + g + 1) * P)
+        def square_on_gpsimd(k, g):
+            h = in_runs(h_parts[k][g][:])
+            nc.gpsimd.tensor_tensor(dealt(squares[k][g][:]), h, h, MULT)
+
+        def turn_squares(k, g, two_banks):
+            for t in range(PACK):
+                nc.tensor.transpose(banks[two_banks[t // 2]][:, 2 * (t % 2) + k % 2, :], place(squares[k][g], t), ident[:])
+
+        def make_factors(m, g, u, two_banks):
+            for v in range(2):
+                t = 2 * u + v
+                nc.scalar.activation(
+                    factors[m][g][:, t * 2 * P:(t + 1) * 2 * P],
+                    banks[two_banks[u]][:, 2 * v:2 * v + 2, :].rearrange("p k n -> p (k n)"), ACT.Identity,
+                    bias=tw_cols[:, g, u, v:v + 1], scale=neg_tw_cols[:, g, u, v:v + 1],
+                )
+
+        def make_dz(k, g, bank):
+            group, at = home[k, g]
+            start = at * K_PASS
+            nc.vector.tensor_tensor(
+                dz_bf[group][:, start:start + K_PASS].rearrange("p (c i t) -> p c t i", i=4, t=PACK),
+                banks[bank][:].rearrange("p t (c i) -> p c t i", i=4),
+                factors[k // 2][g][:].rearrange("p (t k c i) -> p k c t i", t=PACK, k=2, i=4)[:, k % 2],
+                MULT,
+            )
+
+        def quantize_x(m):
+            nc.vector.quantize_mx(out=x_codes[m][:].bitcast(E4M3), scales=x_scales[m][:], in_=x_bf[m][:])
+
+        def quantize_dz(group):
+            nc.vector.quantize_mx(out=dz_codes[group][:].bitcast(E5M2), scales=dz_scales[group][:], in_=dz_bf[group][:, 0:len(groups[group]) * K_PASS])
+
+        def multiply(j, g, k, width, acc, start, stop):
+            cols = slice((PASSES * (j % 2) + g) * P, (PASSES * (j % 2) + g + 1) * P)
+            group, at = home[k, g]
+            moving = slice(at * P, at * P + width)
             nc.tensor.matmul_mx(
-                out=banks[ACC_BANKS[j]][:].rearrange("p t n -> p (t n)"),
-                lhsT=x_codes[:, cols].bitcast(E4M3), lhsT_scale=x_scales[:, cols],
-                rhs=dz_codes[g][:].bitcast(E5M2), rhs_scale=dz_scales[g][:],
-                start=(g == 0), stop=(g == PASSES - 1),
+                out=acc, lhsT=x_codes[j // 2][:, cols].bitcast(E4M3), lhsT_scale=x_scales[j // 2][:, cols],
+                rhs=dz_codes[group][:, moving].bitcast(E5M2), rhs_scale=dz_scales[group][:, moving],
+                start=start, stop=stop,
             )
 
-        spare = keep.tile([P, 2 * DV], F32, name="spare")
-        staged = [squares[0][:], spare[:, 0:DV], spare[:, DV:2 * DV], squares[1][:]]
+        def multiply_left(m, bank):
+            for s in range(2):
+                for g in range(PASSES):
+                    acc = banks[bank][:, 2 * s:2 * s + 2, :].rearrange("p k n -> p (k n)")
+                    multiply(2 * m + s, g, 0, 2 * P, acc, g == 0, g == PASSES - 1)
 
-        def store(j):
-            acc = banks[ACC_BANKS[j]][:].rearrange("p t n -> p (t n)")
-            pieces = 2 if j == last else 1
-            piece_cols = DV // pieces
-            for piece in range(pieces):
-                cols = slice(piece * piece_cols, (piece + 1) * piece_cols)
-                nc.scalar.copy(staged[j][:, cols], acc[:, cols])
-                nc.sync.dma_start(out[j * P:(j + 1) * P, cols], staged[j][:, cols])
+        def multiply_column(k, g, bank, tiles=range(TILES)):
+            for j in tiles:
+                multiply(j, g, k, P, banks[bank][:, j, :], (g, j) == (0, 0), (g, j) == (PASSES - 1, TILES - 1))
 
-        early_words = factor_room[:, (CHUNKS - 3) * K_PASS:(CHUNKS - 1) * K_PASS]
-        for j in range(GPSIMD_X_TILES):
-            turn_words(banks[X_BANKS[j]], x_pairs[j][:].bitcast(F32), PASSES)
-            weave_words(nc.scalar.copy, early_words[:, j * K_PASS:(j + 1) * K_PASS], banks[X_BANKS[j]], PASSES)
+        def store(move, first_tile, tiles, first_col, width, bank, part):
+            move(part, banks[bank][:].rearrange("p t n -> p (t n)"))
+            nc.sync.dma_start(
+                out[first_tile * P:(first_tile + tiles) * P, first_col:first_col + width].rearrange("(j p) n -> p j n", p=P),
+                part.rearrange("p (j n) -> p j n", n=width),
+            )
+
+        square(0, 0)
+        turn_squares(0, 0, (0, 1))
+        turn_weights()
+        gather_x_dealt(0, 0)
+        gather_x(0, 1)
+        copy_weights()
+        turn_values(x_picked[0][0], 7)
+        gather_dy(0, 0)
+        square(1, 0)
+        turn_squares(1, 0, (0, 1))
+        gather_dy(0, 1)
+        pair_x(0, 1)
+        make_factors(0, 0, 0, (0, 1))
+        scale_x(0, 0, 7)
+        make_factors(0, 0, 1, (0, 1))
+        square_on_gpsimd(0, 1)
+        turn_pairs(0, 1, 6)
+        turn_values(dy_picked[0][0], 1)
+        gather_x(1, 1)
+        weave_x(nc.vector.tensor_copy, 0, 1, 1, 6)
+        turn_squares(0, 1, (2, 3))
+        gather_dy(1, 0)
+        gather_x(1, 0)
+        pair_x(1, 1)
+        turn_values(dy_picked[1][0], 0)
+        gather_dy(1, 1)
+        square_on_gpsimd(1, 1)
+        turn_pairs(1, 1, 6)
+        gather_x(2, 1)
+        make_dz(0, 0, 1)
+        make_dz(1, 0, 0)
+        turn_squares(1, 1, (2, 3))
+        pair_x(1, 0)
+        gather_dy(2, 0)
+        gather_x(2, 0)
+        pair_x(2, 1)
+        turn_pairs(1, 0, 6)
+        gather_dy(2, 1)
+        make_factors(0, 1, 0, (2, 3))
+        turn_values(dy_picked[0][1], 2)
+        make_factors(0, 1, 1, (2, 3))
+        turn_values(dy_picked[1][1], 3)
+        square(2, 0)
+        turn_squares(2, 0, (4, 5))
+        pair_x(2, 0)
+        square(3, 0)
+        make_dz(0, 1, 2)
+        weave_x(nc.vector.tensor_copy, 1, 0, 2, 6)
+        turn_pairs(2, 1, 2)
+        turn_squares(3, 0, (4, 5))
+        make_dz(1, 1, 3)
+        turn_pairs(2, 0, 2)
+        turn_values(dy_picked[2][1], 6)
+        gather_x(3, 1)
+        gather_x(3, 0)
+        quantize_x(0)
         quantize_dz(0)
-        quantize_x(0, early_words[:, 0:K_PASS])
+        pair_x(3, 1)
+        weave_x(nc.scalar.copy, 2, 0, 2, 2)
+        gather_dy(3, 0)
+        gather_dy(3, 1)
+        multiply_left(0, 3)
+        make_factors(1, 0, 0, (4, 5))
+        turn_values(dy_picked[2][0], 4)
+        pair_x(3, 0)
+        make_factors(1, 0, 1, (4, 5))
+        turn_values(dy_picked[3][0], 5)
+        square(2, 1)
+        square(3, 1)
+        make_dz(2, 0, 4)
+        turn_squares(2, 1, (0, 1))
+        turn_pairs(3, 1, 4)
+        turn_pairs(3, 0, 4)
+        make_dz(3, 0, 5)
+        turn_squares(3, 1, (0, 1))
         quantize_dz(1)
-        quantize_x(PASSES, early_words[:, K_PASS:2 * K_PASS])
-        for j in range(GPSIMD_X_TILES):
-            for g in range(PASSES):
-                multiply(j, g)
-        store(0)
-
-        j = GPSIMD_X_TILES
-        xe = factor_room[:, (GPSIMD_CHUNKS - 2) * K_PASS:GPSIMD_CHUNKS * K_PASS]
-        nc.vector.tensor_tensor(xe, x_tiles[j][:].indirect(src_list[:]), sw_rows[:], MULT)
-        nc.scalar.copy(dealt(turned[0][:].bitcast(BF16)), in_runs(xe))
-        turn_words(banks[X_BANKS[j]], turned[0], PASSES)
-        weave_words(nc.scalar.copy, factors[0], banks[X_BANKS[j]], PASSES)
-
-        dz_room = [dz_bf[g][:].rearrange("p n t -> p (n t)").bitcast(F32) for g in range(PASSES)]
-        pair_room = [spare[:, DV - 3 * P // 2:DV + P // 2], dz_room[0][:, 0:K_PASS // 2]]
-        last_words = keep.tile([P, K_PASS // 2], F32, name="last_words", align_bytes=64)
-        for g in range(PASSES):
-            final = g == PASSES - 1
-            move = nc.vector.tensor_copy if final else nc.scalar.copy
-            pairs = pair_room[g].bitcast(BF16).rearrange("p (u b r) -> p u b r", u=2, r=RUN)
-            cuts = (0, K_PASS - LAST_EDGES, K_PASS) if final else (0, K_PASS)
-            for first, end in zip(cuts, cuts[1:]):
-                cols = slice(first, end)
-                xe = dz_room[g][:, cols]
-                nc.vector.tensor_tensor(
-                    xe,
-                    x_tiles[last][:].indirect(edges(src_list, g)[:, cols.start // 16:cols.stop // 16]),
-                    sw_rows[:, g * K_PASS:(g + 1) * K_PASS][:, cols], MULT,
-                )
-                (move if end == K_PASS else nc.scalar.copy)(
-                    pairs[:, :, cols.start // (2 * RUN):cols.stop // (2 * RUN), :],
-                    xe.rearrange("p (b u r) -> p u b r", u=2, r=RUN),
-                )
-            if not final:
-                quantize_x(PASSES * j, factors[0])
-                multiply(j, 0)
-                multiply(j, 1)
-            bank = banks[X_BANKS[last + g]]
-            turn_words(bank, pair_room[g], 1)
-            weave_words(move, last_words[:], bank, 1)
-            if not final:
-                store(1)
-                store(2)
-            quantize_x(PASSES * last + g, last_words[:])
-            multiply(last, g)
-        store(last)
+        weave_x(nc.scalar.copy, 3, 0, 2, 4)
+        turn_values(dy_picked[3][1], 4)
+        multiply_column(2, 0, 7, (0, 1))
+        multiply_column(3, 0, 5, (0, 1))
+        make_factors(1, 1, 0, (0, 1))
+        quantize_x(1)
+        make_factors(1, 1, 1, (0, 1))
+        store(nc.vector.tensor_copy, 0, 2, 0, 2 * P, 3, staged[0][:])
+        multiply_left(1, 2)
+        multiply_column(2, 0, 7, (2, 3))
+        multiply_column(3, 0, 5, (2, 3))
+        make_dz(2, 1, 6)
+        make_dz(3, 1, 4)
+        quantize_dz(2)
+        quantize_dz(3)
+        store(nc.scalar.copy, 2, 2, 0, 2 * P, 2, staged[1][:])
+        multiply_column(2, 1, 7)
+        multiply_column(3, 1, 5)
+        store(nc.scalar.copy, 0, TILES, 2 * P, P, 7, staged[2][:])
+        store(nc.vector.tensor_copy, 0, TILES, 3 * P, P, 5, staged[3][:])

@@ -24,11 +24,8 @@ RUN = 16
 LIST_COLS = K_PASS // 16
 TILES = D // P
 PAIRS = TILES // 2
-W_BANK = 7
-ROOMS = {
-    ("x_bf", 0): "dy0", ("dz_bf", 0): "dy1", ("factor", 0, 1): "x2", ("factor", 1, 0): "x3",
-    ("x_pairs", 1, 1): "h0_1",
-}
+W_BANK = 6
+ROOMS = {("x_picked", 0, 1): "h_pair0", "x_bf": "x2", ("dz_bf", 0): "dy0", ("dz_codes", 0): "dy3"}
 
 
 def tile_attend_gmw_tnh_kernel(tc, xT, dyT, hE, sw, tw, offs, offs2, out):
@@ -48,11 +45,16 @@ def tile_attend_gmw_tnh_kernel(tc, xT, dyT, hE, sw, tw, offs, offs2, out):
         x_tiles = [room("x%d" % j, V, F32) for j in range(TILES)]
         dy_tiles = [room("dy%d" % k, V, F32) for k in range(TILES)]
         h_parts = grid("h", K_PASS, F32)
+        h_pairs = [room("h_pair%d" % g, E, F32) for g in range(PASSES)]
+        x_bf = room("x_bf", TILES * E, BF16, ROOMS["x_bf"])
+        for k in range(2):
+            for g in range(PASSES):
+                h_parts[k][g] = h_pairs[g][:, k * K_PASS:(k + 1) * K_PASS]
+        h_parts[2][0] = x_bf[:, E:2 * E].bitcast(F32)
         sw_rows = [room("sw_rows%d" % g, K_PASS, F32) for g in range(PASSES)]
         w_rows = room("w_rows", K_PASS, F32)
         tw_cols = keep.tile([P, PASSES, 2, 2], F32, name="tw_cols")
         neg_tw_cols = keep.tile([P, PASSES, 2, 2], F32, name="neg_tw_cols")
-        sw_cols = keep.tile([P, PASSES, 2, 2], F32, name="sw_cols")
         ident = keep.tile([P, P], F32, name="ident")
         banks = [psum.tile([P, PACK, P], F32, name="bank%d" % b) for b in range(8)]
 
@@ -73,6 +75,11 @@ def tile_attend_gmw_tnh_kernel(tc, xT, dyT, hE, sw, tw, offs, offs2, out):
         def load_h(k, g):
             nc.sync.dma_start(h_parts[k][g][:], hE[rows(k), edge_cols(g)])
 
+        def load_h_pair(g):
+            nc.sync.dma_start(
+                h_pairs[g][:].rearrange("p (k e) -> p k e", k=2), hE[0:2 * P, edge_cols(g)].rearrange("(k p) e -> p k e", p=P),
+            )
+
         def load_sw(g):
             nc.sync.dma_start(sw_rows[g][:], sw[:, edge_cols(g)])
 
@@ -82,26 +89,23 @@ def tile_attend_gmw_tnh_kernel(tc, xT, dyT, hE, sw, tw, offs, offs2, out):
                 weights[0, :].rearrange("(b u r) -> u b r", u=2, r=RUN),
             )
 
-        load_h(0, 0)
-        load_x(0)
-        nc.sync.dma_start(src_list[:], offs)
+        load_h_pair(0)
         load_row(0, tw)
-        load_row(2, sw)
+        nc.sync.dma_start(src_list[:], offs)
+        load_x(0)
         load_dy(0)
         nc.sync.dma_start(dst_list[:], offs2)
-        load_h(1, 0)
-        load_sw(1)
         load_x(1)
+        load_sw(1)
         load_dy(1)
-        load_h(0, 1)
-        load_h(1, 1)
-        load_sw(0)
         load_x(2)
+        load_sw(0)
         load_dy(2)
-        load_h(2, 0)
-        load_h(3, 0)
+        load_h_pair(1)
         load_x(3)
         load_dy(3)
+        load_h(2, 0)
+        load_h(3, 0)
         load_h(2, 1)
         load_h(3, 1)
 
@@ -114,9 +118,8 @@ def tile_attend_gmw_tnh_kernel(tc, xT, dyT, hE, sw, tw, offs, offs2, out):
 
         def copy_weights():
             tw_turned = banks[W_BANK][:, :, 0:2].rearrange("p (g v) u -> p g u v", v=2)
-            nc.scalar.copy(tw_cols[:], tw_turned)
-            nc.scalar.activation(neg_tw_cols[:], tw_turned, ACT.Copy, scale=-1.0)
-            nc.scalar.copy(sw_cols[:], banks[W_BANK][:, :, 2:4].rearrange("p (g v) u -> p g u v", v=2))
+            nc.vector.tensor_copy(tw_cols[:], tw_turned)
+            nc.vector.tensor_scalar_mul(neg_tw_cols[:], tw_turned, -1.0)
 
         def in_runs(ap):
             return ap.rearrange("p (b u r) -> p b u r", u=2, r=RUN)
@@ -137,28 +140,19 @@ def tile_attend_gmw_tnh_kernel(tc, xT, dyT, hE, sw, tw, offs, offs2, out):
 
         x_picked = grid("x_picked", K_PASS, F32)
         x_pairs = grid("x_pairs", K_PASS, BF16)
-        x_bf = [room("x_bf%d" % m, 2 * E, BF16, ROOMS.get(("x_bf", m))) for m in range(PAIRS)]
         dy_picked = grid("dy_picked", K_PASS, F32)
         squares = grid("sq", K_PASS, F32)
         factors = grid("factor", 2 * K_PASS, F32, PAIRS)
         groups = (((0, 0), (1, 0), (0, 1), (1, 1)), ((2, 0), (3, 0)), ((2, 1),), ((3, 1),))
         home = {chunk: (n, at) for n, group in enumerate(groups) for at, chunk in enumerate(group)}
-        dz_bf = [room("dz_bf%d" % n, len(group) * K_PASS + (E if n == 0 else 0), BF16, ROOMS.get(("dz_bf", n))) for n, group in enumerate(groups)]
-        x_codes = [room("x_codes%d" % m, 2 * PASSES * P, U32, ROOMS.get(("x_codes", m))) for m in range(PAIRS)]
-        x_scales = [room("x_scales%d" % m, 2 * PASSES * P, U8) for m in range(PAIRS)]
+        dz_bf = [room("dz_bf%d" % n, len(group) * K_PASS, BF16, ROOMS.get(("dz_bf", n))) for n, group in enumerate(groups)]
+        x_codes = room("x_codes", TILES * PASSES * P, U32, ROOMS.get("x_codes"))
+        x_scales = room("x_scales", TILES * PASSES * P, U8)
         dz_codes = [room("dz_codes%d" % n, len(group) * P, U32, ROOMS.get(("dz_codes", n))) for n, group in enumerate(groups)]
         dz_scales = [room("dz_scales%d" % n, len(group) * P, U8) for n, group in enumerate(groups)]
         staged = [room("staged%d" % n, K_PASS, F32, ROOMS.get(("staged", n))) for n in range(TILES)]
-        x_pairs[3] = [dz_bf[0][:, g * K_PASS:(g + 1) * K_PASS] for g in range(PASSES)]
-        x_bf[1] = dz_bf[0][:, E:3 * E]
-        dy_picked[1][1] = x_bf[0][:, E:2 * E].bitcast(F32)
-        dy_picked[3] = [x_bf[0][:, g * E:(g + 1) * E].bitcast(F32) for g in range(PASSES)]
-        squares[2][1] = x_picked[3][1]
-        staged[0] = x_bf[1][:, 0:E].bitcast(F32)
-
-        def x_part(j, first, count):
-            start = ((j % 2) * PASSES + first) * K_PASS
-            return x_bf[j // 2][:, start:start + count * K_PASS]
+        x_pairs[3] = [factors[1][0][:, g * 2 * P:(g + 1) * 2 * P].bitcast(BF16) for g in range(PASSES)]
+        squares[1][1] = x_bf[:, 0:E].bitcast(F32)
 
         def gather_x(j, g):
             nc.scalar.activation(x_picked[j][g][:], x_tiles[j][:].indirect(edges(src_list, g)), ACT.Copy)
@@ -166,29 +160,18 @@ def tile_attend_gmw_tnh_kernel(tc, xT, dyT, hE, sw, tw, offs, offs2, out):
         def pair_x(j, g, engine=nc.gpsimd):
             engine.tensor_tensor(dealt(x_pairs[j][g][:]), in_runs(x_picked[j][g][:]), in_runs(sw_rows[g][:]), MULT)
 
-        def turn_pairs(j, g, bank):
+        def turn_pairs(j, g, bank, slot):
             words = x_pairs[j][g][:].bitcast(F32)
             for u in range(2):
-                nc.tensor.transpose(banks[bank][:, 2 * g + u, :], words[:, u * P:(u + 1) * P], ident[:])
+                nc.tensor.transpose(banks[bank][:, 2 * slot + u, :], words[:, u * P:(u + 1) * P], ident[:])
 
-        def weave_x(move, j, first, count, bank):
-            move(
-                x_part(j, first, count).bitcast(F32).rearrange("p (g d u) -> p g d u", g=count, u=2),
-                banks[bank][:, 2 * first:2 * (first + count), :].rearrange("p (g u) d -> p g d u", u=2),
-            )
+        def weave_x(chunks, bank):
+            words = x_bf[:].bitcast(F32).rearrange("p (c d u) -> p c d u", d=P, u=2)
+            first, second = [TILES * g + j for j, g in chunks]
+            nc.scalar.copy(words[:, first:second + 1:second - first], banks[bank][:].rearrange("p (c u) d -> p c d u", u=2))
 
-        def gather_x_dealt(j, g):
-            nc.vector.tensor_copy(
-                dealt(x_picked[j][g][:].bitcast(U32)), x_tiles[j][:].bitcast(U32).indirect(edges(src_list, g)),
-            )
-
-        def scale_x(j, g, bank):
-            nc.vector.tensor_tensor(
-                x_part(j, g, 1).rearrange("p (d t) -> p d t", t=PACK),
-                banks[bank][:].rearrange("p t d -> p d t"),
-                sw_cols[:, g].rearrange("p u v -> p (u v)").unsqueeze(1).to_broadcast([P, P, PACK]),
-                MULT,
-            )
+        def gather_x_plain(j, g):
+            nc.vector.tensor_copy(x_picked[j][g][:].bitcast(U32), x_tiles[j][:].bitcast(U32).indirect(edges(src_list, g)))
 
         def gather_dy(k, g):
             nc.vector.tensor_copy(
@@ -225,18 +208,18 @@ def tile_attend_gmw_tnh_kernel(tc, xT, dyT, hE, sw, tw, offs, offs2, out):
                 MULT,
             )
 
-        def quantize_x(m):
-            nc.vector.quantize_mx(out=x_codes[m][:].bitcast(E4M3), scales=x_scales[m][:], in_=x_bf[m][:])
+        def quantize_x():
+            nc.vector.quantize_mx(out=x_codes[:].bitcast(E4M3), scales=x_scales[:], in_=x_bf[:])
 
         def quantize_dz(group):
             nc.vector.quantize_mx(out=dz_codes[group][:].bitcast(E5M2), scales=dz_scales[group][:], in_=dz_bf[group][:, 0:len(groups[group]) * K_PASS])
 
         def multiply(j, g, k, width, acc, start, stop):
-            cols = slice((PASSES * (j % 2) + g) * P, (PASSES * (j % 2) + g + 1) * P)
+            cols = slice((TILES * g + j) * P, (TILES * g + j + 1) * P)
             group, at = home[k, g]
             moving = slice(at * P, at * P + width)
             nc.tensor.matmul_mx(
-                out=acc, lhsT=x_codes[j // 2][:, cols].bitcast(E4M3), lhsT_scale=x_scales[j // 2][:, cols],
+                out=acc, lhsT=x_codes[:, cols].bitcast(E4M3), lhsT_scale=x_scales[:, cols],
                 rhs=dz_codes[group][:, moving].bitcast(E5M2), rhs_scale=dz_scales[group][:, moving],
                 start=start, stop=stop,
             )
@@ -247,110 +230,110 @@ def tile_attend_gmw_tnh_kernel(tc, xT, dyT, hE, sw, tw, offs, offs2, out):
                     acc = banks[bank][:, 2 * s:2 * s + 2, :].rearrange("p k n -> p (k n)")
                     multiply(2 * m + s, g, 0, 2 * P, acc, g == 0, g == PASSES - 1)
 
-        def multiply_column(k, g, bank, tiles=range(TILES)):
-            for j in tiles:
-                multiply(j, g, k, P, banks[bank][:, j, :], (g, j) == (0, 0), (g, j) == (PASSES - 1, TILES - 1))
+        def multiply_column(k, g, bank, tiles):
+            for s, j in enumerate(tiles):
+                multiply(j, g, k, P, banks[bank][:, s, :], (g, s) == (0, 0), (g, s) == (PASSES - 1, len(tiles) - 1))
 
         def store(move, first_tile, tiles, first_col, width, bank, part):
-            move(part, banks[bank][:].rearrange("p t n -> p (t n)"))
+            move(part, banks[bank][:].rearrange("p t n -> p (t n)")[:, 0:tiles * width])
             nc.sync.dma_start(
                 out[first_tile * P:(first_tile + tiles) * P, first_col:first_col + width].rearrange("(j p) n -> p j n", p=P),
                 part.rearrange("p (j n) -> p j n", n=width),
             )
 
-        square(0, 0)
-        turn_squares(0, 0, (0, 1))
         turn_weights()
-        gather_x_dealt(0, 0)
-        gather_x(0, 1)
         copy_weights()
-        turn_values(x_picked[0][0], 7)
-        gather_dy(0, 0)
+        square(0, 0)
         square(1, 0)
+        turn_squares(0, 0, (0, 1))
         turn_squares(1, 0, (0, 1))
-        gather_dy(0, 1)
-        pair_x(0, 1)
+        gather_x_plain(0, 0)
+        gather_x(0, 1)
+        gather_dy(0, 0)
         make_factors(0, 0, 0, (0, 1))
-        scale_x(0, 0, 7)
         make_factors(0, 0, 1, (0, 1))
-        square_on_gpsimd(0, 1)
-        turn_pairs(0, 1, 6)
-        turn_values(dy_picked[0][0], 1)
+        turn_values(dy_picked[0][0], 0)
+        gather_dy(0, 1)
         gather_x(1, 1)
-        weave_x(nc.vector.tensor_copy, 0, 1, 1, 6)
-        turn_squares(0, 1, (2, 3))
-        gather_dy(1, 0)
+        pair_x(0, 1)
+        make_dz(0, 0, 0)
         gather_x(1, 0)
         pair_x(1, 1)
-        turn_values(dy_picked[1][0], 0)
+        gather_dy(1, 0)
+        turn_values(dy_picked[0][1], 0)
+        turn_pairs(0, 1, 1, 0)
+        gather_x(2, 0)
+        turn_values(dy_picked[1][0], 6)
         gather_dy(1, 1)
-        square_on_gpsimd(1, 1)
-        turn_pairs(1, 1, 6)
+        turn_pairs(1, 1, 1, 1)
+        pair_x(0, 0)
         gather_x(2, 1)
-        make_dz(0, 0, 1)
-        make_dz(1, 0, 0)
-        turn_squares(1, 1, (2, 3))
+        make_dz(1, 0, 6)
+        turn_values(dy_picked[1][1], 6)
         pair_x(1, 0)
         gather_dy(2, 0)
-        gather_x(2, 0)
-        pair_x(2, 1)
-        turn_pairs(1, 0, 6)
+        weave_x(((0, 1), (1, 1)), 1)
+        square(0, 1)
+        turn_pairs(0, 0, 1, 0)
+        turn_pairs(1, 0, 1, 1)
         gather_dy(2, 1)
-        make_factors(0, 1, 0, (2, 3))
-        turn_values(dy_picked[0][1], 2)
-        make_factors(0, 1, 1, (2, 3))
-        turn_values(dy_picked[1][1], 3)
-        square(2, 0)
-        turn_squares(2, 0, (4, 5))
         pair_x(2, 0)
-        square(3, 0)
-        make_dz(0, 1, 2)
-        weave_x(nc.vector.tensor_copy, 1, 0, 2, 6)
-        turn_pairs(2, 1, 2)
-        turn_squares(3, 0, (4, 5))
-        make_dz(1, 1, 3)
-        turn_pairs(2, 0, 2)
-        turn_values(dy_picked[2][1], 6)
-        gather_x(3, 1)
+        square(1, 1)
+        turn_squares(0, 1, (2, 3))
         gather_x(3, 0)
-        quantize_x(0)
-        quantize_dz(0)
-        pair_x(3, 1)
-        weave_x(nc.scalar.copy, 2, 0, 2, 2)
+        turn_squares(1, 1, (2, 3))
+        gather_x_plain(3, 1)
+        pair_x(2, 1)
+        weave_x(((0, 0), (1, 0)), 1)
+        make_factors(0, 1, 0, (2, 3))
         gather_dy(3, 0)
+        pair_x(3, 1)
+        turn_values(dy_picked[2][1], 1)
+        turn_values(dy_picked[2][0], 2)
+        make_factors(0, 1, 1, (2, 3))
         gather_dy(3, 1)
-        multiply_left(0, 3)
-        make_factors(1, 0, 0, (4, 5))
-        turn_values(dy_picked[2][0], 4)
+        turn_pairs(2, 0, 3, 0)
+        turn_pairs(2, 1, 3, 1)
+        square(2, 0)
         pair_x(3, 0)
-        make_factors(1, 0, 1, (4, 5))
-        turn_values(dy_picked[3][0], 5)
-        square(2, 1)
+        turn_squares(2, 0, (4, 5))
+        weave_x(((2, 0), (2, 1)), 3)
+        make_dz(0, 1, 0)
+        square(3, 0)
+        make_dz(1, 1, 6)
+        turn_pairs(3, 1, 3, 1)
+        turn_pairs(3, 0, 3, 0)
+        square_on_gpsimd(2, 1)
         square(3, 1)
-        make_dz(2, 0, 4)
-        turn_squares(2, 1, (0, 1))
-        turn_pairs(3, 1, 4)
-        turn_pairs(3, 0, 4)
-        make_dz(3, 0, 5)
-        turn_squares(3, 1, (0, 1))
+        turn_squares(3, 0, (4, 5))
+        weave_x(((3, 0), (3, 1)), 3)
+        quantize_dz(0)
+        turn_squares(3, 1, (0, 6))
+        turn_squares(2, 1, (0, 6))
+        make_factors(1, 0, 0, (4, 5))
+        turn_values(dy_picked[3][0], 4)
+        quantize_x()
+        make_factors(1, 0, 1, (4, 5))
+        turn_values(dy_picked[3][1], 5)
+        make_factors(1, 1, 0, (0, 6))
+        make_dz(2, 0, 2)
+        multiply_left(0, 0)
+        make_factors(1, 1, 1, (0, 6))
+        make_dz(3, 0, 4)
+        multiply_left(1, 6)
+        make_dz(2, 1, 1)
         quantize_dz(1)
-        weave_x(nc.scalar.copy, 3, 0, 2, 4)
-        turn_values(dy_picked[3][1], 4)
-        multiply_column(2, 0, 7, (0, 1))
-        multiply_column(3, 0, 5, (0, 1))
-        make_factors(1, 1, 0, (0, 1))
-        quantize_x(1)
-        make_factors(1, 1, 1, (0, 1))
-        store(nc.vector.tensor_copy, 0, 2, 0, 2 * P, 3, staged[0][:])
-        multiply_left(1, 2)
-        multiply_column(2, 0, 7, (2, 3))
-        multiply_column(3, 0, 5, (2, 3))
-        make_dz(2, 1, 6)
-        make_dz(3, 1, 4)
+        store(nc.scalar.copy, 0, 2, 0, 2 * P, 0, staged[0][:])
+        multiply_column(2, 0, 2, range(TILES))
         quantize_dz(2)
+        make_dz(3, 1, 5)
+        store(nc.scalar.copy, 2, 2, 0, 2 * P, 6, staged[1][:])
+        multiply_column(2, 1, 2, range(TILES))
+        multiply_column(3, 0, 4, (0, 1))
+        multiply_column(3, 0, 7, (2, 3))
         quantize_dz(3)
-        store(nc.scalar.copy, 2, 2, 0, 2 * P, 2, staged[1][:])
-        multiply_column(2, 1, 7)
-        multiply_column(3, 1, 5)
-        store(nc.scalar.copy, 0, TILES, 2 * P, P, 7, staged[2][:])
-        store(nc.vector.tensor_copy, 0, TILES, 3 * P, P, 5, staged[3][:])
+        store(nc.scalar.copy, 0, TILES, 2 * P, P, 2, staged[2][:])
+        multiply_column(3, 1, 4, (0, 1))
+        multiply_column(3, 1, 7, (2, 3))
+        store(nc.vector.tensor_copy, 0, 2, 3 * P, P, 4, staged[3][:, 0:2 * P])
+        store(nc.scalar.copy, 2, 2, 3 * P, P, 7, staged[3][:, 2 * P:4 * P])

@@ -1,7 +1,6 @@
 from contextlib import ExitStack
 
 import concourse.mybir as mybir
-from concourse.masks import make_identity
 
 V, E, D, DV = 1024, 1024, 512, 512
 FLOPS = 2 * E * D * DV
@@ -24,8 +23,10 @@ RUN = 16
 LIST_COLS = K_PASS // 16
 TILES = D // P
 PAIRS = TILES // 2
+QUAD = 32
 W_BANK = 6
-ROOMS = {("x_picked", 0, 1): "h_pair0", "x_bf": "x2", ("dz_bf", 0): "dy0", ("dz_codes", 0): "dy3"}
+ROOMS = {("x_picked", 0, 1): "h_pair0", "x_bf": "x2", ("dz_codes", 0): "dy3", ("dz_codes", 1): "neg_tw_cols"}
+SPARE = 352
 
 
 def tile_attend_gmw_tnh_kernel(tc, xT, dyT, hE, sw, tw, offs, offs2, out):
@@ -43,19 +44,20 @@ def tile_attend_gmw_tnh_kernel(tc, xT, dyT, hE, sw, tw, offs, offs2, out):
         src_list = keep.tile([P, E // 16], U16, name="src_list")
         dst_list = keep.tile([P, E // 16], U16, name="dst_list")
         x_tiles = [room("x%d" % j, V, F32) for j in range(TILES)]
-        dy_tiles = [room("dy%d" % k, V, F32) for k in range(TILES)]
+        dy_tiles = [room("dy%d" % k, V + (SPARE if k > 1 else 0), F32) for k in range(TILES)]
         h_parts = grid("h", K_PASS, F32)
         h_pairs = [room("h_pair%d" % g, E, F32) for g in range(PASSES)]
         x_bf = room("x_bf", TILES * E, BF16, ROOMS["x_bf"])
         for k in range(2):
             for g in range(PASSES):
                 h_parts[k][g] = h_pairs[g][:, k * K_PASS:(k + 1) * K_PASS]
-        h_parts[2][0] = x_bf[:, E:2 * E].bitcast(F32)
-        sw_rows = [room("sw_rows%d" % g, K_PASS, F32) for g in range(PASSES)]
+        sw_all = room("sw_all", E, F32)
+        sw_rows = [sw_all[:, g * K_PASS:(g + 1) * K_PASS] for g in range(PASSES)]
         w_rows = room("w_rows", K_PASS, F32)
         tw_cols = keep.tile([P, PASSES, 2, 2], F32, name="tw_cols")
-        neg_tw_cols = keep.tile([P, PASSES, 2, 2], F32, name="neg_tw_cols")
+        neg_tw_cols = room("neg_tw_cols", PASSES * PACK, F32)[:].rearrange("p (g u v) -> p g u v", u=2, v=2)
         ident = keep.tile([P, P], F32, name="ident")
+        ones, columns, lanes = [room(name, QUAD, F32) for name in ("ones", "columns", "lanes")]
         banks = [psum.tile([P, PACK, P], F32, name="bank%d" % b) for b in range(8)]
 
         nc.vector.memset(w_rows[:], 0.0)
@@ -70,7 +72,7 @@ def tile_attend_gmw_tnh_kernel(tc, xT, dyT, hE, sw, tw, offs, offs2, out):
             nc.sync.dma_start(x_tiles[j][:], xT[rows(j), :])
 
         def load_dy(k):
-            nc.sync.dma_start(dy_tiles[k][:], dyT[rows(k), :])
+            nc.sync.dma_start(dy_tiles[k][:, 0:V], dyT[rows(k), :])
 
         def load_h(k, g):
             nc.sync.dma_start(h_parts[k][g][:], hE[rows(k), edge_cols(g)])
@@ -106,10 +108,16 @@ def tile_attend_gmw_tnh_kernel(tc, xT, dyT, hE, sw, tw, offs, offs2, out):
         load_dy(3)
         load_h(2, 0)
         load_h(3, 0)
-        load_h(2, 1)
         load_h(3, 1)
+        load_h(2, 1)
 
-        make_identity(nc, ident[:])
+        nc.vector.memset(ones[:], 1.0)
+        nc.vector.memset(ident[:], 0.0)
+        nc.vector.tensor_tensor_scan(columns[:], ones[:], ones[:], 0.0, MULT, mybir.AluOpType.add)
+        nc.vector.transpose(lanes[:], columns[:])
+        for first in range(0, P, QUAD):
+            quad = slice(first, first + QUAD)
+            nc.vector.tensor_tensor(ident[quad, quad], columns[quad, :], lanes[quad, :], mybir.AluOpType.is_equal)
 
         def turn_weights():
             for g in range(PASSES):
@@ -151,14 +159,33 @@ def tile_attend_gmw_tnh_kernel(tc, xT, dyT, hE, sw, tw, offs, offs2, out):
         dz_codes = [room("dz_codes%d" % n, len(group) * P, U32, ROOMS.get(("dz_codes", n))) for n, group in enumerate(groups)]
         dz_scales = [room("dz_scales%d" % n, len(group) * P, U8) for n, group in enumerate(groups)]
         staged = [room("staged%d" % n, K_PASS, F32, ROOMS.get(("staged", n))) for n in range(TILES)]
-        x_pairs[3] = [factors[1][0][:, g * 2 * P:(g + 1) * 2 * P].bitcast(BF16) for g in range(PASSES)]
+        x_pairs[3][1] = x_picked[3][0][:, 0:K_PASS // 2].bitcast(BF16)
         squares[1][1] = x_bf[:, 0:E].bitcast(F32)
+        low_picked, low_pairs = room("low_picked", E, F32), room("low_pairs", E, BF16)
+        mid_picked, mid_pairs = room("mid_picked", E, F32), room("mid_pairs", E, BF16)
+        for half in range(2):
+            x_picked[half][0] = low_picked[:, half * K_PASS:(half + 1) * K_PASS]
+            x_picked[2][half] = mid_picked[:, half * K_PASS:(half + 1) * K_PASS]
+        dy_whole = [None, None] + [room("dy_whole%d" % k, E, F32) for k in range(2, TILES)]
 
         def gather_x(j, g):
             nc.scalar.activation(x_picked[j][g][:], x_tiles[j][:].indirect(edges(src_list, g)), ACT.Copy)
 
         def pair_x(j, g, engine=nc.gpsimd):
             engine.tensor_tensor(dealt(x_pairs[j][g][:]), in_runs(x_picked[j][g][:]), in_runs(sw_rows[g][:]), MULT)
+
+        def pair_two(picked, pairs, weights):
+            nc.gpsimd.tensor_tensor(
+                pairs.rearrange("p (u c b r) -> p c b u r", u=2, c=2, r=RUN),
+                picked.rearrange("p (c b u r) -> p c b u r", c=2, u=2, r=RUN), weights, MULT,
+            )
+
+        def turn_two(pairs, bank):
+            words = pairs.bitcast(F32)
+            for u in range(2):
+                for half in range(2):
+                    first = (2 * u + half) * P
+                    nc.tensor.transpose(banks[bank][:, 2 * half + u, :], words[:, first:first + P], ident[:])
 
         def turn_pairs(j, g, bank, slot):
             words = x_pairs[j][g][:].bitcast(F32)
@@ -177,6 +204,17 @@ def tile_attend_gmw_tnh_kernel(tc, xT, dyT, hE, sw, tw, offs, offs2, out):
             nc.vector.tensor_copy(
                 dealt(dy_picked[k][g][:].bitcast(U32)), dy_tiles[k][:].bitcast(U32).indirect(edges(dst_list, g)),
             )
+
+        def gather_dy_whole(k):
+            nc.vector.tensor_copy(
+                dy_whole[k][:].bitcast(U32).rearrange("p (u b r) -> p b u r", u=2, r=RUN), dy_tiles[k][:].bitcast(U32).indirect(dst_list[:]),
+            )
+
+        def turn_whole(k, g, bank):
+            for t in range(PACK):
+                u, v = divmod(t, 2)
+                first = (2 * u + g) * 2 * P
+                nc.tensor.transpose(banks[bank][:, t, :], dy_whole[k][:, first + v:first + 2 * P:2], ident[:])
 
         def square(k, g):
             nc.scalar.activation(dealt(squares[k][g][:]), in_runs(h_parts[k][g][:]), ACT.Square)
@@ -241,6 +279,8 @@ def tile_attend_gmw_tnh_kernel(tc, xT, dyT, hE, sw, tw, offs, offs2, out):
                 part.rearrange("p (j n) -> p j n", n=width),
             )
 
+        for k in range(2, TILES):
+            nc.vector.memset(dy_tiles[k][:, V:], 0.0)
         turn_weights()
         copy_weights()
         square(0, 0)
@@ -266,68 +306,62 @@ def tile_attend_gmw_tnh_kernel(tc, xT, dyT, hE, sw, tw, offs, offs2, out):
         turn_values(dy_picked[1][0], 6)
         gather_dy(1, 1)
         turn_pairs(1, 1, 1, 1)
-        pair_x(0, 0)
         gather_x(2, 1)
         make_dz(1, 0, 6)
         turn_values(dy_picked[1][1], 6)
-        pair_x(1, 0)
-        gather_dy(2, 0)
+        pair_two(low_picked[:], low_pairs[:], sw_rows[0].rearrange("p (b u r) -> p b u r", u=2, r=RUN).unsqueeze(1).to_broadcast([P, 2, RUN, 2, RUN]))
+        gather_dy_whole(2)
         weave_x(((0, 1), (1, 1)), 1)
         square(0, 1)
-        turn_pairs(0, 0, 1, 0)
-        turn_pairs(1, 0, 1, 1)
-        gather_dy(2, 1)
-        pair_x(2, 0)
+        turn_two(low_pairs[:], 1)
+        pair_two(mid_picked[:], mid_pairs[:], sw_all[:].rearrange("p (c b u r) -> p c b u r", c=2, u=2, r=RUN))
         square(1, 1)
         turn_squares(0, 1, (2, 3))
         gather_x(3, 0)
         turn_squares(1, 1, (2, 3))
         gather_x_plain(3, 1)
-        pair_x(2, 1)
         weave_x(((0, 0), (1, 0)), 1)
         make_factors(0, 1, 0, (2, 3))
-        gather_dy(3, 0)
-        pair_x(3, 1)
-        turn_values(dy_picked[2][1], 1)
-        turn_values(dy_picked[2][0], 2)
-        make_factors(0, 1, 1, (2, 3))
-        gather_dy(3, 1)
-        turn_pairs(2, 0, 3, 0)
-        turn_pairs(2, 1, 3, 1)
-        square(2, 0)
+        gather_dy_whole(3)
         pair_x(3, 0)
+        turn_two(mid_pairs[:], 1)
+        turn_whole(2, 0, 2)
+        make_factors(0, 1, 1, (2, 3))
+        turn_whole(2, 1, 3)
+        weave_x(((2, 0), (2, 1)), 1)
+        square(2, 0)
+        pair_x(3, 1)
         turn_squares(2, 0, (4, 5))
-        weave_x(((2, 0), (2, 1)), 3)
         make_dz(0, 1, 0)
         square(3, 0)
         make_dz(1, 1, 6)
-        turn_pairs(3, 1, 3, 1)
-        turn_pairs(3, 0, 3, 0)
+        turn_pairs(3, 0, 1, 0)
+        turn_pairs(3, 1, 1, 1)
         square_on_gpsimd(2, 1)
-        square(3, 1)
         turn_squares(3, 0, (4, 5))
-        weave_x(((3, 0), (3, 1)), 3)
+        weave_x(((3, 0), (3, 1)), 1)
+        square(3, 1)
         quantize_dz(0)
-        turn_squares(3, 1, (0, 6))
         turn_squares(2, 1, (0, 6))
+        turn_whole(3, 1, 1)
+        turn_squares(3, 1, (0, 6))
         make_factors(1, 0, 0, (4, 5))
-        turn_values(dy_picked[3][0], 4)
+        turn_whole(3, 0, 4)
         quantize_x()
         make_factors(1, 0, 1, (4, 5))
-        turn_values(dy_picked[3][1], 5)
         make_factors(1, 1, 0, (0, 6))
         make_dz(2, 0, 2)
-        multiply_left(0, 0)
+        multiply_left(0, 5)
         make_factors(1, 1, 1, (0, 6))
         make_dz(3, 0, 4)
-        multiply_left(1, 6)
-        make_dz(2, 1, 1)
+        multiply_left(1, 0)
+        make_dz(2, 1, 3)
         quantize_dz(1)
-        store(nc.scalar.copy, 0, 2, 0, 2 * P, 0, staged[0][:])
+        store(nc.scalar.copy, 0, 2, 0, 2 * P, 5, staged[0][:])
         multiply_column(2, 0, 2, range(TILES))
         quantize_dz(2)
-        make_dz(3, 1, 5)
-        store(nc.scalar.copy, 2, 2, 0, 2 * P, 6, staged[1][:])
+        make_dz(3, 1, 1)
+        store(nc.scalar.copy, 2, 2, 0, 2 * P, 0, staged[1][:])
         multiply_column(2, 1, 2, range(TILES))
         multiply_column(3, 0, 4, (0, 1))
         multiply_column(3, 0, 7, (2, 3))

@@ -13,20 +13,20 @@ U8 = mybir.dt.uint8
 E4M3 = mybir.dt.float8_e4m3fn_x4
 E5M2 = mybir.dt.float8_e5m2_x4
 ACT = mybir.ActivationFunctionType
-MULT = mybir.AluOpType.mult
+ALU = mybir.AluOpType
 
 P = 128
 PACK = 4
 K_PASS = P * PACK
 PASSES = E // K_PASS
-RUN = 16
-LIST_COLS = K_PASS // 16
 TILES = D // P
 PAIRS = TILES // 2
+RUN = 16
+LIST_COLS = K_PASS // 16
 QUAD = 32
-W_BANK = 6
-ROOMS = {("x_picked", 0, 1): "h_pair0", "x_bf": "x2", ("dz_codes", 0): "dy3", ("dz_codes", 1): "neg_tw_cols"}
 SPARE = 352
+BANKS = 8
+DZ_GROUPS = (((0, 0), (1, 0), (0, 1), (1, 1)), ((2, 0), (3, 0)), ((2, 1),), ((3, 1),))
 
 
 def tile_attend_gmw_tnh_kernel(tc, xT, dyT, hE, sw, tw, offs, offs2, out):
@@ -35,38 +35,61 @@ def tile_attend_gmw_tnh_kernel(tc, xT, dyT, hE, sw, tw, offs, offs2, out):
         keep = ctx.enter_context(tc.tile_pool(name="keep", bufs=1))
         psum = ctx.enter_context(tc.psum_pool(name="psum", bufs=1))
 
-        def room(name, width, dtype, tag=None):
-            return keep.tile([P, width], dtype, name=name, tag=tag or name, align_bytes=64)
+        def room(name, width, dtype, after=None):
+            return keep.tile([P, width], dtype, name=name, tag=after or name, align_bytes=64)
 
-        def grid(name, width, dtype, count=TILES):
-            return [[room("%s%d_%d" % (name, j, g), width, dtype, ROOMS.get((name, j, g))) for g in range(PASSES)] for j in range(count)]
+        def half(tile, n):
+            return tile[:, n * K_PASS:(n + 1) * K_PASS]
 
+        def rows(first, count=1):
+            return slice(first * P, (first + count) * P)
+
+        def in_runs(ap):
+            return ap.rearrange("p (b u r) -> p b u r", u=2, r=RUN)
+
+        def dealt(ap):
+            return ap.rearrange("p (u b r) -> p b u r", u=2, r=RUN)
+
+        banks = [psum.tile([P, PACK, P], F32, name="bank%d" % b) for b in range(BANKS)]
         src_list = keep.tile([P, E // 16], U16, name="src_list")
         dst_list = keep.tile([P, E // 16], U16, name="dst_list")
         x_tiles = [room("x%d" % j, V, F32) for j in range(TILES)]
-        dy_tiles = [room("dy%d" % k, V + (SPARE if k > 1 else 0), F32) for k in range(TILES)]
-        h_parts = grid("h", K_PASS, F32)
-        h_pairs = [room("h_pair%d" % g, E, F32) for g in range(PASSES)]
-        x_bf = room("x_bf", TILES * E, BF16, ROOMS["x_bf"])
-        for k in range(2):
-            for g in range(PASSES):
-                h_parts[k][g] = h_pairs[g][:, k * K_PASS:(k + 1) * K_PASS]
-        sw_all = room("sw_all", E, F32)
-        sw_rows = [sw_all[:, g * K_PASS:(g + 1) * K_PASS] for g in range(PASSES)]
-        w_rows = room("w_rows", K_PASS, F32)
-        tw_cols = keep.tile([P, PASSES, 2, 2], F32, name="tw_cols")
-        neg_tw_cols = room("neg_tw_cols", PASSES * PACK, F32)[:].rearrange("p (g u v) -> p g u v", u=2, v=2)
-        ident = keep.tile([P, P], F32, name="ident")
+        dy_tiles = [room("dy%d" % k, V + (SPARE if k >= 2 else 0), F32) for k in range(TILES)]
+        h_pairs = [[room("h%d_%d" % (m, g), E, F32) for g in range(PASSES)] for m in range(PAIRS)]
+        sw_rows = room("sw_rows", E, F32)
+        tw_rows = room("tw_rows", K_PASS, F32)
+        tw_cols = room("tw_cols", PASSES * PACK, F32)
+        neg_tw_cols = room("neg_tw_cols", PASSES * PACK, F32)
+        ident = room("ident", P, F32)
         ones, columns, lanes = [room(name, QUAD, F32) for name in ("ones", "columns", "lanes")]
-        banks = [psum.tile([P, PACK, P], F32, name="bank%d" % b) for b in range(8)]
 
-        nc.vector.memset(w_rows[:], 0.0)
-
-        def rows(j):
-            return slice(j * P, (j + 1) * P)
-
-        def edge_cols(g):
-            return slice(g * K_PASS, (g + 1) * K_PASS)
+        x_bf = room("x_bf", TILES * E, BF16, after="x2")
+        dz_bf = [room("dz_bf%d" % n, len(group) * K_PASS, BF16) for n, group in enumerate(DZ_GROUPS)]
+        home = {chunk: (n, at) for n, group in enumerate(DZ_GROUPS) for at, chunk in enumerate(group)}
+        low_picked, low_pairs = room("low_picked", E, F32), room("low_pairs", E, BF16)
+        mid_picked, mid_pairs = room("mid_picked", E, F32), room("mid_pairs", E, BF16)
+        x_picked = {chunk: room("x_picked%d_%d" % chunk, K_PASS, F32)[:] for chunk in ((0, 1), (1, 1), (3, 0), (3, 1))}
+        x_pairs = {chunk: room("x_pairs%d_%d" % chunk, K_PASS, BF16)[:] for chunk in ((0, 1), (1, 1), (3, 0))}
+        x_pairs[3, 1] = x_picked[3, 0][:, 0:K_PASS // 2].bitcast(BF16)
+        for n in range(2):
+            x_picked[n, 0] = half(low_picked, n)
+            x_picked[2, n] = half(mid_picked, n)
+        dy_picked = {(k, g): room("dy_picked%d_%d" % (k, g), K_PASS, F32)[:] for k in range(2) for g in range(PASSES)}
+        dy_whole = {k: room("dy_whole%d" % k, E, F32) for k in range(2, TILES)}
+        squares = {
+            (k, g): room("square%d_%d" % (k, g), K_PASS, F32)[:]
+            for k in range(TILES) for g in range(PASSES) if (k, g) != (1, 1)
+        }
+        squares[1, 1] = x_bf[:, 0:E].bitcast(F32)
+        factors = [[room("factor%d_%d" % (m, g), E, F32) for g in range(PASSES)] for m in range(PAIRS)]
+        x_codes = room("x_codes", TILES * PASSES * P, U32)
+        x_scales = room("x_scales", TILES * PASSES * P, U8)
+        dz_codes = [
+            room("dz_codes%d" % n, len(group) * P, U32, after)
+            for n, (group, after) in enumerate(zip(DZ_GROUPS, ("dy3", "neg_tw_cols", None, None)))
+        ]
+        dz_scales = [room("dz_scales%d" % n, len(group) * P, U8) for n, group in enumerate(DZ_GROUPS)]
+        staged = [room("staged%d" % n, K_PASS, F32) for n in range(TILES)]
 
         def load_x(j):
             nc.sync.dma_start(x_tiles[j][:], xT[rows(j), :])
@@ -74,25 +97,20 @@ def tile_attend_gmw_tnh_kernel(tc, xT, dyT, hE, sw, tw, offs, offs2, out):
         def load_dy(k):
             nc.sync.dma_start(dy_tiles[k][:, 0:V], dyT[rows(k), :])
 
-        def load_h(k, g):
-            nc.sync.dma_start(h_parts[k][g][:], hE[rows(k), edge_cols(g)])
-
-        def load_h_pair(g):
+        def load_h(m, g):
             nc.sync.dma_start(
-                h_pairs[g][:].rearrange("p (k e) -> p k e", k=2), hE[0:2 * P, edge_cols(g)].rearrange("(k p) e -> p k e", p=P),
+                h_pairs[m][g][:].rearrange("p (k e) -> p k e", k=2),
+                half(hE[rows(2 * m, 2), :], g).rearrange("(k p) e -> p k e", p=P),
             )
 
         def load_sw(g):
-            nc.sync.dma_start(sw_rows[g][:], sw[:, edge_cols(g)])
+            nc.sync.dma_start(half(sw_rows, g), half(sw, g))
 
-        def load_row(first, weights):
-            nc.sync.dma_start(
-                w_rows[first:first + 2, :].rearrange("u (b r) -> u b r", r=RUN),
-                weights[0, :].rearrange("(b u r) -> u b r", u=2, r=RUN),
-            )
-
-        load_h_pair(0)
-        load_row(0, tw)
+        nc.vector.memset(tw_rows[:], 0.0)
+        load_h(0, 0)
+        nc.sync.dma_start(
+            tw_rows[0:2, :].rearrange("u (b r) -> u b r", r=RUN), tw[0, :].rearrange("(b u r) -> u b r", u=2, r=RUN),
+        )
         nc.sync.dma_start(src_list[:], offs)
         load_x(0)
         load_dy(0)
@@ -103,161 +121,122 @@ def tile_attend_gmw_tnh_kernel(tc, xT, dyT, hE, sw, tw, offs, offs2, out):
         load_x(2)
         load_sw(0)
         load_dy(2)
-        load_h_pair(1)
+        load_h(0, 1)
         load_x(3)
         load_dy(3)
-        load_h(2, 0)
-        load_h(3, 0)
-        load_h(3, 1)
-        load_h(2, 1)
+        load_h(1, 0)
+        load_h(1, 1)
 
         nc.vector.memset(ones[:], 1.0)
         nc.vector.memset(ident[:], 0.0)
-        nc.vector.tensor_tensor_scan(columns[:], ones[:], ones[:], 0.0, MULT, mybir.AluOpType.add)
+        nc.vector.tensor_tensor_scan(columns[:], ones[:], ones[:], 0.0, ALU.mult, ALU.add)
         nc.vector.transpose(lanes[:], columns[:])
         for first in range(0, P, QUAD):
             quad = slice(first, first + QUAD)
-            nc.vector.tensor_tensor(ident[quad, quad], columns[quad, :], lanes[quad, :], mybir.AluOpType.is_equal)
+            nc.vector.tensor_tensor(ident[quad, quad], columns[quad, :], lanes[quad, :], ALU.is_equal)
+        for k in dy_whole:
+            nc.vector.memset(dy_tiles[k][:, V:], 0.0)
 
-        def turn_weights():
-            for g in range(PASSES):
-                for v in range(2):
-                    nc.tensor.transpose(banks[W_BANK][:, 2 * g + v, :], w_rows[:, g * 2 * P + v:(g + 1) * 2 * P:2], ident[:])
+        def turn(bank, slot, src):
+            nc.tensor.transpose(banks[bank][:, slot, :], src, ident[:])
 
-        def copy_weights():
-            tw_turned = banks[W_BANK][:, :, 0:2].rearrange("p (g v) u -> p g u v", v=2)
-            nc.vector.tensor_copy(tw_cols[:], tw_turned)
-            nc.vector.tensor_scalar_mul(neg_tw_cols[:], tw_turned, -1.0)
-
-        def in_runs(ap):
-            return ap.rearrange("p (b u r) -> p b u r", u=2, r=RUN)
-
-        def dealt(ap):
-            return ap.rearrange("p (u b r) -> p b u r", u=2, r=RUN)
+        def every_second(src, run, v):
+            return src[:, run * 2 * P + v:(run + 1) * 2 * P:2]
 
         def edges(index_list, g):
             return index_list[:, g * LIST_COLS:(g + 1) * LIST_COLS]
 
-        def place(src, t):
-            u, v = divmod(t, 2)
-            return src[:, u * 2 * P + v:(u + 1) * 2 * P:2]
+        def weight_columns(bank):
+            for g in range(PASSES):
+                for v in range(2):
+                    turn(bank, 2 * g + v, every_second(tw_rows, g, v))
+            turned = banks[bank][:, :, 0:2].rearrange("p (g v) u -> p g u v", v=2)
+            nc.vector.tensor_copy(tw_cols[:].rearrange("p (g u v) -> p g u v", u=2, v=2), turned)
+            nc.vector.tensor_scalar_mul(neg_tw_cols[:].rearrange("p (g u v) -> p g u v", u=2, v=2), turned, -1.0)
 
-        def turn_values(src, bank):
-            for t in range(PACK):
-                nc.tensor.transpose(banks[bank][:, t, :], place(src, t), ident[:])
+        def gather_x_on_scalar(j, g):
+            nc.scalar.activation(x_picked[j, g], x_tiles[j][:].indirect(edges(src_list, g)), ACT.Copy)
 
-        x_picked = grid("x_picked", K_PASS, F32)
-        x_pairs = grid("x_pairs", K_PASS, BF16)
-        dy_picked = grid("dy_picked", K_PASS, F32)
-        squares = grid("sq", K_PASS, F32)
-        factors = grid("factor", 2 * K_PASS, F32, PAIRS)
-        groups = (((0, 0), (1, 0), (0, 1), (1, 1)), ((2, 0), (3, 0)), ((2, 1),), ((3, 1),))
-        home = {chunk: (n, at) for n, group in enumerate(groups) for at, chunk in enumerate(group)}
-        dz_bf = [room("dz_bf%d" % n, len(group) * K_PASS, BF16, ROOMS.get(("dz_bf", n))) for n, group in enumerate(groups)]
-        x_codes = room("x_codes", TILES * PASSES * P, U32, ROOMS.get("x_codes"))
-        x_scales = room("x_scales", TILES * PASSES * P, U8)
-        dz_codes = [room("dz_codes%d" % n, len(group) * P, U32, ROOMS.get(("dz_codes", n))) for n, group in enumerate(groups)]
-        dz_scales = [room("dz_scales%d" % n, len(group) * P, U8) for n, group in enumerate(groups)]
-        staged = [room("staged%d" % n, K_PASS, F32, ROOMS.get(("staged", n))) for n in range(TILES)]
-        x_pairs[3][1] = x_picked[3][0][:, 0:K_PASS // 2].bitcast(BF16)
-        squares[1][1] = x_bf[:, 0:E].bitcast(F32)
-        low_picked, low_pairs = room("low_picked", E, F32), room("low_pairs", E, BF16)
-        mid_picked, mid_pairs = room("mid_picked", E, F32), room("mid_pairs", E, BF16)
-        for half in range(2):
-            x_picked[half][0] = low_picked[:, half * K_PASS:(half + 1) * K_PASS]
-            x_picked[2][half] = mid_picked[:, half * K_PASS:(half + 1) * K_PASS]
-        dy_whole = [None, None] + [room("dy_whole%d" % k, E, F32) for k in range(2, TILES)]
+        def gather_x_on_vector(j, g):
+            nc.vector.tensor_copy(x_picked[j, g].bitcast(U32), x_tiles[j][:].bitcast(U32).indirect(edges(src_list, g)))
 
-        def gather_x(j, g):
-            nc.scalar.activation(x_picked[j][g][:], x_tiles[j][:].indirect(edges(src_list, g)), ACT.Copy)
-
-        def pair_x(j, g, engine=nc.gpsimd):
-            engine.tensor_tensor(dealt(x_pairs[j][g][:]), in_runs(x_picked[j][g][:]), in_runs(sw_rows[g][:]), MULT)
+        def pair_x(j, g):
+            nc.gpsimd.tensor_tensor(dealt(x_pairs[j, g]), in_runs(x_picked[j, g]), in_runs(half(sw_rows, g)), ALU.mult)
 
         def pair_two(picked, pairs, weights):
             nc.gpsimd.tensor_tensor(
-                pairs.rearrange("p (u c b r) -> p c b u r", u=2, c=2, r=RUN),
-                picked.rearrange("p (c b u r) -> p c b u r", c=2, u=2, r=RUN), weights, MULT,
+                pairs[:].rearrange("p (u c b r) -> p c b u r", u=2, c=2, r=RUN),
+                picked[:].rearrange("p (c b u r) -> p c b u r", c=2, u=2, r=RUN), weights, ALU.mult,
             )
 
+        def turn_pairs(j, g, bank, c):
+            for u in range(2):
+                turn(bank, 2 * c + u, x_pairs[j, g].bitcast(F32)[:, rows(u)])
+
         def turn_two(pairs, bank):
-            words = pairs.bitcast(F32)
             for u in range(2):
-                for half in range(2):
-                    first = (2 * u + half) * P
-                    nc.tensor.transpose(banks[bank][:, 2 * half + u, :], words[:, first:first + P], ident[:])
+                for c in range(2):
+                    turn(bank, 2 * c + u, pairs[:].bitcast(F32)[:, rows(2 * u + c)])
 
-        def turn_pairs(j, g, bank, slot):
-            words = x_pairs[j][g][:].bitcast(F32)
-            for u in range(2):
-                nc.tensor.transpose(banks[bank][:, 2 * slot + u, :], words[:, u * P:(u + 1) * P], ident[:])
-
-        def weave_x(chunks, bank):
+        def weave_x(chunks, bank, move=nc.scalar.copy):
             words = x_bf[:].bitcast(F32).rearrange("p (c d u) -> p c d u", d=P, u=2)
             first, second = [TILES * g + j for j, g in chunks]
-            nc.scalar.copy(words[:, first:second + 1:second - first], banks[bank][:].rearrange("p (c u) d -> p c d u", u=2))
-
-        def gather_x_plain(j, g):
-            nc.vector.tensor_copy(x_picked[j][g][:].bitcast(U32), x_tiles[j][:].bitcast(U32).indirect(edges(src_list, g)))
+            move(words[:, first:second + 1:second - first], banks[bank][:].rearrange("p (c u) d -> p c d u", u=2))
 
         def gather_dy(k, g):
             nc.vector.tensor_copy(
-                dealt(dy_picked[k][g][:].bitcast(U32)), dy_tiles[k][:].bitcast(U32).indirect(edges(dst_list, g)),
+                dealt(dy_picked[k, g].bitcast(U32)), dy_tiles[k][:].bitcast(U32).indirect(edges(dst_list, g)),
             )
 
         def gather_dy_whole(k):
-            nc.vector.tensor_copy(
-                dy_whole[k][:].bitcast(U32).rearrange("p (u b r) -> p b u r", u=2, r=RUN), dy_tiles[k][:].bitcast(U32).indirect(dst_list[:]),
-            )
+            nc.vector.tensor_copy(dealt(dy_whole[k][:].bitcast(U32)), dy_tiles[k][:].bitcast(U32).indirect(dst_list[:]))
 
-        def turn_whole(k, g, bank):
+        def turn_dy(k, g, bank):
             for t in range(PACK):
                 u, v = divmod(t, 2)
-                first = (2 * u + g) * 2 * P
-                nc.tensor.transpose(banks[bank][:, t, :], dy_whole[k][:, first + v:first + 2 * P:2], ident[:])
+                if k in dy_whole:
+                    turn(bank, t, every_second(dy_whole[k], PASSES * u + g, v))
+                else:
+                    turn(bank, t, every_second(dy_picked[k, g], u, v))
 
         def square(k, g):
-            nc.scalar.activation(dealt(squares[k][g][:]), in_runs(h_parts[k][g][:]), ACT.Square)
+            nc.scalar.activation(dealt(squares[k, g]), in_runs(half(h_pairs[k // 2][g], k % 2)), ACT.Square)
 
         def square_on_gpsimd(k, g):
-            h = in_runs(h_parts[k][g][:])
-            nc.gpsimd.tensor_tensor(dealt(squares[k][g][:]), h, h, MULT)
+            h = in_runs(half(h_pairs[k // 2][g], k % 2))
+            nc.gpsimd.tensor_tensor(dealt(squares[k, g]), h, h, ALU.mult)
 
         def turn_squares(k, g, two_banks):
             for t in range(PACK):
-                nc.tensor.transpose(banks[two_banks[t // 2]][:, 2 * (t % 2) + k % 2, :], place(squares[k][g], t), ident[:])
+                u, v = divmod(t, 2)
+                turn(two_banks[u], 2 * v + k % 2, every_second(squares[k, g], u, v))
 
-        def make_factors(m, g, u, two_banks):
+        def make_factors(m, g, u, bank):
             for v in range(2):
                 t = 2 * u + v
+                at = slice(PACK * g + t, PACK * g + t + 1)
                 nc.scalar.activation(
-                    factors[m][g][:, t * 2 * P:(t + 1) * 2 * P],
-                    banks[two_banks[u]][:, 2 * v:2 * v + 2, :].rearrange("p k n -> p (k n)"), ACT.Identity,
-                    bias=tw_cols[:, g, u, v:v + 1], scale=neg_tw_cols[:, g, u, v:v + 1],
+                    factors[m][g][:, rows(2 * t, 2)], banks[bank][:, 2 * v:2 * v + 2, :].rearrange("p k n -> p (k n)"),
+                    ACT.Identity, bias=tw_cols[:, at], scale=neg_tw_cols[:, at],
                 )
 
         def make_dz(k, g, bank):
             group, at = home[k, g]
-            start = at * K_PASS
             nc.vector.tensor_tensor(
-                dz_bf[group][:, start:start + K_PASS].rearrange("p (c i t) -> p c t i", i=4, t=PACK),
+                half(dz_bf[group], at).rearrange("p (c i t) -> p c t i", i=4, t=PACK),
                 banks[bank][:].rearrange("p t (c i) -> p c t i", i=4),
                 factors[k // 2][g][:].rearrange("p (t k c i) -> p k c t i", t=PACK, k=2, i=4)[:, k % 2],
-                MULT,
+                ALU.mult,
             )
 
-        def quantize_x():
-            nc.vector.quantize_mx(out=x_codes[:].bitcast(E4M3), scales=x_scales[:], in_=x_bf[:])
-
         def quantize_dz(group):
-            nc.vector.quantize_mx(out=dz_codes[group][:].bitcast(E5M2), scales=dz_scales[group][:], in_=dz_bf[group][:, 0:len(groups[group]) * K_PASS])
+            nc.vector.quantize_mx(out=dz_codes[group][:].bitcast(E5M2), scales=dz_scales[group][:], in_=dz_bf[group][:])
 
-        def multiply(j, g, k, width, acc, start, stop):
-            cols = slice((TILES * g + j) * P, (TILES * g + j + 1) * P)
+        def multiply(j, g, k, count, acc, start, stop):
             group, at = home[k, g]
-            moving = slice(at * P, at * P + width)
+            still, moving = rows(TILES * g + j), rows(at, count)
             nc.tensor.matmul_mx(
-                out=acc, lhsT=x_codes[:, cols].bitcast(E4M3), lhsT_scale=x_scales[:, cols],
+                out=acc, lhsT=x_codes[:, still].bitcast(E4M3), lhsT_scale=x_scales[:, still],
                 rhs=dz_codes[group][:, moving].bitcast(E5M2), rhs_scale=dz_scales[group][:, moving],
                 start=start, stop=stop,
             )
@@ -266,69 +245,68 @@ def tile_attend_gmw_tnh_kernel(tc, xT, dyT, hE, sw, tw, offs, offs2, out):
             for s in range(2):
                 for g in range(PASSES):
                     acc = banks[bank][:, 2 * s:2 * s + 2, :].rearrange("p k n -> p (k n)")
-                    multiply(2 * m + s, g, 0, 2 * P, acc, g == 0, g == PASSES - 1)
+                    multiply(2 * m + s, g, 0, 2, acc, g == 0, g == PASSES - 1)
 
         def multiply_column(k, g, bank, tiles):
             for s, j in enumerate(tiles):
-                multiply(j, g, k, P, banks[bank][:, s, :], (g, s) == (0, 0), (g, s) == (PASSES - 1, len(tiles) - 1))
+                multiply(j, g, k, 1, banks[bank][:, s, :], (g, s) == (0, 0), (g, s) == (PASSES - 1, len(tiles) - 1))
 
-        def store(move, first_tile, tiles, first_col, width, bank, part):
-            move(part, banks[bank][:].rearrange("p t n -> p (t n)")[:, 0:tiles * width])
+        def store(move, row_tiles, col_tiles, bank, part):
+            width = col_tiles.stop - col_tiles.start
+            move(part, banks[bank][:].rearrange("p t n -> p (t n)")[:, 0:part.shape[1]])
             nc.sync.dma_start(
-                out[first_tile * P:(first_tile + tiles) * P, first_col:first_col + width].rearrange("(j p) n -> p j n", p=P),
-                part.rearrange("p (j n) -> p j n", n=width),
+                out[row_tiles, col_tiles].rearrange("(j p) n -> p j n", p=P), part.rearrange("p (j n) -> p j n", n=width),
             )
 
-        for k in range(2, TILES):
-            nc.vector.memset(dy_tiles[k][:, V:], 0.0)
-        turn_weights()
-        copy_weights()
+        weight_columns(6)
         square(0, 0)
         square(1, 0)
         turn_squares(0, 0, (0, 1))
         turn_squares(1, 0, (0, 1))
-        gather_x_plain(0, 0)
-        gather_x(0, 1)
+        gather_x_on_vector(0, 0)
+        gather_x_on_scalar(0, 1)
         gather_dy(0, 0)
-        make_factors(0, 0, 0, (0, 1))
-        make_factors(0, 0, 1, (0, 1))
-        turn_values(dy_picked[0][0], 0)
+        make_factors(0, 0, 0, 0)
+        make_factors(0, 0, 1, 1)
+        turn_dy(0, 0, 0)
         gather_dy(0, 1)
-        gather_x(1, 1)
+        gather_x_on_scalar(1, 1)
         pair_x(0, 1)
         make_dz(0, 0, 0)
-        gather_x(1, 0)
+        gather_x_on_scalar(1, 0)
         pair_x(1, 1)
         gather_dy(1, 0)
-        turn_values(dy_picked[0][1], 0)
+        turn_dy(0, 1, 0)
         turn_pairs(0, 1, 1, 0)
-        gather_x(2, 0)
-        turn_values(dy_picked[1][0], 6)
+        gather_x_on_scalar(2, 0)
+        turn_dy(1, 0, 6)
         gather_dy(1, 1)
         turn_pairs(1, 1, 1, 1)
-        gather_x(2, 1)
+        gather_x_on_scalar(2, 1)
         make_dz(1, 0, 6)
-        turn_values(dy_picked[1][1], 6)
-        pair_two(low_picked[:], low_pairs[:], sw_rows[0].rearrange("p (b u r) -> p b u r", u=2, r=RUN).unsqueeze(1).to_broadcast([P, 2, RUN, 2, RUN]))
+        turn_dy(1, 1, 6)
+        pair_two(low_picked, low_pairs, in_runs(half(sw_rows, 0)).unsqueeze(1).to_broadcast([P, 2, RUN, 2, RUN]))
         gather_dy_whole(2)
         weave_x(((0, 1), (1, 1)), 1)
+
         square(0, 1)
-        turn_two(low_pairs[:], 1)
-        pair_two(mid_picked[:], mid_pairs[:], sw_all[:].rearrange("p (c b u r) -> p c b u r", c=2, u=2, r=RUN))
+        turn_two(low_pairs, 1)
+        pair_two(mid_picked, mid_pairs, sw_rows[:].rearrange("p (c b u r) -> p c b u r", c=2, u=2, r=RUN))
         square(1, 1)
         turn_squares(0, 1, (2, 3))
-        gather_x(3, 0)
+        gather_x_on_scalar(3, 0)
         turn_squares(1, 1, (2, 3))
-        gather_x_plain(3, 1)
+        gather_x_on_vector(3, 1)
         weave_x(((0, 0), (1, 0)), 1)
-        make_factors(0, 1, 0, (2, 3))
+        make_factors(0, 1, 0, 2)
         gather_dy_whole(3)
         pair_x(3, 0)
-        turn_two(mid_pairs[:], 1)
-        turn_whole(2, 0, 2)
-        make_factors(0, 1, 1, (2, 3))
-        turn_whole(2, 1, 3)
+        turn_two(mid_pairs, 1)
+        turn_dy(2, 0, 2)
+        make_factors(0, 1, 1, 3)
+        turn_dy(2, 1, 3)
         weave_x(((2, 0), (2, 1)), 1)
+
         square(2, 0)
         pair_x(3, 1)
         turn_squares(2, 0, (4, 5))
@@ -343,31 +321,31 @@ def tile_attend_gmw_tnh_kernel(tc, xT, dyT, hE, sw, tw, offs, offs2, out):
         square(3, 1)
         quantize_dz(0)
         turn_squares(2, 1, (0, 6))
-        turn_whole(3, 1, 1)
+        turn_dy(3, 1, 1)
         turn_squares(3, 1, (0, 6))
-        make_factors(1, 0, 0, (4, 5))
-        turn_whole(3, 0, 4)
-        quantize_x()
-        make_factors(1, 0, 1, (4, 5))
-        make_factors(1, 1, 0, (0, 6))
+        make_factors(1, 0, 0, 4)
+        turn_dy(3, 0, 4)
+        nc.vector.quantize_mx(out=x_codes[:].bitcast(E4M3), scales=x_scales[:], in_=x_bf[:])
+        make_factors(1, 0, 1, 5)
+        make_factors(1, 1, 0, 0)
         make_dz(2, 0, 2)
         multiply_left(0, 5)
-        make_factors(1, 1, 1, (0, 6))
+        make_factors(1, 1, 1, 6)
         make_dz(3, 0, 4)
         multiply_left(1, 0)
         make_dz(2, 1, 3)
         quantize_dz(1)
-        store(nc.scalar.copy, 0, 2, 0, 2 * P, 5, staged[0][:])
+        store(nc.scalar.copy, rows(0, 2), rows(0, 2), 5, staged[0][:])
         multiply_column(2, 0, 2, range(TILES))
         quantize_dz(2)
         make_dz(3, 1, 1)
-        store(nc.scalar.copy, 2, 2, 0, 2 * P, 0, staged[1][:])
+        store(nc.scalar.copy, rows(2, 2), rows(0, 2), 0, staged[1][:])
         multiply_column(2, 1, 2, range(TILES))
         multiply_column(3, 0, 4, (0, 1))
         multiply_column(3, 0, 7, (2, 3))
         quantize_dz(3)
-        store(nc.scalar.copy, 0, TILES, 2 * P, P, 2, staged[2][:])
+        store(nc.scalar.copy, rows(0, TILES), rows(2), 2, staged[2][:])
         multiply_column(3, 1, 4, (0, 1))
         multiply_column(3, 1, 7, (2, 3))
-        store(nc.vector.tensor_copy, 0, 2, 3 * P, P, 4, staged[3][:, 0:2 * P])
-        store(nc.scalar.copy, 2, 2, 3 * P, P, 7, staged[3][:, 2 * P:4 * P])
+        store(nc.vector.tensor_copy, rows(0, 2), rows(3), 4, staged[3][:, rows(0, 2)])
+        store(nc.scalar.copy, rows(2, 2), rows(3), 7, staged[3][:, rows(2, 2)])

from contextlib import ExitStack

import concourse.mybir as mybir

V, E, D, DV = 1024, 1024, 512, 512
FLOPS = 2 * E * D * DV

F32 = mybir.dt.float32
BF16 = mybir.dt.bfloat16
U32 = mybir.dt.uint32
U16 = mybir.dt.uint16
U8 = mybir.dt.uint8
E4M3 = mybir.dt.float8_e4m3fn_x4
E5M2 = mybir.dt.float8_e5m2_x4
ACT = mybir.ActivationFunctionType
ALU = mybir.AluOpType

P = 128
PACK = 4
K_PASS = P * PACK
PASSES = E // K_PASS
TILES = D // P
PAIRS = TILES // 2
RUN = 16
LIST_COLS = K_PASS // 16
QUAD = 32
SPARE = 352
BANKS = 8
DZ_GROUPS = (((0, 0), (1, 0), (0, 1), (1, 1)), ((2, 0), (3, 0)), ((2, 1),), ((3, 1),))


def tile_attend_gmw_tnh_kernel(tc, xT, dyT, hE, sw, tw, offs, offs2, out):
    nc = tc.nc
    with ExitStack() as ctx:
        keep = ctx.enter_context(tc.tile_pool(name="keep", bufs=1))
        psum = ctx.enter_context(tc.psum_pool(name="psum", bufs=1))

        def room(name, width, dtype, after=None):
            return keep.tile([P, width], dtype, name=name, tag=after or name, align_bytes=64)

        def half(tile, n):
            return tile[:, n * K_PASS:(n + 1) * K_PASS]

        def rows(first, count=1):
            return slice(first * P, (first + count) * P)

        def in_runs(ap):
            return ap.rearrange("p (b u r) -> p b u r", u=2, r=RUN)

        def dealt(ap):
            return ap.rearrange("p (u b r) -> p b u r", u=2, r=RUN)

        banks = [psum.tile([P, PACK, P], F32, name="bank%d" % b) for b in range(BANKS)]
        src_list = keep.tile([P, E // 16], U16, name="src_list")
        dst_list = keep.tile([P, E // 16], U16, name="dst_list")
        x_tiles = [room("x%d" % j, V, F32) for j in range(TILES)]
        dy_tiles = [room("dy%d" % k, V + (SPARE if k >= 2 else 0), F32) for k in range(TILES)]
        h_pairs = [[room("h%d_%d" % (m, g), E, F32) for g in range(PASSES)] for m in range(PAIRS)]
        sw_rows = room("sw_rows", E, F32)
        tw_rows = room("tw_rows", K_PASS, F32)
        tw_cols = room("tw_cols", PASSES * PACK, F32)
        neg_tw_cols = room("neg_tw_cols", PASSES * PACK, F32)
        ident = room("ident", P, F32)
        ones, columns, lanes = [room(name, QUAD, F32) for name in ("ones", "columns", "lanes")]

        x_bf = room("x_bf", TILES * E, BF16, after="x2")
        dz_bf = [room("dz_bf%d" % n, len(group) * K_PASS, BF16) for n, group in enumerate(DZ_GROUPS)]
        home = {chunk: (n, at) for n, group in enumerate(DZ_GROUPS) for at, chunk in enumerate(group)}
        low_picked, low_pairs = room("low_picked", E, F32), room("low_pairs", E, BF16)
        mid_picked, mid_pairs = room("mid_picked", E, F32), room("mid_pairs", E, BF16)
        x_picked = {chunk: room("x_picked%d_%d" % chunk, K_PASS, F32)[:] for chunk in ((0, 1), (1, 1), (3, 0), (3, 1))}
        x_pairs = {chunk: room("x_pairs%d_%d" % chunk, K_PASS, BF16)[:] for chunk in ((0, 1), (1, 1), (3, 0))}
        x_pairs[3, 1] = x_picked[3, 0][:, 0:K_PASS // 2].bitcast(BF16)
        for n in range(2):
            x_picked[n, 0] = half(low_picked, n)
            x_picked[2, n] = half(mid_picked, n)
        dy_picked = {(k, g): room("dy_picked%d_%d" % (k, g), K_PASS, F32)[:] for k in range(2) for g in range(PASSES)}
        dy_whole = {k: room("dy_whole%d" % k, E, F32) for k in range(2, TILES)}
        squares = {
            (k, g): room("square%d_%d" % (k, g), K_PASS, F32)[:]
            for k in range(TILES) for g in range(PASSES) if (k, g) != (1, 1)
        }
        squares[1, 1] = x_bf[:, 0:E].bitcast(F32)
        factors = [[room("factor%d_%d" % (m, g), E, F32) for g in range(PASSES)] for m in range(PAIRS)]
        x_codes = room("x_codes", TILES * PASSES * P, U32)
        x_scales = room("x_scales", TILES * PASSES * P, U8)
        dz_codes = [
            room("dz_codes%d" % n, len(group) * P, U32, after)
            for n, (group, after) in enumerate(zip(DZ_GROUPS, ("dy3", "neg_tw_cols", None, None)))
        ]
        dz_scales = [room("dz_scales%d" % n, len(group) * P, U8) for n, group in enumerate(DZ_GROUPS)]
        staged = [room("staged%d" % n, K_PASS, F32) for n in range(TILES)]

        def load_x(j):
            nc.sync.dma_start(x_tiles[j][:], xT[rows(j), :])

        def load_dy(k):
            nc.sync.dma_start(dy_tiles[k][:, 0:V], dyT[rows(k), :])

        def load_h(m, g):
            nc.sync.dma_start(
                h_pairs[m][g][:].rearrange("p (k e) -> p k e", k=2),
                half(hE[rows(2 * m, 2), :], g).rearrange("(k p) e -> p k e", p=P),
            )

        def load_sw(g):
            nc.sync.dma_start(half(sw_rows, g), half(sw, g))

        nc.vector.memset(tw_rows[:], 0.0)
        load_h(0, 0)
        nc.sync.dma_start(
            tw_rows[0:2, :].rearrange("u (b r) -> u b r", r=RUN), tw[0, :].rearrange("(b u r) -> u b r", u=2, r=RUN),
        )
        nc.sync.dma_start(src_list[:], offs)
        load_x(0)
        load_dy(0)
        nc.sync.dma_start(dst_list[:], offs2)
        load_x(1)
        load_sw(1)
        load_dy(1)
        load_x(2)
        load_sw(0)
        load_dy(2)
        load_h(0, 1)
        load_x(3)
        load_dy(3)
        load_h(1, 0)
        load_h(1, 1)

        nc.vector.memset(ones[:], 1.0)
        nc.vector.memset(ident[:], 0.0)
        nc.vector.tensor_tensor_scan(columns[:], ones[:], ones[:], 0.0, ALU.mult, ALU.add)
        nc.vector.transpose(lanes[:], columns[:])
        for first in range(0, P, QUAD):
            quad = slice(first, first + QUAD)
            nc.vector.tensor_tensor(ident[quad, quad], columns[quad, :], lanes[quad, :], ALU.is_equal)
        for k in dy_whole:
            nc.vector.memset(dy_tiles[k][:, V:], 0.0)

        def turn(bank, slot, src):
            nc.tensor.transpose(banks[bank][:, slot, :], src, ident[:])

        def every_second(src, run, v):
            return src[:, run * 2 * P + v:(run + 1) * 2 * P:2]

        def edges(index_list, g):
            return index_list[:, g * LIST_COLS:(g + 1) * LIST_COLS]

        def weight_columns(bank):
            for g in range(PASSES):
                for v in range(2):
                    turn(bank, 2 * g + v, every_second(tw_rows, g, v))
            turned = banks[bank][:, :, 0:2].rearrange("p (g v) u -> p g u v", v=2)
            nc.vector.tensor_copy(tw_cols[:].rearrange("p (g u v) -> p g u v", u=2, v=2), turned)
            nc.vector.tensor_scalar_mul(neg_tw_cols[:].rearrange("p (g u v) -> p g u v", u=2, v=2), turned, -1.0)

        def gather_x_on_scalar(j, g):
            nc.scalar.activation(x_picked[j, g], x_tiles[j][:].indirect(edges(src_list, g)), ACT.Copy)

        def gather_x_on_vector(j, g):
            nc.vector.tensor_copy(x_picked[j, g].bitcast(U32), x_tiles[j][:].bitcast(U32).indirect(edges(src_list, g)))

        def pair_x(j, g):
            nc.gpsimd.tensor_tensor(dealt(x_pairs[j, g]), in_runs(x_picked[j, g]), in_runs(half(sw_rows, g)), ALU.mult)

        def pair_two(picked, pairs, weights):
            nc.gpsimd.tensor_tensor(
                pairs[:].rearrange("p (u c b r) -> p c b u r", u=2, c=2, r=RUN),
                picked[:].rearrange("p (c b u r) -> p c b u r", c=2, u=2, r=RUN), weights, ALU.mult,
            )

        def turn_pairs(j, g, bank, c):
            for u in range(2):
                turn(bank, 2 * c + u, x_pairs[j, g].bitcast(F32)[:, rows(u)])

        def turn_two(pairs, bank):
            for u in range(2):
                for c in range(2):
                    turn(bank, 2 * c + u, pairs[:].bitcast(F32)[:, rows(2 * u + c)])

        def weave_x(chunks, bank, move=nc.scalar.copy):
            words = x_bf[:].bitcast(F32).rearrange("p (c d u) -> p c d u", d=P, u=2)
            first, second = [TILES * g + j for j, g in chunks]
            move(words[:, first:second + 1:second - first], banks[bank][:].rearrange("p (c u) d -> p c d u", u=2))

        def gather_dy(k, g):
            nc.vector.tensor_copy(
                dealt(dy_picked[k, g].bitcast(U32)), dy_tiles[k][:].bitcast(U32).indirect(edges(dst_list, g)),
            )

        def gather_dy_whole(k):
            nc.vector.tensor_copy(dealt(dy_whole[k][:].bitcast(U32)), dy_tiles[k][:].bitcast(U32).indirect(dst_list[:]))

        def turn_dy(k, g, bank):
            for t in range(PACK):
                u, v = divmod(t, 2)
                if k in dy_whole:
                    turn(bank, t, every_second(dy_whole[k], PASSES * u + g, v))
                else:
                    turn(bank, t, every_second(dy_picked[k, g], u, v))

        def square(k, g):
            nc.scalar.activation(dealt(squares[k, g]), in_runs(half(h_pairs[k // 2][g], k % 2)), ACT.Square)

        def square_on_gpsimd(k, g):
            h = in_runs(half(h_pairs[k // 2][g], k % 2))
            nc.gpsimd.tensor_tensor(dealt(squares[k, g]), h, h, ALU.mult)

        def turn_squares(k, g, two_banks):
            for t in range(PACK):
                u, v = divmod(t, 2)
                turn(two_banks[u], 2 * v + k % 2, every_second(squares[k, g], u, v))

        def make_factors(m, g, u, bank):
            for v in range(2):
                t = 2 * u + v
                at = slice(PACK * g + t, PACK * g + t + 1)
                nc.scalar.activation(
                    factors[m][g][:, rows(2 * t, 2)], banks[bank][:, 2 * v:2 * v + 2, :].rearrange("p k n -> p (k n)"),
                    ACT.Identity, bias=tw_cols[:, at], scale=neg_tw_cols[:, at],
                )

        def make_dz(k, g, bank):
            group, at = home[k, g]
            nc.vector.tensor_tensor(
                half(dz_bf[group], at).rearrange("p (c i t) -> p c t i", i=4, t=PACK),
                banks[bank][:].rearrange("p t (c i) -> p c t i", i=4),
                factors[k // 2][g][:].rearrange("p (t k c i) -> p k c t i", t=PACK, k=2, i=4)[:, k % 2],
                ALU.mult,
            )

        def quantize_dz(group):
            nc.vector.quantize_mx(out=dz_codes[group][:].bitcast(E5M2), scales=dz_scales[group][:], in_=dz_bf[group][:])

        def multiply(j, g, k, count, acc, start, stop):
            group, at = home[k, g]
            still, moving = rows(TILES * g + j), rows(at, count)
            nc.tensor.matmul_mx(
                out=acc, lhsT=x_codes[:, still].bitcast(E4M3), lhsT_scale=x_scales[:, still],
                rhs=dz_codes[group][:, moving].bitcast(E5M2), rhs_scale=dz_scales[group][:, moving],
                start=start, stop=stop,
            )

        def multiply_left(m, bank):
            for s in range(2):
                for g in range(PASSES):
                    acc = banks[bank][:, 2 * s:2 * s + 2, :].rearrange("p k n -> p (k n)")
                    multiply(2 * m + s, g, 0, 2, acc, g == 0, g == PASSES - 1)

        def multiply_column(k, g, bank, tiles):
            for s, j in enumerate(tiles):
                multiply(j, g, k, 1, banks[bank][:, s, :], (g, s) == (0, 0), (g, s) == (PASSES - 1, len(tiles) - 1))

        def store(move, row_tiles, col_tiles, bank, part):
            width = col_tiles.stop - col_tiles.start
            move(part, banks[bank][:].rearrange("p t n -> p (t n)")[:, 0:part.shape[1]])
            nc.sync.dma_start(
                out[row_tiles, col_tiles].rearrange("(j p) n -> p j n", p=P), part.rearrange("p (j n) -> p j n", n=width),
            )

        weight_columns(6)
        square(0, 0)
        square(1, 0)
        turn_squares(0, 0, (0, 1))
        turn_squares(1, 0, (0, 1))
        gather_x_on_vector(0, 0)
        gather_x_on_scalar(0, 1)
        gather_dy(0, 0)
        make_factors(0, 0, 0, 0)
        make_factors(0, 0, 1, 1)
        turn_dy(0, 0, 0)
        gather_dy(0, 1)
        gather_x_on_scalar(1, 1)
        pair_x(0, 1)
        make_dz(0, 0, 0)
        gather_x_on_scalar(1, 0)
        pair_x(1, 1)
        gather_dy(1, 0)
        turn_dy(0, 1, 0)
        turn_pairs(0, 1, 1, 0)
        gather_x_on_scalar(2, 0)
        turn_dy(1, 0, 6)
        gather_dy(1, 1)
        turn_pairs(1, 1, 1, 1)
        gather_x_on_scalar(2, 1)
        make_dz(1, 0, 6)
        turn_dy(1, 1, 6)
        pair_two(low_picked, low_pairs, in_runs(half(sw_rows, 0)).unsqueeze(1).to_broadcast([P, 2, RUN, 2, RUN]))
        gather_dy_whole(2)
        weave_x(((0, 1), (1, 1)), 1)

        square(0, 1)
        turn_two(low_pairs, 1)
        pair_two(mid_picked, mid_pairs, sw_rows[:].rearrange("p (c b u r) -> p c b u r", c=2, u=2, r=RUN))
        square(1, 1)
        turn_squares(0, 1, (2, 3))
        gather_x_on_scalar(3, 0)
        turn_squares(1, 1, (2, 3))
        gather_x_on_vector(3, 1)
        weave_x(((0, 0), (1, 0)), 1)
        make_factors(0, 1, 0, 2)
        gather_dy_whole(3)
        pair_x(3, 0)
        turn_two(mid_pairs, 1)
        turn_dy(2, 0, 2)
        make_factors(0, 1, 1, 3)
        turn_dy(2, 1, 3)
        weave_x(((2, 0), (2, 1)), 1)

        square(2, 0)
        pair_x(3, 1)
        turn_squares(2, 0, (4, 5))
        make_dz(0, 1, 0)
        square(3, 0)
        make_dz(1, 1, 6)
        turn_pairs(3, 0, 1, 0)
        turn_pairs(3, 1, 1, 1)
        square_on_gpsimd(2, 1)
        turn_squares(3, 0, (4, 5))
        weave_x(((3, 0), (3, 1)), 1)
        square(3, 1)
        quantize_dz(0)
        turn_squares(2, 1, (0, 6))
        turn_dy(3, 1, 1)
        turn_squares(3, 1, (0, 6))
        make_factors(1, 0, 0, 4)
        turn_dy(3, 0, 4)
        nc.vector.quantize_mx(out=x_codes[:].bitcast(E4M3), scales=x_scales[:], in_=x_bf[:])
        make_factors(1, 0, 1, 5)
        make_factors(1, 1, 0, 0)
        make_dz(2, 0, 2)
        multiply_left(0, 5)
        make_factors(1, 1, 1, 6)
        make_dz(3, 0, 4)
        multiply_left(1, 0)
        make_dz(2, 1, 3)
        quantize_dz(1)
        store(nc.scalar.copy, rows(0, 2), rows(0, 2), 5, staged[0][:])
        multiply_column(2, 0, 2, range(TILES))
        quantize_dz(2)
        make_dz(3, 1, 1)
        store(nc.scalar.copy, rows(2, 2), rows(0, 2), 0, staged[1][:])
        multiply_column(2, 1, 2, range(TILES))
        multiply_column(3, 0, 4, (0, 1))
        multiply_column(3, 0, 7, (2, 3))
        quantize_dz(3)
        store(nc.scalar.copy, rows(0, TILES), rows(2), 2, staged[2][:])
        multiply_column(3, 1, 4, (0, 1))
        multiply_column(3, 1, 7, (2, 3))
        store(nc.vector.tensor_copy, rows(0, 2), rows(3), 4, staged[3][:, rows(0, 2)])
        store(nc.scalar.copy, rows(2, 2), rows(3), 7, staged[3][:, rows(2, 2)])
